import numpy as np
import ml_dtypes


def mxq(x, axis, fmt="e4m3"):
    dtype, down = {"e4m3": (ml_dtypes.float8_e4m3fn, 7), "e5m2": (ml_dtypes.float8_e5m2, 14)}[fmt]
    v = np.moveaxis(np.asarray(x, np.float32).astype(ml_dtypes.bfloat16).astype(np.float64), axis, -1)
    blocks = v.reshape(v.shape[:-1] + (-1, 32))
    amax = np.abs(blocks).max(-1, keepdims=True)
    byte = np.maximum(np.where(amax > 0, np.frexp(amax)[1] - 1 + 127, 0) - down, 1)
    scale = np.exp2(byte - 127.0)
    codes = (blocks / scale).astype(np.float32).astype(dtype).astype(np.float64)
    return np.moveaxis((codes * scale).reshape(v.shape), -1, axis)


WIDE = False


def mx_kscale(k):
    if not WIDE:
        return np.ones(k)
    levels = np.array([30, -30])
    if k % 512:
        return np.exp2(np.random.permutation(np.resize(levels, k // 32))).repeat(32)
    a = np.empty((k // 512, 16))
    for p in range(k // 512):
        a[p, :8] = np.random.permutation(np.resize(levels, 8))
        for g in range(8):
            far = levels[np.abs(levels - a[p, g]) >= 10]
            a[p, g + 8] = far[np.random.randint(len(far))]
    return np.exp2(a.ravel()).repeat(32)


def f64(x):
    return np.asarray(x).astype(np.float64)


def striped(idx):
    return np.tile(idx.reshape(-1, 16).T, (8, 1)).astype(np.uint16)


def unstriped(offs):
    return offs[:16].T.reshape(-1).astype(np.int64)


E2M1 = np.array([0.0, 0.5, 1.0, 1.5, 2.0, 3.0, 4.0, 6.0, -0.0, -0.5, -1.0, -1.5, -2.0, -3.0, -4.0, -6.0])


def pack_weight(w, fmt):
    k, n = w.shape
    w = f64(np.asarray(w, np.float32).astype(ml_dtypes.bfloat16)).reshape(k // 32, 32, n)
    amax = np.abs(w).max(1)
    if fmt == "e4m3":
        byte = np.frexp(amax)[1] - 1 + 127 - 7
    else:
        mant, ex = np.frexp(amax / 6.0)
        byte = np.where(mant > 0.5, ex, ex - 1) + 127
    byte = np.clip(np.where(amax > 0, byte, 1), 1, 254)
    scaled = (w * np.exp2(127.0 - byte)[:, None, :]).reshape(k, n).astype(np.float32)
    by_word = np.ascontiguousarray(scaled.reshape(k // 512, 128, 4, n).transpose(0, 1, 3, 2))
    if fmt == "e4m3":
        words = by_word.astype(ml_dtypes.float8_e4m3fn).view(np.uint8)
    else:
        c = by_word.astype(ml_dtypes.float4_e2m1fn).view(np.uint8) & 0xF
        words = (c[..., 0::2] | (c[..., 1::2] << 4)).reshape(k // 512, 128, 2 * n)
    return np.ascontiguousarray(words), np.ascontiguousarray(byte.astype(np.uint8).reshape(k // 512, 16, n))


def unpack_weight(words, scales, fmt):
    g, _, n = scales.shape
    words = np.ascontiguousarray(words).reshape(g, 128, n, -1)
    if fmt == "e4m3":
        vals = words.view(ml_dtypes.float8_e4m3fn).astype(np.float64)
    else:
        nib = np.empty((g, 128, n, 4), np.uint8)
        nib[..., 0::2] = words & 0xF
        nib[..., 1::2] = words >> 4
        vals = E2M1[nib]
    vals = vals * np.repeat(np.exp2(scales.astype(np.float64) - 127.0), 8, axis=1)[..., None]
    return vals.transpose(0, 1, 3, 2).reshape(g * 512, n)


def planes(y):
    n, m = y.shape
    v = y.astype(np.float32).astype(ml_dtypes.bfloat16).astype(np.float64).reshape(n // 32, 32, m)
    top = np.abs(v).max(1)
    byte = np.clip(np.where(top > 0, np.frexp(top)[1] - 1 + 127 - 7, 1), 1, 254)
    codes = (v * np.exp2(127.0 - byte)[:, None, :]).reshape(n, m).astype(np.float32).astype(ml_dtypes.float8_e4m3fn).view(np.uint8)
    words = codes.reshape(n // 512, 128, 4, m).transpose(0, 1, 3, 2)
    return np.ascontiguousarray(words), np.ascontiguousarray(byte.astype(np.uint8).reshape(n // 512, 16, m))


K, N, T, J = 512, 512, 2048, 1024


def setup_inputs():
    n = np.random.standard_normal
    s = mx_kscale(K)[:, None]
    m = np.exp(0.5 * n((1, J)))
    p_w = pack_weight(n((K, N)) / np.sqrt(K) / s, "e4m3")
    return {
        "dy": (m * n((K, J)) * s).astype(np.float32),
        "w_words": p_w[0],
        "w_scales": p_w[1],
        "wgo": np.tile(np.random.uniform(0.5, 2.0, J), (128, 1)).astype(np.float32),
        "offs": striped(np.random.permutation(T)[:J]),
    }


def reference(dy, w_words, w_scales, wgo, offs):
    idx = unstriped(offs)
    dy_q_ = mxq(f64(dy), 0, "e5m2")
    dy_r_ = mxq(f64(dy) - dy_q_, 0, "e4m3")
    w_ = unpack_weight(w_words, w_scales, "e4m3")
    dx = w_.T @ dy_q_ + w_.T @ dy_r_
    out = np.zeros((N, T))
    out[:, idx] = f64(wgo)[0] * (dx)
    return (out,) + planes(out)

@@ -1,0 +1,167 @@
+from contextlib import ExitStack
+
+import concourse.mybir as mybir
+from concourse.masks import make_identity
+
+K, N, T, J = 512, 512, 2048, 1024
+FLOPS = 2 * K * N * J * 3
+
+F32 = mybir.dt.float32
+BF16 = mybir.dt.bfloat16
+I32 = mybir.dt.int32
+U32 = mybir.dt.uint32
+U16 = mybir.dt.uint16
+U8 = mybir.dt.uint8
+E4M3 = mybir.dt.float8_e4m3fn_x4
+E5M2 = mybir.dt.float8_e5m2_x4
+MULT = mybir.AluOpType.mult
+SUB = mybir.AluOpType.subtract
+
+P = 128
+PACK = 4
+HALF = 512
+PIECE = 256
+CHUNK = 512
+QUADS = 4
+
+
+def woven(tile3):
+    return tile3.rearrange("p (c i) t -> p c t i", i=PACK)
+
+
+def planar(tile3):
+    return tile3.rearrange("p t (c i) -> p c t i", i=PACK)
+
+
+def flat(tile3):
+    return tile3.rearrange("p a b -> p (a b)")
+
+
+def tile_list_embg_tgq8_noneP_kernel(tc, dy, w_words, w_scales, wgo, offs, out_0, out_1, out_2):
+    nc = tc.nc
+    halves = J // HALF
+    pieces = J // PIECE
+    per_half = HALF // PIECE
+    chunks = T // CHUNK
+
+    with ExitStack() as ctx:
+        sb = ctx.enter_context(tc.tile_pool(name="sb", bufs=1))
+        psum = ctx.enter_context(tc.psum_pool(name="psum", bufs=1))
+
+        def sbuf(name, shape, dtype, tag=None):
+            return sb.tile(shape, dtype, name=name, tag=tag or name, align_bytes=64)
+
+        dy_planes = dy.rearrange("(p t) j -> p t j", t=PACK)
+        raw = [sbuf("raw%d" % c, [P, PACK, PIECE], F32) for c in range(pieces)]
+        for c in range(pieces):
+            nc.sync.dma_start(out=raw[c][:], in_=dy_planes[:, :, c * PIECE:(c + 1) * PIECE])
+
+        w_in = sbuf("w_in", [P, N], I32)
+        nc.sync.dma_start(out=w_in[:], in_=w_words[0].rearrange("p n i -> p (n i)").bitcast(I32))
+        ws_in = sbuf("ws_in", [P, N], U8)
+        nc.vector.memset(ws_in[:].bitcast(I32), 0)
+        for q in range(QUADS):
+            nc.sync.dma_start(out=ws_in[32 * q:32 * q + 4, :].bitcast(I32), in_=w_scales[0, 4 * q:4 * q + 4, :].bitcast(I32))
+        gain = sbuf("gain", [P, J], F32)
+        nc.sync.dma_start(out=gain[:], in_=wgo)
+        offsets = sb.tile([P, J // 16], U16, name="offsets")
+        nc.sync.dma_start(offsets[:], offs)
+
+        eye = sbuf("eye", [P, P], BF16)
+        make_identity(nc, eye[:])
+        eye_in = sbuf("eye_in", [P, PACK, P, PACK], BF16)
+        nc.vector.memset(eye_in[:].rearrange("p t m i -> p (t m i)").bitcast(I32), 0)
+        for t in range(PACK):
+            nc.scalar.copy(out=eye_in[:, t, :, t], in_=eye[:])
+        eye_codes = sbuf("eye_codes", [P, K], U32)
+        eye_scales = sbuf("eye_scales", [P, K], U8)
+        nc.vector.quantize_mx(out=eye_codes[:].bitcast(E4M3), scales=eye_scales[:], in_=eye_in[:].rearrange("p t m i -> p (t m i)"))
+
+        first_page = sbuf("page0", [P, T], F32)
+        nc.vector.memset(first_page[:], 0.0)
+
+        q_codes = [sbuf("q_codes%d" % h, [P, HALF], U32) for h in range(halves)]
+        q_scales = [sbuf("q_scales%d" % h, [P, HALF], U8) for h in range(halves)]
+        r_codes = [sbuf("r_codes%d" % h, [P, HALF], U32) for h in range(halves)]
+        r_scales = [sbuf("r_scales%d" % h, [P, HALF], U8) for h in range(halves)]
+        back = [sbuf("back%d" % h, [P, PACK, HALF], F32) for h in range(halves)]
+
+        def bank(h, t):
+            return psum.tile([P, HALF], F32, name="bank%d" % (PACK * h + t))
+
+        for h in range(halves):
+            rounded = []
+            for s in range(per_half):
+                c = h * per_half + s
+                x = sbuf("rounded%d" % c, [P, PIECE, PACK], BF16)
+                nc.vector.tensor_copy(out=woven(x[:]), in_=planar(raw[c][:]))
+                rounded.append(x)
+            for s in range(per_half):
+                cols = slice(s * PIECE, (s + 1) * PIECE)
+                nc.vector.quantize_mx(out=q_codes[h][:, cols].bitcast(E5M2), scales=q_scales[h][:, cols], in_=flat(rounded[s][:]))
+            for t in range(PACK):
+                acc = bank(h, t)
+                rows = slice(t * P, (t + 1) * P)
+                nc.tensor.matmul_mx(out=acc[:], lhsT=eye_codes[:, rows].bitcast(E4M3), lhsT_scale=eye_scales[:, rows],
+                                    rhs=q_codes[h][:].bitcast(E5M2), rhs_scale=q_scales[h][:], start=True, stop=True)
+                nc.scalar.copy(out=back[h][:, t, :], in_=acc[:])
+
+        w_codes = sbuf("w_codes", [P, PACK, P], I32)
+        w_plane = sbuf("w_plane", [P, PACK, P], U8)
+        nc.vector.tensor_copy(out=w_codes[:], in_=w_in[:].rearrange("p (m t) -> p t m", t=PACK))
+        nc.vector.tensor_copy(out=w_plane[:], in_=ws_in[:].rearrange("p (m t) -> p t m", t=PACK))
+
+        dx_first = [sbuf("dx0_%d" % h, [P, HALF], F32) for h in range(halves)]
+        dx = [None] + [sbuf("dx%d" % t, [P, J], F32) for t in range(1, PACK)]
+        for h in range(halves):
+            left = []
+            for s in range(per_half):
+                c = h * per_half + s
+                cols = slice(s * PIECE, (s + 1) * PIECE)
+                x = sbuf("left%d" % c, [P, PIECE, PACK], BF16)
+                nc.vector.tensor_tensor(woven(x[:]), planar(raw[c][:]), planar(back[h][:, :, cols]), SUB)
+                left.append(x)
+            for s in range(per_half):
+                cols = slice(s * PIECE, (s + 1) * PIECE)
+                nc.vector.quantize_mx(out=r_codes[h][:, cols].bitcast(E4M3), scales=r_scales[h][:, cols], in_=flat(left[s][:]))
+            for t in range(PACK):
+                acc = bank(h, t)
+                nc.tensor.matmul_mx(out=acc[:], lhsT=w_codes[:, t, :].bitcast(E4M3), lhsT_scale=w_plane[:, t, :],
+                                    rhs=q_codes[h][:].bitcast(E5M2), rhs_scale=q_scales[h][:], start=True, stop=False)
+                nc.tensor.matmul_mx(out=acc[:], lhsT=w_codes[:, t, :].bitcast(E4M3), lhsT_scale=w_plane[:, t, :],
+                                    rhs=r_codes[h][:].bitcast(E4M3), rhs_scale=r_scales[h][:], start=False, stop=True)
+                nc.scalar.copy(out=dx_first[h][:] if t == 0 else dx[t][:, h * HALF:(h + 1) * HALF], in_=acc[:])
+
+        out_planes = out_0.rearrange("(p t) c -> p t c", t=PACK)
+        grouped = [sbuf("grouped%d" % c, [P, CHUNK, PACK], BF16) for c in range(chunks)]
+        pages = [first_page]
+        heirs = ["left%d" % (pieces - 1), "dx0_0", "dx0_1"]
+        for h in range(halves):
+            cols = slice(h * HALF, (h + 1) * HALF)
+            nc.vector.tensor_tensor(first_page[:].indirect(offsets[:, h * HALF // 16:(h + 1) * HALF // 16]), dx_first[h][:], gain[:, cols], MULT)
+        for t in range(1, PACK):
+            page = sbuf("page%d" % t, [P, T], F32, tag=heirs[t - 1])
+            nc.gpsimd.memset(page[:], 0.0)
+            pages.append(page)
+        for t in range(PACK):
+            if t > 0:
+                nc.vector.tensor_tensor(pages[t][:].indirect(offsets[:]), dx[t][:], gain[:], MULT)
+            nc.sync.dma_start(out=out_planes[:, t, :], in_=pages[t][:])
+            for c in range(chunks):
+                cols = slice(c * CHUNK, (c + 1) * CHUNK)
+                if t == PACK - 1 and c < chunks // 2:
+                    nc.vector.tensor_copy(out=grouped[c][:, :, t], in_=pages[t][:, cols])
+                elif t == PACK - 2 and c < chunks // 2:
+                    nc.scalar.copy(out=grouped[c][:, :, t:], in_=pages[t][:, cols].unsqueeze(2).to_broadcast([P, CHUNK, 2]))
+                else:
+                    nc.scalar.copy(out=grouped[c][:, :, t], in_=pages[t][:, cols])
+
+        words_out = out_1[0].rearrange("p c i -> p (c i)").bitcast(I32)
+        y_scales = sbuf("y_scales", [P, T], U8)
+        for c in range(chunks):
+            cols = slice(c * CHUNK, (c + 1) * CHUNK)
+            y_codes = sbuf("y_codes%d" % c, [P, CHUNK], U32)
+            nc.vector.quantize_mx(out=y_codes[:].bitcast(E4M3), scales=y_scales[:, cols], in_=flat(grouped[c][:]))
+            nc.sync.dma_start(out=words_out[:, cols], in_=y_codes[:].bitcast(I32))
+        for q in range(QUADS):
+            nc.scalar.dma_start(out=out_2[0, 4 * q:4 * q + 4, :].bitcast(I32), in_=y_scales[32 * q:32 * q + 4, :].bitcast(I32))

@@ -62,23 +62,29 @@ def tile_list_embg_tgq8_noneP_kernel(tc, dy, w_words, w_scales, wgo, offs, out_0
         nc.vector.memset(ws_in[:].bitcast(I32), 0)
         for q in range(QUADS):
             nc.sync.dma_start(out=ws_in[32 * q:32 * q + 4, :].bitcast(I32), in_=w_scales[0, 4 * q:4 * q + 4, :].bitcast(I32))
-        gain = sbuf("gain", [P, J], F32)
-        nc.sync.dma_start(out=gain[:], in_=wgo)
+        eye = sbuf("eye", [P, P], BF16)
+        make_identity(nc, eye[:])
         offsets = sb.tile([P, J // 16], U16, name="offsets")
         nc.sync.dma_start(offsets[:], offs)
 
-        eye = sbuf("eye", [P, P], BF16)
-        make_identity(nc, eye[:])
-        eye_in = sbuf("eye_in", [P, PACK, P, PACK], BF16)
-        nc.vector.memset(eye_in[:].rearrange("p t m i -> p (t m i)").bitcast(I32), 0)
+        eye_in = sbuf("eye_in", [P, P, PACK], BF16, tag="ring0")
+        nc.gpsimd.memset(flat(eye_in[:]).bitcast(I32), 0)
+        eye_codes = sbuf("eye_codes", [P, PACK, P, PACK], U8)
+        nc.vector.memset(eye_codes[:].rearrange("p t m i -> p (t m i)").bitcast(I32), 0)
+        nc.scalar.copy(out=eye_in[:, :, 0], in_=eye[:])
+        eye_base = sbuf("eye_base", [P, P, PACK], U8, tag="ring1")
+        eye_scales = sbuf("eye_scales", [P, P], U8)
+        nc.vector.quantize_mx(out=flat(eye_base[:]).bitcast(E4M3), scales=eye_scales[:], in_=flat(eye_in[:]))
         for t in range(PACK):
-            nc.scalar.copy(out=eye_in[:, t, :, t], in_=eye[:])
-        eye_codes = sbuf("eye_codes", [P, K], U32)
-        eye_scales = sbuf("eye_scales", [P, K], U8)
-        nc.vector.quantize_mx(out=eye_codes[:].bitcast(E4M3), scales=eye_scales[:], in_=eye_in[:].rearrange("p t m i -> p (t m i)"))
+            nc.vector.tensor_copy(out=eye_codes[:, t, :, t], in_=eye_base[:, :, 0])
+
+        gain = sbuf("gain", [P, J], F32, tag="eye")
+        nc.sync.dma_start(out=gain[:], in_=wgo)
 
         first_page = sbuf("page0", [P, T], F32)
         nc.vector.memset(first_page[:], 0.0)
+        second_page = sbuf("page1", [P, T], F32)
+        nc.vector.memset(second_page[:], 0.0)
 
         q_codes = [sbuf("q_codes%d" % h, [P, HALF], U32) for h in range(halves)]
         q_scales = [sbuf("q_scales%d" % h, [P, HALF], U8) for h in range(halves)]
@@ -93,32 +99,41 @@ def tile_list_embg_tgq8_noneP_kernel(tc, dy, w_words, w_scales, wgo, offs, out_0
             rounded = []
             for s in range(per_half):
                 c = h * per_half + s
-                x = sbuf("rounded%d" % c, [P, PIECE, PACK], BF16)
-                nc.vector.tensor_copy(out=woven(x[:]), in_=planar(raw[c][:]))
+                x = sbuf("rounded%d" % c, [P, PIECE, PACK], BF16, tag="ring%d" % s)
+                if c == 1:
+                    nc.vector.tensor_copy(out=woven(x[:]), in_=planar(raw[c][:]))
+                else:
+                    nc.scalar.copy(out=woven(x[:]), in_=planar(raw[c][:]))
                 rounded.append(x)
             for s in range(per_half):
                 cols = slice(s * PIECE, (s + 1) * PIECE)
                 nc.vector.quantize_mx(out=q_codes[h][:, cols].bitcast(E5M2), scales=q_scales[h][:, cols], in_=flat(rounded[s][:]))
             for t in range(PACK):
                 acc = bank(h, t)
-                rows = slice(t * P, (t + 1) * P)
-                nc.tensor.matmul_mx(out=acc[:], lhsT=eye_codes[:, rows].bitcast(E4M3), lhsT_scale=eye_scales[:, rows],
+                nc.tensor.matmul_mx(out=acc[:], lhsT=flat(eye_codes[:, t]).bitcast(E4M3), lhsT_scale=eye_scales[:],
                                     rhs=q_codes[h][:].bitcast(E5M2), rhs_scale=q_scales[h][:], start=True, stop=True)
                 nc.scalar.copy(out=back[h][:, t, :], in_=acc[:])
 
-        w_codes = sbuf("w_codes", [P, PACK, P], I32)
-        w_plane = sbuf("w_plane", [P, PACK, P], U8)
+        w_codes = sbuf("w_codes", [P, PACK, P], I32, tag="ring0")
+        w_plane = sbuf("w_plane", [P, PACK, P], U8, tag="ring1")
         nc.vector.tensor_copy(out=w_codes[:], in_=w_in[:].rearrange("p (m t) -> p t m", t=PACK))
         nc.vector.tensor_copy(out=w_plane[:], in_=ws_in[:].rearrange("p (m t) -> p t m", t=PACK))
 
-        dx_first = [sbuf("dx0_%d" % h, [P, HALF], F32) for h in range(halves)]
+        pages = [first_page, second_page]
+        for t, heir in ((2, "w_in"), (3, "ws_in")):
+            page = sbuf("page%d" % t, [P, T], F32, tag=heir)
+            nc.vector.memset(page[:], 0.0)
+            pages.append(page)
+
+        dx_first = []
+        first_acc = []
         dx = [None] + [sbuf("dx%d" % t, [P, J], F32) for t in range(1, PACK)]
         for h in range(halves):
             left = []
             for s in range(per_half):
                 c = h * per_half + s
                 cols = slice(s * PIECE, (s + 1) * PIECE)
-                x = sbuf("left%d" % c, [P, PIECE, PACK], BF16)
+                x = sbuf("left%d" % c, [P, PIECE, PACK], BF16, tag="left%d" % s)
                 nc.vector.tensor_tensor(woven(x[:]), planar(raw[c][:]), planar(back[h][:, :, cols]), SUB)
                 left.append(x)
             for s in range(per_half):
@@ -130,19 +145,20 @@ def tile_list_embg_tgq8_noneP_kernel(tc, dy, w_words, w_scales, wgo, offs, out_0
                                     rhs=q_codes[h][:].bitcast(E5M2), rhs_scale=q_scales[h][:], start=True, stop=False)
                 nc.tensor.matmul_mx(out=acc[:], lhsT=w_codes[:, t, :].bitcast(E4M3), lhsT_scale=w_plane[:, t, :],
                                     rhs=r_codes[h][:].bitcast(E4M3), rhs_scale=r_scales[h][:], start=False, stop=True)
-                nc.scalar.copy(out=dx_first[h][:] if t == 0 else dx[t][:, h * HALF:(h + 1) * HALF], in_=acc[:])
+                if t == 0:
+                    first_acc.append(acc)
+                else:
+                    nc.scalar.copy(out=dx[t][:, h * HALF:(h + 1) * HALF], in_=acc[:])
+        for h in range(halves):
+            part = sbuf("dx0_%d" % h, [P, HALF], F32, tag="back1" if h == 0 else "dx0_1")
+            nc.scalar.copy(out=part[:], in_=first_acc[h][:])
+            dx_first.append(part)
 
         out_planes = out_0.rearrange("(p t) c -> p t c", t=PACK)
         grouped = [sbuf("grouped%d" % c, [P, CHUNK, PACK], BF16) for c in range(chunks)]
-        pages = [first_page]
-        heirs = ["left%d" % (pieces - 1), "dx0_0", "dx0_1"]
         for h in range(halves):
             cols = slice(h * HALF, (h + 1) * HALF)
             nc.vector.tensor_tensor(first_page[:].indirect(offsets[:, h * HALF // 16:(h + 1) * HALF // 16]), dx_first[h][:], gain[:, cols], MULT)
-        for t in range(1, PACK):
-            page = sbuf("page%d" % t, [P, T], F32, tag=heirs[t - 1])
-            nc.gpsimd.memset(page[:], 0.0)
-            pages.append(page)
         for t in range(PACK):
             if t > 0:
                 nc.vector.tensor_tensor(pages[t][:].indirect(offsets[:]), dx[t][:], gain[:], MULT)

@@ -21,7 +21,8 @@ P = 128
 PACK = 4
 HALF = 512
 PIECE = 256
-CHUNK = 512
+CHUNKS = (512, 512, 512, 512)
+ON_VECTOR = 2
 QUADS = 4
 
 
@@ -42,7 +43,7 @@ def tile_list_embg_tgq8_noneP_kernel(tc, dy, w_words, w_scales, wgo, offs, out_0
     halves = J // HALF
     pieces = J // PIECE
     per_half = HALF // PIECE
-    chunks = T // CHUNK
+    spans = [slice(sum(CHUNKS[:c]), sum(CHUNKS[:c + 1])) for c in range(len(CHUNKS))]
 
     with ExitStack() as ctx:
         sb = ctx.enter_context(tc.tile_pool(name="sb", bufs=1))
@@ -82,9 +83,7 @@ def tile_list_embg_tgq8_noneP_kernel(tc, dy, w_words, w_scales, wgo, offs, out_0
         nc.sync.dma_start(out=gain[:], in_=wgo)
 
         first_page = sbuf("page0", [P, T], F32)
-        nc.vector.memset(first_page[:], 0.0)
-        second_page = sbuf("page1", [P, T], F32)
-        nc.vector.memset(second_page[:], 0.0)
+        nc.vector.memset(first_page[:].bitcast(I32), 0)
 
         q_codes = [sbuf("q_codes%d" % h, [P, HALF], U32) for h in range(halves)]
         q_scales = [sbuf("q_scales%d" % h, [P, HALF], U8) for h in range(halves)]
@@ -100,10 +99,10 @@ def tile_list_embg_tgq8_noneP_kernel(tc, dy, w_words, w_scales, wgo, offs, out_0
             for s in range(per_half):
                 c = h * per_half + s
                 x = sbuf("rounded%d" % c, [P, PIECE, PACK], BF16, tag="ring%d" % s)
-                if c == 1:
-                    nc.vector.tensor_copy(out=woven(x[:]), in_=planar(raw[c][:]))
-                else:
+                if c == 0:
                     nc.scalar.copy(out=woven(x[:]), in_=planar(raw[c][:]))
+                else:
+                    nc.vector.tensor_copy(out=woven(x[:]), in_=planar(raw[c][:]))
                 rounded.append(x)
             for s in range(per_half):
                 cols = slice(s * PIECE, (s + 1) * PIECE)
@@ -112,18 +111,17 @@ def tile_list_embg_tgq8_noneP_kernel(tc, dy, w_words, w_scales, wgo, offs, out_0
                 acc = bank(h, t)
                 nc.tensor.matmul_mx(out=acc[:], lhsT=flat(eye_codes[:, t]).bitcast(E4M3), lhsT_scale=eye_scales[:],
                                     rhs=q_codes[h][:].bitcast(E5M2), rhs_scale=q_scales[h][:], start=True, stop=True)
-                nc.scalar.copy(out=back[h][:, t, :], in_=acc[:])
+                if h == 0 and t == PACK - 1:
+                    for s in range(per_half):
+                        cols = slice(s * PIECE, (s + 1) * PIECE)
+                        nc.scalar.copy(out=back[h][:, t, cols], in_=acc[:, cols])
+                else:
+                    nc.scalar.copy(out=back[h][:, t, :], in_=acc[:])
 
         w_codes = sbuf("w_codes", [P, PACK, P], I32, tag="ring0")
         w_plane = sbuf("w_plane", [P, PACK, P], U8, tag="ring1")
         nc.vector.tensor_copy(out=w_codes[:], in_=w_in[:].rearrange("p (m t) -> p t m", t=PACK))
         nc.vector.tensor_copy(out=w_plane[:], in_=ws_in[:].rearrange("p (m t) -> p t m", t=PACK))
-
-        pages = [first_page, second_page]
-        for t, heir in ((2, "w_in"), (3, "ws_in")):
-            page = sbuf("page%d" % t, [P, T], F32, tag=heir)
-            nc.vector.memset(page[:], 0.0)
-            pages.append(page)
 
         dx_first = []
         first_acc = []
@@ -155,28 +153,31 @@ def tile_list_embg_tgq8_noneP_kernel(tc, dy, w_words, w_scales, wgo, offs, out_0
             dx_first.append(part)
 
         out_planes = out_0.rearrange("(p t) c -> p t c", t=PACK)
-        grouped = [sbuf("grouped%d" % c, [P, CHUNK, PACK], BF16) for c in range(chunks)]
+        grouped = [sbuf("grouped%d" % c, [P, width, PACK], BF16) for c, width in enumerate(CHUNKS)]
         for h in range(halves):
             cols = slice(h * HALF, (h + 1) * HALF)
             nc.vector.tensor_tensor(first_page[:].indirect(offsets[:, h * HALF // 16:(h + 1) * HALF // 16]), dx_first[h][:], gain[:, cols], MULT)
+        pages = [first_page]
+        for t, heir in ((1, "left1"), (2, "back1"), (3, "dx0_1")):
+            page = sbuf("page%d" % t, [P, T], F32, tag=heir)
+            nc.gpsimd.memset(page[:], 0.0)
+            pages.append(page)
         for t in range(PACK):
             if t > 0:
                 nc.vector.tensor_tensor(pages[t][:].indirect(offsets[:]), dx[t][:], gain[:], MULT)
             nc.sync.dma_start(out=out_planes[:, t, :], in_=pages[t][:])
-            for c in range(chunks):
-                cols = slice(c * CHUNK, (c + 1) * CHUNK)
-                if t == PACK - 1 and c < chunks // 2:
+            for c, cols in enumerate(spans):
+                if t == PACK - 1 and c < ON_VECTOR:
                     nc.vector.tensor_copy(out=grouped[c][:, :, t], in_=pages[t][:, cols])
-                elif t == PACK - 2 and c < chunks // 2:
-                    nc.scalar.copy(out=grouped[c][:, :, t:], in_=pages[t][:, cols].unsqueeze(2).to_broadcast([P, CHUNK, 2]))
+                elif t == PACK - 2 and c < ON_VECTOR:
+                    nc.scalar.copy(out=grouped[c][:, :, t:], in_=pages[t][:, cols].unsqueeze(2).to_broadcast([P, CHUNKS[c], 2]))
                 else:
                     nc.scalar.copy(out=grouped[c][:, :, t], in_=pages[t][:, cols])
 
         words_out = out_1[0].rearrange("p c i -> p (c i)").bitcast(I32)
         y_scales = sbuf("y_scales", [P, T], U8)
-        for c in range(chunks):
-            cols = slice(c * CHUNK, (c + 1) * CHUNK)
-            y_codes = sbuf("y_codes%d" % c, [P, CHUNK], U32)
+        for c, cols in enumerate(spans):
+            y_codes = sbuf("y_codes%d" % c, [P, CHUNKS[c]], U32)
             nc.vector.quantize_mx(out=y_codes[:].bitcast(E4M3), scales=y_scales[:, cols], in_=flat(grouped[c][:]))
             nc.sync.dma_start(out=words_out[:, cols], in_=y_codes[:].bitcast(I32))
         for q in range(QUADS):

@@ -26,12 +26,12 @@ ON_VECTOR = 2
 QUADS = 4
 
 
-def woven(tile3):
-    return tile3.rearrange("p (c i) t -> p c t i", i=PACK)
+def woven(tile3, run=PACK):
+    return tile3.rearrange("p (c i) t -> p c t i", i=run)
 
 
-def planar(tile3):
-    return tile3.rearrange("p t (c i) -> p c t i", i=PACK)
+def planar(tile3, run=PACK):
+    return tile3.rearrange("p t (c i) -> p c t i", i=run)
 
 
 def flat(tile3):
@@ -132,7 +132,7 @@ def tile_list_embg_tgq8_noneP_kernel(tc, dy, w_words, w_scales, wgo, offs, out_0
                 c = h * per_half + s
                 cols = slice(s * PIECE, (s + 1) * PIECE)
                 x = sbuf("left%d" % c, [P, PIECE, PACK], BF16, tag="left%d" % s)
-                nc.vector.tensor_tensor(woven(x[:]), planar(raw[c][:]), planar(back[h][:, :, cols]), SUB)
+                nc.vector.tensor_tensor(woven(x[:], 2), planar(raw[c][:], 2), planar(back[h][:, :, cols], 2), SUB)
                 left.append(x)
             for s in range(per_half):
                 cols = slice(s * PIECE, (s + 1) * PIECE)

@@ -20,9 +20,6 @@ SUB = mybir.AluOpType.subtract
 P = 128
 PACK = 4
 HALF = 512
-PIECE = 256
-CHUNKS = (512, 512, 512, 512)
-ON_VECTOR = 2
 QUADS = 4
 
 
@@ -38,12 +35,17 @@ def flat(tile3):
     return tile3.rearrange("p a b -> p (a b)")
 
 
+PIECE = 256
+CHUNK = 512
+ON_VECTOR = 960
+FIRST = (512, 512)
+
+
 def tile_list_embg_tgq8_noneP_kernel(tc, dy, w_words, w_scales, wgo, offs, out_0, out_1, out_2):
     nc = tc.nc
     halves = J // HALF
-    pieces = J // PIECE
     per_half = HALF // PIECE
-    spans = [slice(sum(CHUNKS[:c]), sum(CHUNKS[:c + 1])) for c in range(len(CHUNKS))]
+    pieces = J // PIECE
 
     with ExitStack() as ctx:
         sb = ctx.enter_context(tc.tile_pool(name="sb", bufs=1))
@@ -63,24 +65,23 @@ def tile_list_embg_tgq8_noneP_kernel(tc, dy, w_words, w_scales, wgo, offs, out_0
         nc.vector.memset(ws_in[:].bitcast(I32), 0)
         for q in range(QUADS):
             nc.sync.dma_start(out=ws_in[32 * q:32 * q + 4, :].bitcast(I32), in_=w_scales[0, 4 * q:4 * q + 4, :].bitcast(I32))
-        eye = sbuf("eye", [P, P], BF16)
-        make_identity(nc, eye[:])
         offsets = sb.tile([P, J // 16], U16, name="offsets")
         nc.sync.dma_start(offsets[:], offs)
+        gain = sbuf("gain", [P, J], F32)
+        nc.sync.dma_start(out=gain[:], in_=wgo)
 
+        eye = sbuf("eye", [P, P], BF16)
+        make_identity(nc, eye[:])
         eye_in = sbuf("eye_in", [P, P, PACK], BF16, tag="ring0")
-        nc.gpsimd.memset(flat(eye_in[:]).bitcast(I32), 0)
-        eye_codes = sbuf("eye_codes", [P, PACK, P, PACK], U8)
-        nc.vector.memset(eye_codes[:].rearrange("p t m i -> p (t m i)").bitcast(I32), 0)
-        nc.scalar.copy(out=eye_in[:, :, 0], in_=eye[:])
+        nc.scalar.copy(out=eye_in[:], in_=eye[:].unsqueeze(2).to_broadcast([P, P, PACK]))
+        row = P * PACK
+        eye_codes = sbuf("eye_codes", [P, PACK * row + 64], U8)
+        nc.vector.memset(eye_codes[:].bitcast(I32), 0)
         eye_base = sbuf("eye_base", [P, P, PACK], U8, tag="ring1")
         eye_scales = sbuf("eye_scales", [P, P], U8)
         nc.vector.quantize_mx(out=flat(eye_base[:]).bitcast(E4M3), scales=eye_scales[:], in_=flat(eye_in[:]))
-        for t in range(PACK):
-            nc.vector.tensor_copy(out=eye_codes[:, t, :, t], in_=eye_base[:, :, 0])
-
-        gain = sbuf("gain", [P, J], F32, tag="eye")
-        nc.sync.dma_start(out=gain[:], in_=wgo)
+        diagonal = eye_codes[:, 0:PACK * (row + 1)].rearrange("p (t x) -> p t x", t=PACK)[:, :, 0:row:PACK]
+        nc.vector.tensor_copy(out=diagonal, in_=eye_base[:].rearrange("p m t -> p t m"))
 
         first_page = sbuf("page0", [P, T], F32)
         nc.vector.memset(first_page[:].bitcast(I32), 0)
@@ -98,6 +99,7 @@ def tile_list_embg_tgq8_noneP_kernel(tc, dy, w_words, w_scales, wgo, offs, out_0
             rounded = []
             for s in range(per_half):
                 c = h * per_half + s
+                cols = slice(s * PIECE, (s + 1) * PIECE)
                 x = sbuf("rounded%d" % c, [P, PIECE, PACK], BF16, tag="ring%d" % s)
                 if c == 0:
                     nc.scalar.copy(out=woven(x[:]), in_=planar(raw[c][:]))
@@ -109,56 +111,64 @@ def tile_list_embg_tgq8_noneP_kernel(tc, dy, w_words, w_scales, wgo, offs, out_0
                 nc.vector.quantize_mx(out=q_codes[h][:, cols].bitcast(E5M2), scales=q_scales[h][:, cols], in_=flat(rounded[s][:]))
             for t in range(PACK):
                 acc = bank(h, t)
-                nc.tensor.matmul_mx(out=acc[:], lhsT=flat(eye_codes[:, t]).bitcast(E4M3), lhsT_scale=eye_scales[:],
+                nc.tensor.matmul_mx(out=acc[:], lhsT=eye_codes[:, t * row:(t + 1) * row].bitcast(E4M3), lhsT_scale=eye_scales[:],
                                     rhs=q_codes[h][:].bitcast(E5M2), rhs_scale=q_scales[h][:], start=True, stop=True)
-                if h == 0 and t == PACK - 1:
-                    for s in range(per_half):
-                        cols = slice(s * PIECE, (s + 1) * PIECE)
-                        nc.scalar.copy(out=back[h][:, t, cols], in_=acc[:, cols])
-                else:
-                    nc.scalar.copy(out=back[h][:, t, :], in_=acc[:])
+                nc.scalar.copy(out=back[h][:, t, :], in_=acc[:])
+
+        def subtract(c):
+            h, s = divmod(c, per_half)
+            left = sbuf("left%d" % c, [P, PIECE, PACK], BF16, tag="left%d" % s)
+            nc.vector.tensor_tensor(woven(left[:], 2), planar(raw[c][:], 2), planar(back[h][:, :, s * PIECE:(s + 1) * PIECE], 2), SUB)
+            return left
+
+        def second(c, left):
+            h, s = divmod(c, per_half)
+            cols = slice(s * PIECE, (s + 1) * PIECE)
+            nc.vector.quantize_mx(out=r_codes[h][:, cols].bitcast(E4M3), scales=r_scales[h][:, cols], in_=flat(left[:]))
 
         w_codes = sbuf("w_codes", [P, PACK, P], I32, tag="ring0")
         w_plane = sbuf("w_plane", [P, PACK, P], U8, tag="ring1")
-        nc.vector.tensor_copy(out=w_codes[:], in_=w_in[:].rearrange("p (m t) -> p t m", t=PACK))
-        nc.vector.tensor_copy(out=w_plane[:], in_=ws_in[:].rearrange("p (m t) -> p t m", t=PACK))
+        accs = [[bank(h, t) for t in range(PACK)] for h in range(halves)]
 
-        dx_first = []
-        first_acc = []
-        dx = [None] + [sbuf("dx%d" % t, [P, J], F32) for t in range(1, PACK)]
-        for h in range(halves):
-            left = []
-            for s in range(per_half):
-                c = h * per_half + s
-                cols = slice(s * PIECE, (s + 1) * PIECE)
-                x = sbuf("left%d" % c, [P, PIECE, PACK], BF16, tag="left%d" % s)
-                nc.vector.tensor_tensor(woven(x[:], 2), planar(raw[c][:], 2), planar(back[h][:, :, cols], 2), SUB)
-                left.append(x)
-            for s in range(per_half):
-                cols = slice(s * PIECE, (s + 1) * PIECE)
-                nc.vector.quantize_mx(out=r_codes[h][:, cols].bitcast(E4M3), scales=r_scales[h][:, cols], in_=flat(left[s][:]))
+        def products(h):
             for t in range(PACK):
-                acc = bank(h, t)
-                nc.tensor.matmul_mx(out=acc[:], lhsT=w_codes[:, t, :].bitcast(E4M3), lhsT_scale=w_plane[:, t, :],
+                nc.tensor.matmul_mx(out=accs[h][t][:], lhsT=w_codes[:, t, :].bitcast(E4M3), lhsT_scale=w_plane[:, t, :],
                                     rhs=q_codes[h][:].bitcast(E5M2), rhs_scale=q_scales[h][:], start=True, stop=False)
-                nc.tensor.matmul_mx(out=acc[:], lhsT=w_codes[:, t, :].bitcast(E4M3), lhsT_scale=w_plane[:, t, :],
+            for t in range(PACK):
+                nc.tensor.matmul_mx(out=accs[h][t][:], lhsT=w_codes[:, t, :].bitcast(E4M3), lhsT_scale=w_plane[:, t, :],
                                     rhs=r_codes[h][:].bitcast(E4M3), rhs_scale=r_scales[h][:], start=False, stop=True)
-                if t == 0:
-                    first_acc.append(acc)
-                else:
-                    nc.scalar.copy(out=dx[t][:, h * HALF:(h + 1) * HALF], in_=acc[:])
+
+        starts = [sum(FIRST[:i]) for i in range(len(FIRST))]
+        dx_first = [sbuf("dx0_%d" % i, [P, width], F32) for i, width in enumerate(FIRST)]
+        dx = [None] + [sbuf("dx%d" % t, [P, J], F32) for t in range(1, PACK)]
+
+        def empty_first(i):
+            h, at = divmod(starts[i], HALF)
+            nc.scalar.copy(out=dx_first[i][:], in_=accs[h][0][:, at:at + FIRST[i]])
+
+        def scatter_first(i):
+            lo, hi = starts[i], starts[i] + FIRST[i]
+            nc.vector.tensor_tensor(first_page[:].indirect(offsets[:, lo // 16:hi // 16]), dx_first[i][:], gain[:, lo:hi], MULT)
+
+        nc.vector.tensor_copy(out=w_codes[:].rearrange("p t m -> p m t"), in_=w_in[:].rearrange("p (m t) -> p m t", t=PACK))
+        nc.vector.tensor_copy(out=w_plane[:], in_=ws_in[:].rearrange("p (m t) -> p t m", t=PACK))
         for h in range(halves):
-            part = sbuf("dx0_%d" % h, [P, HALF], F32, tag="back1" if h == 0 else "dx0_1")
-            nc.scalar.copy(out=part[:], in_=first_acc[h][:])
-            dx_first.append(part)
+            mine = range(h * per_half, (h + 1) * per_half)
+            lefts = [subtract(c) for c in mine]
+            for c, left in zip(mine, lefts):
+                second(c, left)
+            products(h)
+            empty_first(h)
+        for h in range(halves):
+            scatter_first(h)
+        for t in range(1, PACK):
+            for h in range(halves):
+                nc.scalar.copy(out=dx[t][:, h * HALF:(h + 1) * HALF], in_=accs[h][t][:])
 
         out_planes = out_0.rearrange("(p t) c -> p t c", t=PACK)
-        grouped = [sbuf("grouped%d" % c, [P, width, PACK], BF16) for c, width in enumerate(CHUNKS)]
-        for h in range(halves):
-            cols = slice(h * HALF, (h + 1) * HALF)
-            nc.vector.tensor_tensor(first_page[:].indirect(offsets[:, h * HALF // 16:(h + 1) * HALF // 16]), dx_first[h][:], gain[:, cols], MULT)
+        grouped = sbuf("grouped", [P, T, PACK], BF16)
         pages = [first_page]
-        for t, heir in ((1, "left1"), (2, "back1"), (3, "dx0_1")):
+        for t, heir in ((1, "left1"), (2, "dx0_0"), (3, "dx0_1")):
             page = sbuf("page%d" % t, [P, T], F32, tag=heir)
             nc.gpsimd.memset(page[:], 0.0)
             pages.append(page)
@@ -166,19 +176,25 @@ def tile_list_embg_tgq8_noneP_kernel(tc, dy, w_words, w_scales, wgo, offs, out_0
             if t > 0:
                 nc.vector.tensor_tensor(pages[t][:].indirect(offsets[:]), dx[t][:], gain[:], MULT)
             nc.sync.dma_start(out=out_planes[:, t, :], in_=pages[t][:])
-            for c, cols in enumerate(spans):
-                if t == PACK - 1 and c < ON_VECTOR:
-                    nc.vector.tensor_copy(out=grouped[c][:, :, t], in_=pages[t][:, cols])
-                elif t == PACK - 2 and c < ON_VECTOR:
-                    nc.scalar.copy(out=grouped[c][:, :, t:], in_=pages[t][:, cols].unsqueeze(2).to_broadcast([P, CHUNKS[c], 2]))
-                else:
-                    nc.scalar.copy(out=grouped[c][:, :, t], in_=pages[t][:, cols])
+            if t < PACK - 2:
+                nc.scalar.copy(out=grouped[:, :, t], in_=pages[t][:])
+            elif t == PACK - 2:
+                nc.scalar.copy(out=grouped[:, :ON_VECTOR, t:], in_=pages[t][:, :ON_VECTOR].unsqueeze(2).to_broadcast([P, ON_VECTOR, 2]))
+                nc.scalar.copy(out=grouped[:, ON_VECTOR:, t], in_=pages[t][:, ON_VECTOR:])
+            else:
+                for lo, hi in ((0, CHUNK), (CHUNK, ON_VECTOR)):
+                    nc.vector.tensor_copy(out=grouped[:, lo:hi, t], in_=pages[t][:, lo:hi])
+                for lo, hi in ((ON_VECTOR, 3 * CHUNK), (3 * CHUNK, T)):
+                    nc.scalar.copy(out=grouped[:, lo:hi, t], in_=pages[t][:, lo:hi])
 
         words_out = out_1[0].rearrange("p c i -> p (c i)").bitcast(I32)
-        y_scales = sbuf("y_scales", [P, T], U8)
-        for c, cols in enumerate(spans):
-            y_codes = sbuf("y_codes%d" % c, [P, CHUNKS[c]], U32)
-            nc.vector.quantize_mx(out=y_codes[:].bitcast(E4M3), scales=y_scales[:, cols], in_=flat(grouped[c][:]))
+        y_scales = sbuf("y_scales", [P, T // 2], U8)
+        for c in range(T // CHUNK):
+            cols = slice(c * CHUNK, (c + 1) * CHUNK)
+            upper, side = divmod(c, 2)
+            y_codes = sbuf("y_codes%d" % c, [P, CHUNK], U32)
+            nc.vector.quantize_mx(out=y_codes[:].bitcast(E4M3), scales=y_scales[4 * upper:, side * CHUNK:(side + 1) * CHUNK], in_=flat(grouped[:, cols, :]))
             nc.sync.dma_start(out=words_out[:, cols], in_=y_codes[:].bitcast(I32))
         for q in range(QUADS):
-            nc.scalar.dma_start(out=out_2[0, 4 * q:4 * q + 4, :].bitcast(I32), in_=y_scales[32 * q:32 * q + 4, :].bitcast(I32))
+            nc.scalar.dma_start(out=out_2[0, 4 * q:4 * q + 4, :].bitcast(I32).rearrange("r (u x) -> u r x", u=2),
+                                in_=y_scales[32 * q:32 * q + 8, :].bitcast(I32))

@@ -56,11 +56,12 @@ def tile_list_embg_tgq8_noneP_kernel(tc, dy, w_words, w_scales, wgo, offs, out_0
 
         dy_planes = dy.rearrange("(p t) j -> p t j", t=PACK)
         raw = [sbuf("raw%d" % c, [P, PACK, PIECE], F32) for c in range(pieces)]
+        w_in = sbuf("w_in", [P, N], I32, tag="slot3")
         for c in range(pieces):
+            if c == pieces - 1:
+                nc.sync.dma_start(out=w_in[:], in_=w_words[0].rearrange("p n i -> p (n i)").bitcast(I32))
             nc.sync.dma_start(out=raw[c][:], in_=dy_planes[:, :, c * PIECE:(c + 1) * PIECE])
 
-        w_in = sbuf("w_in", [P, N], I32)
-        nc.sync.dma_start(out=w_in[:], in_=w_words[0].rearrange("p n i -> p (n i)").bitcast(I32))
         ws_in = sbuf("ws_in", [P, N], U8)
         nc.vector.memset(ws_in[:].bitcast(I32), 0)
         for q in range(QUADS):
@@ -70,14 +71,14 @@ def tile_list_embg_tgq8_noneP_kernel(tc, dy, w_words, w_scales, wgo, offs, out_0
         gain = sbuf("gain", [P, J], F32)
         nc.sync.dma_start(out=gain[:], in_=wgo)
 
-        eye = sbuf("eye", [P, P], BF16)
+        eye = sbuf("eye", [P, P], BF16, tag="slot0")
         make_identity(nc, eye[:])
-        eye_in = sbuf("eye_in", [P, P, PACK], BF16, tag="ring0")
+        eye_in = sbuf("eye_in", [P, P, PACK], BF16, tag="slot2")
         nc.scalar.copy(out=eye_in[:], in_=eye[:].unsqueeze(2).to_broadcast([P, P, PACK]))
         row = P * PACK
         eye_codes = sbuf("eye_codes", [P, PACK * row + 64], U8)
         nc.vector.memset(eye_codes[:].bitcast(I32), 0)
-        eye_base = sbuf("eye_base", [P, P, PACK], U8, tag="ring1")
+        eye_base = sbuf("eye_base", [P, P, PACK], U8, tag="slot1")
         eye_scales = sbuf("eye_scales", [P, P], U8)
         nc.vector.quantize_mx(out=flat(eye_base[:]).bitcast(E4M3), scales=eye_scales[:], in_=flat(eye_in[:]))
         diagonal = eye_codes[:, 0:PACK * (row + 1)].rearrange("p (t x) -> p t x", t=PACK)[:, :, 0:row:PACK]
@@ -90,35 +91,46 @@ def tile_list_embg_tgq8_noneP_kernel(tc, dy, w_words, w_scales, wgo, offs, out_0
         q_scales = [sbuf("q_scales%d" % h, [P, HALF], U8) for h in range(halves)]
         r_codes = [sbuf("r_codes%d" % h, [P, HALF], U32) for h in range(halves)]
         r_scales = [sbuf("r_scales%d" % h, [P, HALF], U8) for h in range(halves)]
-        back = [sbuf("back%d" % h, [P, PACK, HALF], F32) for h in range(halves)]
+        back = [sbuf("back%d" % c, [P, PACK, PIECE], F32) for c in range(pieces)]
 
         def bank(h, t):
             return psum.tile([P, HALF], F32, name="bank%d" % (PACK * h + t))
 
-        for h in range(halves):
-            rounded = []
-            for s in range(per_half):
-                c = h * per_half + s
-                cols = slice(s * PIECE, (s + 1) * PIECE)
-                x = sbuf("rounded%d" % c, [P, PIECE, PACK], BF16, tag="ring%d" % s)
-                if c == 0:
-                    nc.scalar.copy(out=woven(x[:]), in_=planar(raw[c][:]))
-                else:
-                    nc.vector.tensor_copy(out=woven(x[:]), in_=planar(raw[c][:]))
-                rounded.append(x)
-            for s in range(per_half):
-                cols = slice(s * PIECE, (s + 1) * PIECE)
-                nc.vector.quantize_mx(out=q_codes[h][:, cols].bitcast(E5M2), scales=q_scales[h][:, cols], in_=flat(rounded[s][:]))
+        rounded = [sbuf("rounded%d" % c, [P, PIECE, PACK], BF16, tag="slot%d" % c) for c in range(pieces)]
+        w_codes = sbuf("w_codes", [P, PACK, P], I32, tag="slot0")
+        w_plane = sbuf("w_plane", [P, PACK, P], U8, tag="slot2")
+
+        def first(c):
+            h, s = divmod(c, per_half)
+            cols = slice(s * PIECE, (s + 1) * PIECE)
+            nc.vector.quantize_mx(out=q_codes[h][:, cols].bitcast(E5M2), scales=q_scales[h][:, cols], in_=flat(rounded[c][:]))
+
+        def bring_back(h):
+            accs = [bank(h, t) for t in range(PACK)]
             for t in range(PACK):
-                acc = bank(h, t)
-                nc.tensor.matmul_mx(out=acc[:], lhsT=eye_codes[:, t * row:(t + 1) * row].bitcast(E4M3), lhsT_scale=eye_scales[:],
+                nc.tensor.matmul_mx(out=accs[t][:], lhsT=eye_codes[:, t * row:(t + 1) * row].bitcast(E4M3), lhsT_scale=eye_scales[:],
                                     rhs=q_codes[h][:].bitcast(E5M2), rhs_scale=q_scales[h][:], start=True, stop=True)
-                nc.scalar.copy(out=back[h][:, t, :], in_=acc[:])
+            for s in range(per_half):
+                for t in range(PACK):
+                    nc.scalar.copy(out=back[h * per_half + s][:, t, :], in_=accs[t][:, s * PIECE:(s + 1) * PIECE])
+
+        nc.scalar.copy(out=woven(rounded[0][:]), in_=planar(raw[0][:]))
+        nc.vector.tensor_copy(out=woven(rounded[1][:]), in_=planar(raw[1][:]))
+        nc.scalar.copy(out=woven(rounded[2][:]), in_=planar(raw[2][:]))
+        first(0)
+        first(1)
+        bring_back(0)
+        nc.vector.tensor_copy(out=w_codes[:].rearrange("p t m -> p m t"), in_=w_in[:].rearrange("p (m t) -> p m t", t=PACK))
+        first(2)
+        nc.vector.tensor_copy(out=woven(rounded[3][:]), in_=planar(raw[3][:]))
+        nc.vector.tensor_copy(out=w_plane[:], in_=ws_in[:].rearrange("p (m t) -> p t m", t=PACK))
+        first(3)
+        bring_back(1)
 
         def subtract(c):
             h, s = divmod(c, per_half)
             left = sbuf("left%d" % c, [P, PIECE, PACK], BF16, tag="left%d" % s)
-            nc.vector.tensor_tensor(woven(left[:], 2), planar(raw[c][:], 2), planar(back[h][:, :, s * PIECE:(s + 1) * PIECE], 2), SUB)
+            nc.vector.tensor_tensor(woven(left[:], 2), planar(raw[c][:], 2), planar(back[c][:], 2), SUB)
             return left
 
         def second(c, left):
@@ -126,8 +138,6 @@ def tile_list_embg_tgq8_noneP_kernel(tc, dy, w_words, w_scales, wgo, offs, out_0
             cols = slice(s * PIECE, (s + 1) * PIECE)
             nc.vector.quantize_mx(out=r_codes[h][:, cols].bitcast(E4M3), scales=r_scales[h][:, cols], in_=flat(left[:]))
 
-        w_codes = sbuf("w_codes", [P, PACK, P], I32, tag="ring0")
-        w_plane = sbuf("w_plane", [P, PACK, P], U8, tag="ring1")
         accs = [[bank(h, t) for t in range(PACK)] for h in range(halves)]
 
         def products(h):
@@ -150,8 +160,6 @@ def tile_list_embg_tgq8_noneP_kernel(tc, dy, w_words, w_scales, wgo, offs, out_0
             lo, hi = starts[i], starts[i] + FIRST[i]
             nc.vector.tensor_tensor(first_page[:].indirect(offsets[:, lo // 16:hi // 16]), dx_first[i][:], gain[:, lo:hi], MULT)
 
-        nc.vector.tensor_copy(out=w_codes[:].rearrange("p t m -> p m t"), in_=w_in[:].rearrange("p (m t) -> p m t", t=PACK))
-        nc.vector.tensor_copy(out=w_plane[:], in_=ws_in[:].rearrange("p (m t) -> p t m", t=PACK))
         for h in range(halves):
             mine = range(h * per_half, (h + 1) * per_half)
             lefts = [subtract(c) for c in mine]

@@ -16,6 +16,7 @@ E4M3 = mybir.dt.float8_e4m3fn_x4
 E5M2 = mybir.dt.float8_e5m2_x4
 MULT = mybir.AluOpType.mult
 SUB = mybir.AluOpType.subtract
+ADD = mybir.AluOpType.add
 
 P = 128
 PACK = 4
@@ -38,7 +39,8 @@ def flat(tile3):
 PIECE = 256
 CHUNK = 512
 ON_VECTOR = 960
-FIRST = (512, 512)
+ON_SCALAR = 160
+FIRST = (256, 256, 512)
 
 
 def tile_list_embg_tgq8_noneP_kernel(tc, dy, w_words, w_scales, wgo, offs, out_0, out_1, out_2):
@@ -71,16 +73,19 @@ def tile_list_embg_tgq8_noneP_kernel(tc, dy, w_words, w_scales, wgo, offs, out_0
         gain = sbuf("gain", [P, J], F32)
         nc.sync.dma_start(out=gain[:], in_=wgo)
 
-        eye = sbuf("eye", [P, P], BF16, tag="slot0")
+        even = sbuf("even", [P, PIECE + ON_SCALAR, PACK], BF16)
+        small_eye = flat(even[:])[:, 0:P]
+        make_identity(nc, small_eye)
+        eye = sbuf("eye", [P, P], F32)
         make_identity(nc, eye[:])
-        eye_in = sbuf("eye_in", [P, P, PACK], BF16, tag="slot2")
-        nc.scalar.copy(out=eye_in[:], in_=eye[:].unsqueeze(2).to_broadcast([P, P, PACK]))
+        eye_in = even[:, PIECE + ON_SCALAR - P:, :]
+        nc.scalar.copy(out=eye_in, in_=small_eye.unsqueeze(2).to_broadcast([P, P, PACK]))
         row = P * PACK
         eye_codes = sbuf("eye_codes", [P, PACK * row + 64], U8)
         nc.vector.memset(eye_codes[:].bitcast(I32), 0)
         eye_base = sbuf("eye_base", [P, P, PACK], U8, tag="slot1")
         eye_scales = sbuf("eye_scales", [P, P], U8)
-        nc.vector.quantize_mx(out=flat(eye_base[:]).bitcast(E4M3), scales=eye_scales[:], in_=flat(eye_in[:]))
+        nc.vector.quantize_mx(out=flat(eye_base[:]).bitcast(E4M3), scales=eye_scales[:], in_=flat(eye_in))
         diagonal = eye_codes[:, 0:PACK * (row + 1)].rearrange("p (t x) -> p t x", t=PACK)[:, :, 0:row:PACK]
         nc.vector.tensor_copy(out=diagonal, in_=eye_base[:].rearrange("p m t -> p t m"))
 
@@ -91,98 +96,134 @@ def tile_list_embg_tgq8_noneP_kernel(tc, dy, w_words, w_scales, wgo, offs, out_0
         q_scales = [sbuf("q_scales%d" % h, [P, HALF], U8) for h in range(halves)]
         r_codes = [sbuf("r_codes%d" % h, [P, HALF], U32) for h in range(halves)]
         r_scales = [sbuf("r_scales%d" % h, [P, HALF], U8) for h in range(halves)]
-        back = [sbuf("back%d" % c, [P, PACK, PIECE], F32) for c in range(pieces)]
+        back = sbuf("back", [P, PACK, HALF], F32)
+        minus = [sbuf("minus%d" % s, [P, PACK, PIECE], F32) for s in range(per_half)]
+        left = [sbuf("left%d" % c, [P, PIECE, PACK], BF16) for c in range(per_half)]
+        banks = [[psum.tile([P, HALF], F32, name="bank%d" % (PACK * h + t)) for t in range(PACK)] for h in range(halves)]
 
-        def bank(h, t):
-            return psum.tile([P, HALF], F32, name="bank%d" % (PACK * h + t))
-
-        rounded = [sbuf("rounded%d" % c, [P, PIECE, PACK], BF16, tag="slot%d" % c) for c in range(pieces)]
-        w_codes = sbuf("w_codes", [P, PACK, P], I32, tag="slot0")
-        w_plane = sbuf("w_plane", [P, PACK, P], U8, tag="slot2")
+        rounded = [even[:, 0:PIECE, :], sbuf("rounded1", [P, PIECE, PACK], BF16, tag="slot1")[:],
+                   even[:, ON_SCALAR:, :], sbuf("rounded3", [P, PIECE, PACK], BF16, tag="slot3")[:]]
+        w_codes = sbuf("w_codes", [P, PACK, P], I32, tag="slot1")
+        w_plane = sbuf("w_plane", [P, PACK, P], U8, tag="even")
 
         def first(c):
             h, s = divmod(c, per_half)
             cols = slice(s * PIECE, (s + 1) * PIECE)
-            nc.vector.quantize_mx(out=q_codes[h][:, cols].bitcast(E5M2), scales=q_scales[h][:, cols], in_=flat(rounded[c][:]))
+            nc.vector.quantize_mx(out=q_codes[h][:, cols].bitcast(E5M2), scales=q_scales[h][:, cols], in_=flat(rounded[c]))
 
         def bring_back(h):
-            accs = [bank(h, t) for t in range(PACK)]
             for t in range(PACK):
-                nc.tensor.matmul_mx(out=accs[t][:], lhsT=eye_codes[:, t * row:(t + 1) * row].bitcast(E4M3), lhsT_scale=eye_scales[:],
+                nc.tensor.matmul_mx(out=banks[h][t][:], lhsT=eye_codes[:, t * row:(t + 1) * row].bitcast(E4M3), lhsT_scale=eye_scales[:],
                                     rhs=q_codes[h][:].bitcast(E5M2), rhs_scale=q_scales[h][:], start=True, stop=True)
-            for s in range(per_half):
-                for t in range(PACK):
-                    nc.scalar.copy(out=back[h * per_half + s][:, t, :], in_=accs[t][:, s * PIECE:(s + 1) * PIECE])
 
-        nc.scalar.copy(out=woven(rounded[0][:]), in_=planar(raw[0][:]))
-        nc.vector.tensor_copy(out=woven(rounded[1][:]), in_=planar(raw[1][:]))
-        nc.scalar.copy(out=woven(rounded[2][:]), in_=planar(raw[2][:]))
+        nc.scalar.copy(out=woven(rounded[0]), in_=planar(raw[0][:]))
+        nc.vector.tensor_copy(out=woven(rounded[1]), in_=planar(raw[1][:]))
+        cut = PIECE - ON_SCALAR
+        nc.scalar.copy(out=woven(rounded[2][:, cut:, :]), in_=planar(raw[2][:, :, cut:]))
         first(0)
         first(1)
         bring_back(0)
+        for t in range(PACK):
+            nc.scalar.copy(out=back[:, t, :], in_=banks[0][t][:])
+        nc.vector.tensor_copy(out=woven(rounded[2][:, 0:cut, :]), in_=planar(raw[2][:, :, 0:cut]))
         nc.vector.tensor_copy(out=w_codes[:].rearrange("p t m -> p m t"), in_=w_in[:].rearrange("p (m t) -> p m t", t=PACK))
         first(2)
-        nc.vector.tensor_copy(out=woven(rounded[3][:]), in_=planar(raw[3][:]))
+        nc.vector.tensor_copy(out=woven(rounded[3]), in_=planar(raw[3][:]))
         nc.vector.tensor_copy(out=w_plane[:], in_=ws_in[:].rearrange("p (m t) -> p t m", t=PACK))
         first(3)
         bring_back(1)
 
-        def subtract(c):
-            h, s = divmod(c, per_half)
-            left = sbuf("left%d" % c, [P, PIECE, PACK], BF16, tag="left%d" % s)
-            nc.vector.tensor_tensor(woven(left[:], 2), planar(raw[c][:], 2), planar(back[c][:], 2), SUB)
-            return left
-
-        def second(c, left):
-            h, s = divmod(c, per_half)
-            cols = slice(s * PIECE, (s + 1) * PIECE)
-            nc.vector.quantize_mx(out=r_codes[h][:, cols].bitcast(E4M3), scales=r_scales[h][:, cols], in_=flat(left[:]))
-
-        accs = [[bank(h, t) for t in range(PACK)] for h in range(halves)]
-
-        def products(h):
+        for s in reversed(range(per_half)):
             for t in range(PACK):
-                nc.tensor.matmul_mx(out=accs[h][t][:], lhsT=w_codes[:, t, :].bitcast(E4M3), lhsT_scale=w_plane[:, t, :],
-                                    rhs=q_codes[h][:].bitcast(E5M2), rhs_scale=q_scales[h][:], start=True, stop=False)
-            for t in range(PACK):
-                nc.tensor.matmul_mx(out=accs[h][t][:], lhsT=w_codes[:, t, :].bitcast(E4M3), lhsT_scale=w_plane[:, t, :],
-                                    rhs=r_codes[h][:].bitcast(E4M3), rhs_scale=r_scales[h][:], start=False, stop=True)
+                nc.scalar.mul(minus[s][:, t, :], banks[1][t][:, s * PIECE:(s + 1) * PIECE], -1.0)
+
+        def product(h, t, codes, scales, fmt, opens):
+            nc.tensor.matmul_mx(out=banks[h][t][:], lhsT=w_codes[:, t, :].bitcast(E4M3), lhsT_scale=w_plane[:, t, :],
+                                rhs=codes[h][:].bitcast(fmt), rhs_scale=scales[h][:], start=opens, stop=not opens)
+
+        def upper(h, t):
+            product(h, t, q_codes, q_scales, E5M2, True)
+
+        def lower(h, t):
+            product(h, t, r_codes, r_scales, E4M3, False)
 
         starts = [sum(FIRST[:i]) for i in range(len(FIRST))]
-        dx_first = [sbuf("dx0_%d" % i, [P, width], F32) for i, width in enumerate(FIRST)]
-        dx = [None] + [sbuf("dx%d" % t, [P, J], F32) for t in range(1, PACK)]
+        spill = sbuf("spill", [P, J + 2 * PIECE], F32)
+        turned = [spill[:, J + PIECE:], spill[:, P // 2:P // 2 + PIECE]]
+        dx_first = [sbuf("dx0_0", [P, FIRST[0]], F32)[:], spill[:, 0:FIRST[1]], sbuf("dx0_2", [P, FIRST[2]], F32)[:]]
+        dx = [None, spill[:, PIECE:PIECE + J]] + [None, None]
 
         def empty_first(i):
             h, at = divmod(starts[i], HALF)
-            nc.scalar.copy(out=dx_first[i][:], in_=accs[h][0][:, at:at + FIRST[i]])
+            nc.scalar.copy(out=dx_first[i], in_=banks[h][0][:, at:at + FIRST[i]])
 
         def scatter_first(i):
             lo, hi = starts[i], starts[i] + FIRST[i]
-            nc.vector.tensor_tensor(first_page[:].indirect(offsets[:, lo // 16:hi // 16]), dx_first[i][:], gain[:, lo:hi], MULT)
+            nc.vector.tensor_tensor(first_page[:].indirect(offsets[:, lo // 16:hi // 16]), dx_first[i], gain[:, lo:hi], MULT)
 
-        for h in range(halves):
-            mine = range(h * per_half, (h + 1) * per_half)
-            lefts = [subtract(c) for c in mine]
-            for c, left in zip(mine, lefts):
-                second(c, left)
-            products(h)
-            empty_first(h)
-        for h in range(halves):
-            scatter_first(h)
+        blocks = PIECE // P
+        sums = [banks[0][2 + b] for b in range(blocks)]
+        pairs = sums
+        upper(0, 0)
+        for b in range(blocks):
+            for t in range(PACK):
+                nc.tensor.matmul(sums[b][:, t * P:(t + 1) * P], lhsT=raw[pieces - 1][:, t, b * P:(b + 1) * P], rhs=eye[:],
+                                 is_transpose=True, start=(t == 0), stop=False)
+
+        for c in range(per_half):
+            nc.vector.tensor_tensor(woven(left[c][:], 2), planar(raw[c][:], 2), planar(back[:, :, c * PIECE:(c + 1) * PIECE], 2), SUB)
+        for c in range(per_half):
+            cols = slice(c * PIECE, (c + 1) * PIECE)
+            nc.vector.quantize_mx(out=r_codes[0][:, cols].bitcast(E4M3), scales=r_scales[0][:, cols], in_=flat(left[c][:]))
+        lower(0, 0)
+        empty_first(0)
+
+        late = sbuf("late", [P, HALF, PACK], BF16, tag="left0")
+        nc.vector.tensor_tensor(woven(late[:, 0:PIECE, :], 2), planar(raw[per_half][:], 2), planar(minus[0][:], 2), ADD)
+        scatter_first(0)
+
+        late_words = flat(late[:]).bitcast(F32)
+        for t in range(PACK):
+            for b in range(blocks):
+                nc.tensor.matmul(sums[b][:, t * P:(t + 1) * P], lhsT=minus[1][:, t, b * P:(b + 1) * P], rhs=eye[:],
+                                 is_transpose=True, start=False, stop=(t == PACK - 1))
+        upper(1, 0)
+        for b in range(blocks):
+            nc.scalar.copy(out=turned[b].bitcast(BF16).rearrange("p (u m e) -> p u m e", u=2, e=2),
+                           in_=sums[b][:].rearrange("p (u e m) -> p u m e", u=2, e=2))
+        for b in range(blocks):
+            for u in range(2):
+                nc.tensor.transpose(pairs[b][:, u * P:(u + 1) * P], turned[b][:, u * P:(u + 1) * P], eye[:])
+        for b in range(blocks):
+            at = 2 * (PIECE + b * P)
+            nc.scalar.copy(out=late_words[:, at:at + 2 * P].rearrange("p (j u) -> p j u", u=2),
+                           in_=pairs[b][:, 0:2 * P].rearrange("p (u j) -> p j u", u=2))
+        nc.vector.quantize_mx(out=r_codes[1][:].bitcast(E4M3), scales=r_scales[1][:], in_=flat(late[:]))
+        empty_first(1)
+        lower(1, 0)
+        empty_first(2)
+        scatter_first(1)
+        scatter_first(2)
         for t in range(1, PACK):
             for h in range(halves):
-                nc.scalar.copy(out=dx[t][:, h * HALF:(h + 1) * HALF], in_=accs[h][t][:])
+                upper(h, t)
+                lower(h, t)
+        later = sbuf("later", [P, 2 * J], F32, tag="r_scales1")
+        dx[2:] = [later[:, 0:J], later[:, J:]]
+        for t in range(1, PACK):
+            for h in range(halves):
+                nc.scalar.copy(out=dx[t][:, h * HALF:(h + 1) * HALF], in_=banks[h][t][:])
 
         out_planes = out_0.rearrange("(p t) c -> p t c", t=PACK)
-        grouped = sbuf("grouped", [P, T, PACK], BF16)
+        grouped = sbuf("grouped", [P, T, PACK], BF16, tag="r_codes1")
         pages = [first_page]
-        for t, heir in ((1, "left1"), (2, "dx0_0"), (3, "dx0_1")):
+        for t, heir in ((1, "left0"), (2, "even"), (3, "dx0_2")):
             page = sbuf("page%d" % t, [P, T], F32, tag=heir)
             nc.gpsimd.memset(page[:], 0.0)
             pages.append(page)
         for t in range(PACK):
             if t > 0:
-                nc.vector.tensor_tensor(pages[t][:].indirect(offsets[:]), dx[t][:], gain[:], MULT)
+                nc.vector.tensor_tensor(pages[t][:].indirect(offsets[:]), dx[t], gain[:], MULT)
             nc.sync.dma_start(out=out_planes[:, t, :], in_=pages[t][:])
             if t < PACK - 2:
                 nc.scalar.copy(out=grouped[:, :, t], in_=pages[t][:])

@@ -20,8 +20,16 @@ ADD = mybir.AluOpType.add
 
 P = 128
 PACK = 4
-HALF = 512
 QUADS = 4
+GROUP = 16
+HALF = 512
+PIECE = 256
+CHUNK = 512
+PAD = 64
+
+THIRD_ON_SCALAR = 160
+LAST_ON_VECTOR = 1024
+FIRST_PARTS = (256, 256, 512)
 
 
 def woven(tile3, run=PACK):
@@ -34,13 +42,6 @@ def planar(tile3, run=PACK):
 
 def flat(tile3):
     return tile3.rearrange("p a b -> p (a b)")
-
-
-PIECE = 256
-CHUNK = 512
-ON_VECTOR = 960
-ON_SCALAR = 160
-FIRST = (256, 256, 512)
 
 
 def tile_list_embg_tgq8_noneP_kernel(tc, dy, w_words, w_scales, wgo, offs, out_0, out_1, out_2):
@@ -68,20 +69,20 @@ def tile_list_embg_tgq8_noneP_kernel(tc, dy, w_words, w_scales, wgo, offs, out_0
         nc.vector.memset(ws_in[:].bitcast(I32), 0)
         for q in range(QUADS):
             nc.sync.dma_start(out=ws_in[32 * q:32 * q + 4, :].bitcast(I32), in_=w_scales[0, 4 * q:4 * q + 4, :].bitcast(I32))
-        offsets = sb.tile([P, J // 16], U16, name="offsets")
+        offsets = sb.tile([P, J // GROUP], U16, name="offsets")
         nc.sync.dma_start(offsets[:], offs)
         gain = sbuf("gain", [P, J], F32)
         nc.sync.dma_start(out=gain[:], in_=wgo)
 
-        even = sbuf("even", [P, PIECE + ON_SCALAR, PACK], BF16)
+        even = sbuf("even", [P, PIECE + THIRD_ON_SCALAR, PACK], BF16)
         small_eye = flat(even[:])[:, 0:P]
         make_identity(nc, small_eye)
         eye = sbuf("eye", [P, P], F32)
         make_identity(nc, eye[:])
-        eye_in = even[:, PIECE + ON_SCALAR - P:, :]
+        eye_in = even[:, PIECE + THIRD_ON_SCALAR - P:, :]
         nc.scalar.copy(out=eye_in, in_=small_eye.unsqueeze(2).to_broadcast([P, P, PACK]))
         row = P * PACK
-        eye_codes = sbuf("eye_codes", [P, PACK * row + 64], U8)
+        eye_codes = sbuf("eye_codes", [P, PACK * row + PAD], U8)
         nc.vector.memset(eye_codes[:].bitcast(I32), 0)
         eye_base = sbuf("eye_base", [P, P, PACK], U8, tag="slot1")
         eye_scales = sbuf("eye_scales", [P, P], U8)
@@ -102,11 +103,11 @@ def tile_list_embg_tgq8_noneP_kernel(tc, dy, w_words, w_scales, wgo, offs, out_0
         banks = [[psum.tile([P, HALF], F32, name="bank%d" % (PACK * h + t)) for t in range(PACK)] for h in range(halves)]
 
         rounded = [even[:, 0:PIECE, :], sbuf("rounded1", [P, PIECE, PACK], BF16, tag="slot1")[:],
-                   even[:, ON_SCALAR:, :], sbuf("rounded3", [P, PIECE, PACK], BF16, tag="slot3")[:]]
+                   even[:, THIRD_ON_SCALAR:, :], sbuf("rounded3", [P, PIECE, PACK], BF16, tag="slot3")[:]]
         w_codes = sbuf("w_codes", [P, PACK, P], I32, tag="slot1")
         w_plane = sbuf("w_plane", [P, PACK, P], U8, tag="even")
 
-        def first(c):
+        def quantise_first_tier(c):
             h, s = divmod(c, per_half)
             cols = slice(s * PIECE, (s + 1) * PIECE)
             nc.vector.quantize_mx(out=q_codes[h][:, cols].bitcast(E5M2), scales=q_scales[h][:, cols], in_=flat(rounded[c]))
@@ -118,19 +119,19 @@ def tile_list_embg_tgq8_noneP_kernel(tc, dy, w_words, w_scales, wgo, offs, out_0
 
         nc.scalar.copy(out=woven(rounded[0]), in_=planar(raw[0][:]))
         nc.vector.tensor_copy(out=woven(rounded[1]), in_=planar(raw[1][:]))
-        cut = PIECE - ON_SCALAR
+        cut = PIECE - THIRD_ON_SCALAR
         nc.scalar.copy(out=woven(rounded[2][:, cut:, :]), in_=planar(raw[2][:, :, cut:]))
-        first(0)
-        first(1)
+        quantise_first_tier(0)
+        quantise_first_tier(1)
         bring_back(0)
         for t in range(PACK):
             nc.scalar.copy(out=back[:, t, :], in_=banks[0][t][:])
         nc.vector.tensor_copy(out=woven(rounded[2][:, 0:cut, :]), in_=planar(raw[2][:, :, 0:cut]))
         nc.vector.tensor_copy(out=w_codes[:].rearrange("p t m -> p m t"), in_=w_in[:].rearrange("p (m t) -> p m t", t=PACK))
-        first(2)
+        quantise_first_tier(2)
         nc.vector.tensor_copy(out=woven(rounded[3]), in_=planar(raw[3][:]))
         nc.vector.tensor_copy(out=w_plane[:], in_=ws_in[:].rearrange("p (m t) -> p t m", t=PACK))
-        first(3)
+        quantise_first_tier(3)
         bring_back(1)
 
         for s in reversed(range(per_half)):
@@ -141,30 +142,28 @@ def tile_list_embg_tgq8_noneP_kernel(tc, dy, w_words, w_scales, wgo, offs, out_0
             nc.tensor.matmul_mx(out=banks[h][t][:], lhsT=w_codes[:, t, :].bitcast(E4M3), lhsT_scale=w_plane[:, t, :],
                                 rhs=codes[h][:].bitcast(fmt), rhs_scale=scales[h][:], start=opens, stop=not opens)
 
-        def upper(h, t):
+        def first_tier_pass(h, t):
             product(h, t, q_codes, q_scales, E5M2, True)
 
-        def lower(h, t):
+        def second_tier_pass(h, t):
             product(h, t, r_codes, r_scales, E4M3, False)
 
-        starts = [sum(FIRST[:i]) for i in range(len(FIRST))]
+        starts = [sum(FIRST_PARTS[:i]) for i in range(len(FIRST_PARTS))]
         spill = sbuf("spill", [P, J + 2 * PIECE], F32)
         turned = [spill[:, J + PIECE:], spill[:, P // 2:P // 2 + PIECE]]
-        dx_first = [sbuf("dx0_0", [P, FIRST[0]], F32)[:], spill[:, 0:FIRST[1]], sbuf("dx0_2", [P, FIRST[2]], F32)[:]]
-        dx = [None, spill[:, PIECE:PIECE + J]] + [None, None]
+        dx_first = [sbuf("dx0_0", [P, FIRST_PARTS[0]], F32)[:], spill[:, 0:FIRST_PARTS[1]], sbuf("dx0_2", [P, FIRST_PARTS[2]], F32)[:]]
 
         def empty_first(i):
             h, at = divmod(starts[i], HALF)
-            nc.scalar.copy(out=dx_first[i], in_=banks[h][0][:, at:at + FIRST[i]])
+            nc.scalar.copy(out=dx_first[i], in_=banks[h][0][:, at:at + FIRST_PARTS[i]])
 
         def scatter_first(i):
-            lo, hi = starts[i], starts[i] + FIRST[i]
-            nc.vector.tensor_tensor(first_page[:].indirect(offsets[:, lo // 16:hi // 16]), dx_first[i], gain[:, lo:hi], MULT)
+            lo, hi = starts[i], starts[i] + FIRST_PARTS[i]
+            nc.vector.tensor_tensor(first_page[:].indirect(offsets[:, lo // GROUP:hi // GROUP]), dx_first[i], gain[:, lo:hi], MULT)
 
         blocks = PIECE // P
-        sums = [banks[0][2 + b] for b in range(blocks)]
-        pairs = sums
-        upper(0, 0)
+        sums = banks[0][PACK - blocks:]
+        first_tier_pass(0, 0)
         for b in range(blocks):
             for t in range(PACK):
                 nc.tensor.matmul(sums[b][:, t * P:(t + 1) * P], lhsT=raw[pieces - 1][:, t, b * P:(b + 1) * P], rhs=eye[:],
@@ -175,7 +174,7 @@ def tile_list_embg_tgq8_noneP_kernel(tc, dy, w_words, w_scales, wgo, offs, out_0
         for c in range(per_half):
             cols = slice(c * PIECE, (c + 1) * PIECE)
             nc.vector.quantize_mx(out=r_codes[0][:, cols].bitcast(E4M3), scales=r_scales[0][:, cols], in_=flat(left[c][:]))
-        lower(0, 0)
+        second_tier_pass(0, 0)
         empty_first(0)
 
         late = sbuf("late", [P, HALF, PACK], BF16, tag="left0")
@@ -187,29 +186,29 @@ def tile_list_embg_tgq8_noneP_kernel(tc, dy, w_words, w_scales, wgo, offs, out_0
             for b in range(blocks):
                 nc.tensor.matmul(sums[b][:, t * P:(t + 1) * P], lhsT=minus[1][:, t, b * P:(b + 1) * P], rhs=eye[:],
                                  is_transpose=True, start=False, stop=(t == PACK - 1))
-        upper(1, 0)
+        first_tier_pass(1, 0)
         for b in range(blocks):
             nc.scalar.copy(out=turned[b].bitcast(BF16).rearrange("p (u m e) -> p u m e", u=2, e=2),
                            in_=sums[b][:].rearrange("p (u e m) -> p u m e", u=2, e=2))
         for b in range(blocks):
             for u in range(2):
-                nc.tensor.transpose(pairs[b][:, u * P:(u + 1) * P], turned[b][:, u * P:(u + 1) * P], eye[:])
+                nc.tensor.transpose(sums[b][:, u * P:(u + 1) * P], turned[b][:, u * P:(u + 1) * P], eye[:])
         for b in range(blocks):
             at = 2 * (PIECE + b * P)
             nc.scalar.copy(out=late_words[:, at:at + 2 * P].rearrange("p (j u) -> p j u", u=2),
-                           in_=pairs[b][:, 0:2 * P].rearrange("p (u j) -> p j u", u=2))
+                           in_=sums[b][:, 0:2 * P].rearrange("p (u j) -> p j u", u=2))
         nc.vector.quantize_mx(out=r_codes[1][:].bitcast(E4M3), scales=r_scales[1][:], in_=flat(late[:]))
         empty_first(1)
-        lower(1, 0)
+        second_tier_pass(1, 0)
         empty_first(2)
         scatter_first(1)
         scatter_first(2)
+
         for t in range(1, PACK):
             for h in range(halves):
-                upper(h, t)
-                lower(h, t)
-        later = sbuf("later", [P, 2 * J], F32, tag="r_scales1")
-        dx[2:] = [later[:, 0:J], later[:, J:]]
+                first_tier_pass(h, t)
+                second_tier_pass(h, t)
+        dx = {1: spill[:, PIECE:PIECE + J], 2: sbuf("dx2", [P, J], F32)[:], 3: sbuf("dx3", [P, J], F32)[:]}
         for t in range(1, PACK):
             for h in range(halves):
                 nc.scalar.copy(out=dx[t][:, h * HALF:(h + 1) * HALF], in_=banks[h][t][:])
@@ -217,8 +216,8 @@ def tile_list_embg_tgq8_noneP_kernel(tc, dy, w_words, w_scales, wgo, offs, out_0
         out_planes = out_0.rearrange("(p t) c -> p t c", t=PACK)
         grouped = sbuf("grouped", [P, T, PACK], BF16, tag="r_codes1")
         pages = [first_page]
-        for t, heir in ((1, "left0"), (2, "even"), (3, "dx0_2")):
-            page = sbuf("page%d" % t, [P, T], F32, tag=heir)
+        for t, freed in ((1, "left0"), (2, "even"), (3, "dx0_2")):
+            page = sbuf("page%d" % t, [P, T], F32, tag=freed)
             nc.gpsimd.memset(page[:], 0.0)
             pages.append(page)
         for t in range(PACK):
@@ -228,21 +227,23 @@ def tile_list_embg_tgq8_noneP_kernel(tc, dy, w_words, w_scales, wgo, offs, out_0
             if t < PACK - 2:
                 nc.scalar.copy(out=grouped[:, :, t], in_=pages[t][:])
             elif t == PACK - 2:
-                nc.scalar.copy(out=grouped[:, :ON_VECTOR, t:], in_=pages[t][:, :ON_VECTOR].unsqueeze(2).to_broadcast([P, ON_VECTOR, 2]))
-                nc.scalar.copy(out=grouped[:, ON_VECTOR:, t], in_=pages[t][:, ON_VECTOR:])
+                nc.scalar.copy(out=grouped[:, :LAST_ON_VECTOR, t:],
+                               in_=pages[t][:, :LAST_ON_VECTOR].unsqueeze(2).to_broadcast([P, LAST_ON_VECTOR, 2]))
+                nc.scalar.copy(out=grouped[:, LAST_ON_VECTOR:, t], in_=pages[t][:, LAST_ON_VECTOR:])
             else:
-                for lo, hi in ((0, CHUNK), (CHUNK, ON_VECTOR)):
-                    nc.vector.tensor_copy(out=grouped[:, lo:hi, t], in_=pages[t][:, lo:hi])
-                for lo, hi in ((ON_VECTOR, 3 * CHUNK), (3 * CHUNK, T)):
-                    nc.scalar.copy(out=grouped[:, lo:hi, t], in_=pages[t][:, lo:hi])
+                for lo in range(0, LAST_ON_VECTOR, CHUNK):
+                    nc.vector.tensor_copy(out=grouped[:, lo:lo + CHUNK, t], in_=pages[t][:, lo:lo + CHUNK])
+                for lo in range(LAST_ON_VECTOR, T, CHUNK):
+                    nc.scalar.copy(out=grouped[:, lo:lo + CHUNK, t], in_=pages[t][:, lo:lo + CHUNK])
 
         words_out = out_1[0].rearrange("p c i -> p (c i)").bitcast(I32)
         y_scales = sbuf("y_scales", [P, T // 2], U8)
         for c in range(T // CHUNK):
             cols = slice(c * CHUNK, (c + 1) * CHUNK)
-            upper, side = divmod(c, 2)
+            shift, side = divmod(c, 2)
             y_codes = sbuf("y_codes%d" % c, [P, CHUNK], U32)
-            nc.vector.quantize_mx(out=y_codes[:].bitcast(E4M3), scales=y_scales[4 * upper:, side * CHUNK:(side + 1) * CHUNK], in_=flat(grouped[:, cols, :]))
+            nc.vector.quantize_mx(out=y_codes[:].bitcast(E4M3), scales=y_scales[4 * shift:, side * CHUNK:(side + 1) * CHUNK],
+                                  in_=flat(grouped[:, cols, :]))
             nc.sync.dma_start(out=words_out[:, cols], in_=y_codes[:].bitcast(I32))
         for q in range(QUADS):
             nc.scalar.dma_start(out=out_2[0, 4 * q:4 * q + 4, :].bitcast(I32).rearrange("r (u x) -> u r x", u=2),

@@ -1,7 +1,6 @@
 from contextlib import ExitStack
 
 import concourse.mybir as mybir
-from concourse.masks import make_identity
 
 K, N, T, J = 512, 512, 2048, 1024
 FLOPS = 2 * K * N * J * 3
@@ -16,7 +15,6 @@ E4M3 = mybir.dt.float8_e4m3fn_x4
 E5M2 = mybir.dt.float8_e5m2_x4
 MULT = mybir.AluOpType.mult
 SUB = mybir.AluOpType.subtract
-ADD = mybir.AluOpType.add
 
 P = 128
 PACK = 4
@@ -27,9 +25,9 @@ PIECE = 256
 CHUNK = 512
 PAD = 64
 
-THIRD_ON_SCALAR = 160
+BLOCK = 128
 LAST_ON_VECTOR = 1024
-FIRST_PARTS = (256, 256, 512)
+SEAM = 16
 
 
 def woven(tile3, run=PACK):
@@ -46,8 +44,6 @@ def flat(tile3):
 
 def tile_list_embg_tgq8_noneP_kernel(tc, dy, w_words, w_scales, wgo, offs, out_0, out_1, out_2):
     nc = tc.nc
-    halves = J // HALF
-    per_half = HALF // PIECE
     pieces = J // PIECE
 
     with ExitStack() as ctx:
@@ -59,192 +55,259 @@ def tile_list_embg_tgq8_noneP_kernel(tc, dy, w_words, w_scales, wgo, offs, out_0
 
         dy_planes = dy.rearrange("(p t) j -> p t j", t=PACK)
         raw = [sbuf("raw%d" % c, [P, PACK, PIECE], F32) for c in range(pieces)]
-        w_in = sbuf("w_in", [P, N], I32, tag="slot3")
-        for c in range(pieces):
-            if c == pieces - 1:
-                nc.sync.dma_start(out=w_in[:], in_=w_words[0].rearrange("p n i -> p (n i)").bitcast(I32))
+
+        def load_piece(c):
             nc.sync.dma_start(out=raw[c][:], in_=dy_planes[:, :, c * PIECE:(c + 1) * PIECE])
 
         ws_in = sbuf("ws_in", [P, N], U8)
-        nc.vector.memset(ws_in[:].bitcast(I32), 0)
+        nc.gpsimd.memset(ws_in[:].bitcast(I32), 0)
+        load_piece(0)
+        w_in = sbuf("w_in", [P, N], I32)
+        nc.sync.dma_start(out=w_in[:], in_=w_words[0].rearrange("p n i -> p (n i)").bitcast(I32))
         for q in range(QUADS):
             nc.sync.dma_start(out=ws_in[32 * q:32 * q + 4, :].bitcast(I32), in_=w_scales[0, 4 * q:4 * q + 4, :].bitcast(I32))
+        load_piece(1)
+        load_piece(2)
         offsets = sb.tile([P, J // GROUP], U16, name="offsets")
         nc.sync.dma_start(offsets[:], offs)
-        gain = sbuf("gain", [P, J], F32)
-        nc.sync.dma_start(out=gain[:], in_=wgo)
+        gain = [sbuf("gain%d" % h, [P, HALF], F32) for h in range(2)]
+        nc.sync.dma_start(out=gain[0][:], in_=wgo[:, 0:HALF])
+        load_piece(3)
+        nc.sync.dma_start(out=gain[1][:], in_=wgo[:, HALF:])
 
-        even = sbuf("even", [P, PIECE + THIRD_ON_SCALAR, PACK], BF16)
-        small_eye = flat(even[:])[:, 0:P]
-        make_identity(nc, small_eye)
+        stage = sbuf("stage", [P, 2 * PIECE, PACK], BF16)
+        ones = sbuf("ones", [P, P], F32, tag="page0")
+        nc.gpsimd.memset(ones[:], 1.0)
         eye = sbuf("eye", [P, P], F32)
-        make_identity(nc, eye[:])
-        eye_in = even[:, PIECE + THIRD_ON_SCALAR - P:, :]
-        nc.scalar.copy(out=eye_in, in_=small_eye.unsqueeze(2).to_broadcast([P, P, PACK]))
+        nc.gpsimd.affine_select(out=eye[:], in_=ones[:], pattern=[[-1, P]], compare_op=mybir.AluOpType.is_equal, fill=0.0, base=0, channel_multiplier=1)
+        eye_in = stage[:, PIECE - P // 2:PIECE + P // 2, :]
+        nc.scalar.copy(out=eye_in, in_=eye[:].unsqueeze(2).to_broadcast([P, P, PACK]))
         row = P * PACK
         eye_codes = sbuf("eye_codes", [P, PACK * row + PAD], U8)
         nc.vector.memset(eye_codes[:].bitcast(I32), 0)
-        eye_base = sbuf("eye_base", [P, P, PACK], U8, tag="slot1")
+        eye_base = sbuf("eye_base", [P, P, PACK], U8, tag="slot0")
         eye_scales = sbuf("eye_scales", [P, P], U8)
         nc.vector.quantize_mx(out=flat(eye_base[:]).bitcast(E4M3), scales=eye_scales[:], in_=flat(eye_in))
         diagonal = eye_codes[:, 0:PACK * (row + 1)].rearrange("p (t x) -> p t x", t=PACK)[:, :, 0:row:PACK]
         nc.vector.tensor_copy(out=diagonal, in_=eye_base[:].rearrange("p m t -> p t m"))
 
-        first_page = sbuf("page0", [P, T], F32)
-        nc.vector.memset(first_page[:].bitcast(I32), 0)
+        pages = {0: sbuf("page0", [P, T], F32)}
+        nc.vector.memset(pages[0][:, 0:T // 2].bitcast(I32), 0)
+        nc.gpsimd.memset(pages[0][:, T // 2:], 0.0)
 
-        q_codes = [sbuf("q_codes%d" % h, [P, HALF], U32) for h in range(halves)]
-        q_scales = [sbuf("q_scales%d" % h, [P, HALF], U8) for h in range(halves)]
-        r_codes = [sbuf("r_codes%d" % h, [P, HALF], U32) for h in range(halves)]
-        r_scales = [sbuf("r_scales%d" % h, [P, HALF], U8) for h in range(halves)]
-        back = sbuf("back", [P, PACK, HALF], F32)
-        minus = [sbuf("minus%d" % s, [P, PACK, PIECE], F32) for s in range(per_half)]
-        left = [sbuf("left%d" % c, [P, PIECE, PACK], BF16) for c in range(per_half)]
-        banks = [[psum.tile([P, HALF], F32, name="bank%d" % (PACK * h + t)) for t in range(PACK)] for h in range(halves)]
+        banks = [psum.tile([P, HALF], F32, name="bank%d" % b) for b in range(8)]
 
-        rounded = [even[:, 0:PIECE, :], sbuf("rounded1", [P, PIECE, PACK], BF16, tag="slot1")[:],
-                   even[:, THIRD_ON_SCALAR:, :], sbuf("rounded3", [P, PIECE, PACK], BF16, tag="slot3")[:]]
-        w_codes = sbuf("w_codes", [P, PACK, P], I32, tag="slot1")
-        w_plane = sbuf("w_plane", [P, PACK, P], U8, tag="even")
+        def raw_block(b):
+            c, s = divmod(b, 2)
+            return raw[c][:, :, s * BLOCK:(s + 1) * BLOCK]
 
-        def quantise_first_tier(c):
-            h, s = divmod(c, per_half)
-            cols = slice(s * PIECE, (s + 1) * PIECE)
-            nc.vector.quantize_mx(out=q_codes[h][:, cols].bitcast(E5M2), scales=q_scales[h][:, cols], in_=flat(rounded[c]))
+        def quantise(codes, scales, values, fmt):
+            nc.vector.quantize_mx(out=codes.bitcast(fmt), scales=scales, in_=flat(values))
 
-        def bring_back(h):
+        def bring_back(bank, codes, scales):
             for t in range(PACK):
-                nc.tensor.matmul_mx(out=banks[h][t][:], lhsT=eye_codes[:, t * row:(t + 1) * row].bitcast(E4M3), lhsT_scale=eye_scales[:],
-                                    rhs=q_codes[h][:].bitcast(E5M2), rhs_scale=q_scales[h][:], start=True, stop=True)
+                nc.tensor.matmul_mx(out=bank[:, t * BLOCK:(t + 1) * BLOCK], lhsT=eye_codes[:, t * row:(t + 1) * row].bitcast(E4M3),
+                                    lhsT_scale=eye_scales[:], rhs=codes.bitcast(E5M2), rhs_scale=scales, start=True, stop=True)
 
-        nc.scalar.copy(out=woven(rounded[0]), in_=planar(raw[0][:]))
-        nc.vector.tensor_copy(out=woven(rounded[1]), in_=planar(raw[1][:]))
-        cut = PIECE - THIRD_ON_SCALAR
-        nc.scalar.copy(out=woven(rounded[2][:, cut:, :]), in_=planar(raw[2][:, :, cut:]))
-        quantise_first_tier(0)
-        quantise_first_tier(1)
-        bring_back(0)
-        for t in range(PACK):
-            nc.scalar.copy(out=back[:, t, :], in_=banks[0][t][:])
-        nc.vector.tensor_copy(out=woven(rounded[2][:, 0:cut, :]), in_=planar(raw[2][:, :, 0:cut]))
-        nc.vector.tensor_copy(out=w_codes[:].rearrange("p t m -> p m t"), in_=w_in[:].rearrange("p (m t) -> p m t", t=PACK))
-        quantise_first_tier(2)
-        nc.vector.tensor_copy(out=woven(rounded[3]), in_=planar(raw[3][:]))
-        nc.vector.tensor_copy(out=w_plane[:], in_=ws_in[:].rearrange("p (m t) -> p t m", t=PACK))
-        quantise_first_tier(3)
-        bring_back(1)
+        def subtract(left, b, bank):
+            nc.vector.tensor_tensor(woven(left, 2), planar(raw_block(b), 2), planar(bank[:].rearrange("p (t j) -> p t j", t=PACK), 2), SUB)
 
-        for s in reversed(range(per_half)):
-            for t in range(PACK):
-                nc.scalar.mul(minus[s][:, t, :], banks[1][t][:, s * PIECE:(s + 1) * PIECE], -1.0)
+        def product_pass(out, t, codes, scales, fmt, opens):
+            nc.tensor.matmul_mx(out=out, lhsT=w_codes[:, t, :].bitcast(E4M3), lhsT_scale=w_plane[:, t, :],
+                                rhs=codes.bitcast(fmt), rhs_scale=scales, start=opens, stop=not opens)
 
-        def product(h, t, codes, scales, fmt, opens):
-            nc.tensor.matmul_mx(out=banks[h][t][:], lhsT=w_codes[:, t, :].bitcast(E4M3), lhsT_scale=w_plane[:, t, :],
-                                rhs=codes[h][:].bitcast(fmt), rhs_scale=scales[h][:], start=opens, stop=not opens)
+        def product(out, t, q, r):
+            product_pass(out, t, q[0], q[1], E5M2, True)
+            product_pass(out, t, r[0], r[1], E4M3, False)
 
-        def first_tier_pass(h, t):
-            product(h, t, q_codes, q_scales, E5M2, True)
+        def scatter(t, lo, hi, dx):
+            h = lo // HALF
+            nc.vector.tensor_tensor(pages[t][:].indirect(offsets[:, lo // GROUP:hi // GROUP]), dx, gain[h][:, lo - h * HALF:hi - h * HALF], MULT)
 
-        def second_tier_pass(h, t):
-            product(h, t, r_codes, r_scales, E4M3, False)
+        def clear(t, freed):
+            pages[t] = sbuf("page%d" % t, [P, T], F32, tag=freed)
+            nc.gpsimd.memset(pages[t][:], 0.0)
 
-        starts = [sum(FIRST_PARTS[:i]) for i in range(len(FIRST_PARTS))]
-        spill = sbuf("spill", [P, J + 2 * PIECE], F32)
-        turned = [spill[:, J + PIECE:], spill[:, P // 2:P // 2 + PIECE]]
-        dx_first = [sbuf("dx0_0", [P, FIRST_PARTS[0]], F32)[:], spill[:, 0:FIRST_PARTS[1]], sbuf("dx0_2", [P, FIRST_PARTS[2]], F32)[:]]
+        def operand(name, width, tag=None):
+            return sbuf(name + "_codes", [P, width], U32, tag=tag)[:], sbuf(name + "_scales", [P, width], U8)[:]
 
-        def empty_first(i):
-            h, at = divmod(starts[i], HALF)
-            nc.scalar.copy(out=dx_first[i], in_=banks[h][0][:, at:at + FIRST_PARTS[i]])
+        def cols(pair, lo, hi):
+            return pair[0][:, lo:hi], pair[1][:, lo:hi]
 
-        def scatter_first(i):
-            lo, hi = starts[i], starts[i] + FIRST_PARTS[i]
-            nc.vector.tensor_tensor(first_page[:].indirect(offsets[:, lo // GROUP:hi // GROUP]), dx_first[i], gain[:, lo:hi], MULT)
+        rounded0 = sbuf("rounded0", [P, PIECE, PACK], BF16, tag="slot0")
+        q0 = operand("q0", PIECE)
+        for s in range(2):
+            nc.vector.tensor_copy(out=woven(rounded0[:, s * BLOCK:(s + 1) * BLOCK, :]), in_=planar(raw_block(s)))
+        for s in range(2):
+            quantise(*cols(q0, s * BLOCK, (s + 1) * BLOCK), rounded0[:, s * BLOCK:(s + 1) * BLOCK, :], E5M2)
+        for s in range(2):
+            bring_back(banks[s], *cols(q0, s * BLOCK, (s + 1) * BLOCK))
+        for c in (1, 2):
+            nc.scalar.copy(out=woven(stage[:, (c - 1) * PIECE:c * PIECE, :]), in_=planar(raw[c][:]))
+        w_sorted = sbuf("w_sorted", [P, N * PACK + N], U8, tag="slot0")
+        w_codes = w_sorted[:, 0:N * PACK].bitcast(I32).rearrange("p (t m) -> p t m", t=PACK)
+        w_plane = w_sorted[:, N * PACK:].rearrange("p (t m) -> p t m", t=PACK)
+        nc.vector.tensor_copy(out=w_codes.rearrange("p t m -> p m t"), in_=w_in[:].rearrange("p (m t) -> p m t", t=PACK))
+        nc.vector.tensor_copy(out=w_plane, in_=ws_in[:].rearrange("p (m t) -> p t m", t=PACK))
+        product_pass(banks[4][:, 0:PIECE], 0, q0[0], q0[1], E5M2, True)
+        left0 = sbuf("left0", [P, PIECE, PACK], BF16)
+        for s in range(2):
+            subtract(left0[:, s * BLOCK:(s + 1) * BLOCK, :], s, banks[s])
+        q1 = operand("q1", PIECE, tag="raw0")
+        quantise(*q1, stage[:, 0:PIECE, :], E5M2)
+        r0 = operand("r0", PIECE)
+        quantise(*r0, left0[:], E4M3)
+        bring_back(banks[2], *cols(q1, 0, BLOCK))
+        product_pass(banks[4][:, 0:PIECE], 0, r0[0], r0[1], E4M3, False)
+        dx00 = sbuf("dx00", [P, PIECE], F32)
+        nc.scalar.copy(out=dx00[:], in_=banks[4][:, 0:PIECE])
+        bring_back(banks[3], *cols(q1, BLOCK, PIECE))
+        product(banks[5][:, 0:PIECE], 1, q0, r0)
+        for t in (2, 3):
+            product(banks[6][:, (t - 2) * PIECE:(t - 1) * PIECE], t, q0, r0)
 
-        blocks = PIECE // P
-        sums = banks[0][PACK - blocks:]
-        first_tier_pass(0, 0)
-        for b in range(blocks):
-            for t in range(PACK):
-                nc.tensor.matmul(sums[b][:, t * P:(t + 1) * P], lhsT=raw[pieces - 1][:, t, b * P:(b + 1) * P], rhs=eye[:],
-                                 is_transpose=True, start=(t == 0), stop=False)
+        left1 = sbuf("left1", [P, PIECE, PACK], BF16)
+        subtract(left1[:, 0:BLOCK, :], 2, banks[2])
+        clear(1, "left0")
+        scatter(0, 0, PIECE, dx00[:])
+        rounded3 = sbuf("rounded3", [P, PIECE, PACK], BF16, tag="q0_codes")
+        nc.scalar.copy(out=woven(rounded3[:]), in_=planar(raw[3][:]))
+        dx10 = sbuf("dx10", [P, PIECE], F32, tag="r0_codes")
+        nc.scalar.copy(out=dx10[:], in_=banks[5][:, 0:PIECE])
+        spill = sbuf("spill", [P, J], F32)
+        nc.scalar.copy(out=spill[:].rearrange("p (t c j) -> p t c j", t=2, c=2)[:, :, 0, :], in_=banks[6][:].rearrange("p (t j) -> p t j", t=2))
+        subtract(left1[:, BLOCK:, :], 3, banks[3])
+        q23 = operand("q23", HALF, tag="raw1")
+        quantise(*cols(q23, 0, PIECE), stage[:, PIECE:, :], E5M2)
+        r1 = operand("r1", PIECE)
+        quantise(*r1, left1[:], E4M3)
+        quantise(*cols(q23, PIECE, HALF), rounded3[:], E5M2)
+        scatter(1, 0, PIECE, dx10[:])
+        clear(2, "r0_codes")
 
-        for c in range(per_half):
-            nc.vector.tensor_tensor(woven(left[c][:], 2), planar(raw[c][:], 2), planar(back[:, :, c * PIECE:(c + 1) * PIECE], 2), SUB)
-        for c in range(per_half):
-            cols = slice(c * PIECE, (c + 1) * PIECE)
-            nc.vector.quantize_mx(out=r_codes[0][:, cols].bitcast(E4M3), scales=r_scales[0][:, cols], in_=flat(left[c][:]))
-        second_tier_pass(0, 0)
-        empty_first(0)
-
-        late = sbuf("late", [P, HALF, PACK], BF16, tag="left0")
-        nc.vector.tensor_tensor(woven(late[:, 0:PIECE, :], 2), planar(raw[per_half][:], 2), planar(minus[0][:], 2), ADD)
-        scatter_first(0)
-
+        back_banks = {4: banks[0], 5: banks[1], 6: banks[7], 7: banks[1]}
+        sum_banks = {4: banks[2], 5: banks[3], 6: banks[6], 7: banks[0]}
+        late = sbuf("late", [P, HALF, PACK], BF16)
         late_words = flat(late[:]).bitcast(F32)
-        for t in range(PACK):
-            for b in range(blocks):
-                nc.tensor.matmul(sums[b][:, t * P:(t + 1) * P], lhsT=minus[1][:, t, b * P:(b + 1) * P], rhs=eye[:],
-                                 is_transpose=True, start=False, stop=(t == PACK - 1))
-        first_tier_pass(1, 0)
-        for b in range(blocks):
-            nc.scalar.copy(out=turned[b].bitcast(BF16).rearrange("p (u m e) -> p u m e", u=2, e=2),
-                           in_=sums[b][:].rearrange("p (u e m) -> p u m e", u=2, e=2))
-        for b in range(blocks):
-            for u in range(2):
-                nc.tensor.transpose(sums[b][:, u * P:(u + 1) * P], turned[b][:, u * P:(u + 1) * P], eye[:])
-        for b in range(blocks):
-            at = 2 * (PIECE + b * P)
-            nc.scalar.copy(out=late_words[:, at:at + 2 * P].rearrange("p (j u) -> p j u", u=2),
-                           in_=sums[b][:, 0:2 * P].rearrange("p (u j) -> p j u", u=2))
-        nc.vector.quantize_mx(out=r_codes[1][:].bitcast(E4M3), scales=r_scales[1][:], in_=flat(late[:]))
-        empty_first(1)
-        second_tier_pass(1, 0)
-        empty_first(2)
-        scatter_first(1)
-        scatter_first(2)
+        minus = {}
+        turned = {}
 
-        for t in range(1, PACK):
-            for h in range(halves):
-                first_tier_pass(h, t)
-                second_tier_pass(h, t)
-        dx = {1: spill[:, PIECE:PIECE + J], 2: sbuf("dx2", [P, J], F32)[:], 3: sbuf("dx3", [P, J], F32)[:]}
-        for t in range(1, PACK):
-            for h in range(halves):
-                nc.scalar.copy(out=dx[t][:, h * HALF:(h + 1) * HALF], in_=banks[h][t][:])
+        def back(b):
+            bring_back(back_banks[b], *cols(q23, (b - 4) * BLOCK, (b - 3) * BLOCK))
+
+        def turn(b, values, first):
+            for t in range(PACK):
+                nc.tensor.matmul(sum_banks[b][:, t * P:(t + 1) * P], lhsT=values[:, t, :], rhs=eye[:], is_transpose=True,
+                                 start=(first and t == 0), stop=(not first and t == PACK - 1))
+
+        def negate(b):
+            minus[b] = sbuf("minus%d" % b, [P, PACK, BLOCK], F32)
+            nc.scalar.mul(flat(minus[b][:]), back_banks[b][:], -1.0)
+
+        def round_sums(b):
+            turned[b] = spill[:, J - PIECE:] if b == 7 else sbuf("turned%d" % b, [P, 2 * P], F32)[:]
+            nc.scalar.copy(out=turned[b].bitcast(BF16).rearrange("p (u m e) -> p u m e", u=2, e=2),
+                           in_=sum_banks[b][:].rearrange("p (u e m) -> p u m e", u=2, e=2))
+
+        def turn_back(b):
+            for u in range(2):
+                nc.tensor.transpose(sum_banks[b][:, u * P:(u + 1) * P], turned[b][:, u * P:(u + 1) * P], eye[:])
+
+        def lay_words(b):
+            at = 2 * (b - 4) * BLOCK
+            nc.scalar.copy(out=late_words[:, at:at + 2 * P].rearrange("p (j u) -> p j u", u=2),
+                           in_=sum_banks[b][:, 0:2 * P].rearrange("p (u j) -> p j u", u=2))
+
+        back(4)
+        back(5)
+        for t in (0, 1):
+            product(banks[4][:, t * PIECE:(t + 1) * PIECE], t, q1, r1)
+        dx1 = sbuf("dx1", [P, 2, PIECE], F32)
+        nc.scalar.copy(out=flat(dx1[:]), in_=banks[4][:])
+        scatter(0, PIECE, HALF, dx1[:, 0, :])
+        scatter(1, PIECE, HALF, dx1[:, 1, :])
+        clear(3, "dx1")
+        for b in (4, 5):
+            turn(b, raw_block(b), True)
+        for b in (4, 5):
+            negate(b)
+            turn(b, minus[b], False)
+        back(6)
+        back(7)
+        for t in (2, 3):
+            product(banks[5][:, (t - 2) * PIECE:(t - 1) * PIECE], t, q1, r1)
+        nc.scalar.copy(out=spill[:, PIECE:HALF], in_=banks[5][:, 0:PIECE])
+        scatter(2, 0, HALF, spill[:, 0:HALF])
+        scatter(3, 0, PIECE, spill[:, HALF:HALF + PIECE])
+        for b in (6, 7):
+            turn(b, raw_block(b), True)
+        for b in (4, 5):
+            round_sums(b)
+            turn_back(b)
+        for b in (6, 7):
+            negate(b)
+            turn(b, minus[b], False)
+        for b in (4, 5):
+            lay_words(b)
+        for b in (6, 7):
+            round_sums(b)
+            turn_back(b)
+        for b in (6, 7):
+            lay_words(b)
+        r23 = operand("r23", HALF)
+        quantise(*r23, late[:], E4M3)
+        nc.scalar.copy(out=spill[:, J - PIECE:], in_=banks[5][:, PIECE:])
+        scatter(3, PIECE, HALF, spill[:, J - PIECE:])
+
+        last_banks = [banks[4], banks[7], banks[2], banks[3]]
+        dx23 = []
+        for t in range(PACK):
+            product(last_banks[t][:], t, q23, r23)
+        for t in range(PACK):
+            dx23.append(sbuf("dx23_%d" % t, [P, HALF], F32))
+            nc.scalar.copy(out=dx23[t][:], in_=last_banks[t][:])
 
         out_planes = out_0.rearrange("(p t) c -> p t c", t=PACK)
-        grouped = sbuf("grouped", [P, T, PACK], BF16, tag="r_codes1")
-        pages = [first_page]
-        for t, freed in ((1, "left0"), (2, "even"), (3, "dx0_2")):
-            page = sbuf("page%d" % t, [P, T], F32, tag=freed)
-            nc.gpsimd.memset(page[:], 0.0)
-            pages.append(page)
+        shares = ((0, LAST_ON_VECTOR), (LAST_ON_VECTOR, T))
+        pairs = [sbuf("pairs%d" % i, [P, PACK * (hi - lo)], BF16, tag=tag) for (i, (lo, hi)), tag in zip(enumerate(shares), ("r23_codes", "late"))]
+
+        def pair_view(i):
+            return pairs[i][:].rearrange("p (u c e) -> p u c e", u=2, e=2)
+
         for t in range(PACK):
-            if t > 0:
-                nc.vector.tensor_tensor(pages[t][:].indirect(offsets[:]), dx[t], gain[:], MULT)
+            scatter(t, HALF, J, dx23[t][:])
             nc.sync.dma_start(out=out_planes[:, t, :], in_=pages[t][:])
-            if t < PACK - 2:
-                nc.scalar.copy(out=grouped[:, :, t], in_=pages[t][:])
-            elif t == PACK - 2:
-                nc.scalar.copy(out=grouped[:, :LAST_ON_VECTOR, t:],
-                               in_=pages[t][:, :LAST_ON_VECTOR].unsqueeze(2).to_broadcast([P, LAST_ON_VECTOR, 2]))
-                nc.scalar.copy(out=grouped[:, LAST_ON_VECTOR:, t], in_=pages[t][:, LAST_ON_VECTOR:])
-            else:
-                for lo in range(0, LAST_ON_VECTOR, CHUNK):
-                    nc.vector.tensor_copy(out=grouped[:, lo:lo + CHUNK, t], in_=pages[t][:, lo:lo + CHUNK])
-                for lo in range(LAST_ON_VECTOR, T, CHUNK):
-                    nc.scalar.copy(out=grouped[:, lo:lo + CHUNK, t], in_=pages[t][:, lo:lo + CHUNK])
+            u, e = divmod(t, 2)
+            for i, (lo, hi) in enumerate(shares):
+                if t == PACK - 1 and i == 0:
+                    nc.vector.tensor_copy(out=pair_view(i)[:, u, :, e], in_=pages[t][:, lo:hi])
+                elif t == PACK - 2 and i == 0:
+                    nc.scalar.copy(out=pair_view(i)[:, u, 0:hi - SEAM, e], in_=pages[t][:, 0:hi - SEAM])
+                    nc.scalar.copy(out=pair_view(i)[:, u, hi - SEAM:hi, :], in_=pages[t][:, hi - SEAM:hi].unsqueeze(2).to_broadcast([P, SEAM, 2]))
+                else:
+                    nc.scalar.copy(out=pair_view(i)[:, u, :, e], in_=pages[t][:, lo:hi])
 
         words_out = out_1[0].rearrange("p c i -> p (c i)").bitcast(I32)
         y_scales = sbuf("y_scales", [P, T // 2], U8)
+        grouped = []
         for c in range(T // CHUNK):
-            cols = slice(c * CHUNK, (c + 1) * CHUNK)
+            i = 0 if c * CHUNK < LAST_ON_VECTOR else 1
+            at = c * CHUNK - shares[i][0]
+            grouped.append(sbuf("grouped%d" % c, [P, CHUNK * PACK], BF16))
+            word = (I32, U32)[i]
+            src = pairs[i][:].bitcast(word).rearrange("p (u c) -> p u c", u=2)[:, :, at:at + CHUNK].rearrange("p u (c i) -> p c u i", i=PACK)
+            dst = grouped[c][:].bitcast(word).rearrange("p (c i u) -> p c u i", i=PACK, u=2)
+            if i == 0:
+                nc.vector.tensor_copy(out=dst, in_=src)
+            else:
+                nc.scalar.copy(out=dst, in_=src)
+        for c in range(T // CHUNK):
+            columns = slice(c * CHUNK, (c + 1) * CHUNK)
             shift, side = divmod(c, 2)
             y_codes = sbuf("y_codes%d" % c, [P, CHUNK], U32)
             nc.vector.quantize_mx(out=y_codes[:].bitcast(E4M3), scales=y_scales[4 * shift:, side * CHUNK:(side + 1) * CHUNK],
-                                  in_=flat(grouped[:, cols, :]))
-            nc.sync.dma_start(out=words_out[:, cols], in_=y_codes[:].bitcast(I32))
+                                  in_=grouped[c][:])
+            nc.sync.dma_start(out=words_out[:, columns], in_=y_codes[:].bitcast(I32))
         for q in range(QUADS):
             nc.scalar.dma_start(out=out_2[0, 4 * q:4 * q + 4, :].bitcast(I32).rearrange("r (u x) -> u r x", u=2),
                                 in_=y_scales[32 * q:32 * q + 8, :].bitcast(I32))

@@ -28,6 +28,7 @@ PAD = 64
 BLOCK = 128
 LAST_ON_VECTOR = 1024
 SEAM = 16
+CLEARED_BY_VECTOR = 512
 
 
 def woven(tile3, run=PACK):
@@ -54,19 +55,25 @@ def tile_list_embg_tgq8_noneP_kernel(tc, dy, w_words, w_scales, wgo, offs, out_0
             return sb.tile(shape, dtype, name=name, tag=tag or name, align_bytes=64)
 
         dy_planes = dy.rearrange("(p t) j -> p t j", t=PACK)
-        raw = [sbuf("raw%d" % c, [P, PACK, PIECE], F32) for c in range(pieces)]
+        ws_in = sbuf("ws_in", [P, N], U8)
+        for q in range(QUADS):
+            nc.sync.dma_start(out=ws_in[32 * q:32 * (q + 1), :].bitcast(I32),
+                              in_=w_scales[0, 4 * q:4 * q + 4, :].bitcast(I32).unsqueeze(0).to_broadcast([8, 4, N // 4]))
+        first = [sbuf("first%d" % s, [P, PACK, BLOCK], F32) for s in range(4)]
+
+        def load_block(b):
+            nc.sync.dma_start(out=first[b][:], in_=dy_planes[:, :, b * BLOCK:(b + 1) * BLOCK])
+
+        for b in range(3):
+            load_block(b)
+        raw = {c: sbuf("raw%d" % c, [P, PACK, PIECE], F32) for c in range(2, pieces)}
 
         def load_piece(c):
             nc.sync.dma_start(out=raw[c][:], in_=dy_planes[:, :, c * PIECE:(c + 1) * PIECE])
 
-        ws_in = sbuf("ws_in", [P, N], U8)
-        nc.gpsimd.memset(ws_in[:].bitcast(I32), 0)
-        load_piece(0)
         w_in = sbuf("w_in", [P, N], I32)
         nc.sync.dma_start(out=w_in[:], in_=w_words[0].rearrange("p n i -> p (n i)").bitcast(I32))
-        for q in range(QUADS):
-            nc.sync.dma_start(out=ws_in[32 * q:32 * q + 4, :].bitcast(I32), in_=w_scales[0, 4 * q:4 * q + 4, :].bitcast(I32))
-        load_piece(1)
+        load_block(3)
         load_piece(2)
         offsets = sb.tile([P, J // GROUP], U16, name="offsets")
         nc.sync.dma_start(offsets[:], offs)
@@ -75,30 +82,34 @@ def tile_list_embg_tgq8_noneP_kernel(tc, dy, w_words, w_scales, wgo, offs, out_0
         load_piece(3)
         nc.sync.dma_start(out=gain[1][:], in_=wgo[:, HALF:])
 
-        stage = sbuf("stage", [P, 2 * PIECE, PACK], BF16)
-        ones = sbuf("ones", [P, P], F32, tag="page0")
+        ones = sbuf("ones", [P, P], BF16, tag="page0")
         nc.gpsimd.memset(ones[:], 1.0)
+        small_eye = sbuf("small_eye", [P, P], BF16)
+        nc.gpsimd.affine_select(out=small_eye[:], in_=ones[:], pattern=[[-1, P]], compare_op=mybir.AluOpType.is_equal, fill=0.0, base=0, channel_multiplier=1)
         eye = sbuf("eye", [P, P], F32)
-        nc.gpsimd.affine_select(out=eye[:], in_=ones[:], pattern=[[-1, P]], compare_op=mybir.AluOpType.is_equal, fill=0.0, base=0, channel_multiplier=1)
-        eye_in = stage[:, PIECE - P // 2:PIECE + P // 2, :]
-        nc.scalar.copy(out=eye_in, in_=eye[:].unsqueeze(2).to_broadcast([P, P, PACK]))
+        nc.scalar.copy(out=eye[:], in_=small_eye[:])
         row = P * PACK
         eye_codes = sbuf("eye_codes", [P, PACK * row + PAD], U8)
         nc.vector.memset(eye_codes[:].bitcast(I32), 0)
-        eye_base = sbuf("eye_base", [P, P, PACK], U8, tag="slot0")
-        eye_scales = sbuf("eye_scales", [P, P], U8)
-        nc.vector.quantize_mx(out=flat(eye_base[:]).bitcast(E4M3), scales=eye_scales[:], in_=flat(eye_in))
-        diagonal = eye_codes[:, 0:PACK * (row + 1)].rearrange("p (t x) -> p t x", t=PACK)[:, :, 0:row:PACK]
-        nc.vector.tensor_copy(out=diagonal, in_=eye_base[:].rearrange("p m t -> p t m"))
-
+        eye_in = sbuf("eye_in", [P, P, PACK], BF16)
+        nc.vector.tensor_copy(out=eye_in[:], in_=small_eye[:].unsqueeze(2).to_broadcast([P, P, PACK]))
         pages = {0: sbuf("page0", [P, T], F32)}
-        nc.vector.memset(pages[0][:, 0:T // 2].bitcast(I32), 0)
-        nc.gpsimd.memset(pages[0][:, T // 2:], 0.0)
+        nc.vector.memset(pages[0][:, 0:CLEARED_BY_VECTOR].bitcast(I32), 0)
+        nc.gpsimd.memset(pages[0][:, CLEARED_BY_VECTOR:], 0.0)
+        eye_base = sbuf("eye_base", [P, P, PACK], U8)
+        eye_scales = sbuf("eye_scales", [P, P], U8)
+        nc.vector.quantize_mx(out=flat(eye_base[:]).bitcast(E4M3), scales=eye_scales[:], in_=flat(eye_in[:]))
+        diagonal = eye_codes[:, 0:PACK * (row + 1)].rearrange("p (t x) -> p t x", t=PACK)[:, :, 0:row:PACK]
+        w_plane = sbuf("w_plane", [P, PACK, P], U8, tag="eye_in")
+        nc.vector.tensor_copy(out=diagonal, in_=eye_base[:].rearrange("p m t -> p t m"))
+        nc.vector.tensor_copy(out=w_plane[:], in_=ws_in[:].rearrange("p (m t) -> p t m", t=PACK))
 
         banks = [psum.tile([P, HALF], F32, name="bank%d" % b) for b in range(8)]
 
         def raw_block(b):
             c, s = divmod(b, 2)
+            if b < 4:
+                return first[b][:]
             return raw[c][:, :, s * BLOCK:(s + 1) * BLOCK]
 
         def quantise(codes, scales, values, fmt):
@@ -134,29 +145,30 @@ def tile_list_embg_tgq8_noneP_kernel(tc, dy, w_words, w_scales, wgo, offs, out_0
         def cols(pair, lo, hi):
             return pair[0][:, lo:hi], pair[1][:, lo:hi]
 
-        rounded0 = sbuf("rounded0", [P, PIECE, PACK], BF16, tag="slot0")
+        early = sbuf("early", [P, 2 * BLOCK, PACK], BF16, tag="eye_base")
+        rounded = {0: sbuf("rounded0", [P, BLOCK, PACK], BF16, tag="ws_in")[:], 1: early[:, 0:BLOCK, :], 2: early[:, BLOCK:, :]}
         q0 = operand("q0", PIECE)
+        nc.vector.tensor_copy(out=woven(rounded[0]), in_=planar(raw_block(0)))
+        for b in (1, 2):
+            nc.scalar.copy(out=woven(rounded[b]), in_=planar(raw_block(b)))
         for s in range(2):
-            nc.vector.tensor_copy(out=woven(rounded0[:, s * BLOCK:(s + 1) * BLOCK, :]), in_=planar(raw_block(s)))
-        for s in range(2):
-            quantise(*cols(q0, s * BLOCK, (s + 1) * BLOCK), rounded0[:, s * BLOCK:(s + 1) * BLOCK, :], E5M2)
+            quantise(*cols(q0, s * BLOCK, (s + 1) * BLOCK), rounded[s], E5M2)
         for s in range(2):
             bring_back(banks[s], *cols(q0, s * BLOCK, (s + 1) * BLOCK))
-        for c in (1, 2):
-            nc.scalar.copy(out=woven(stage[:, (c - 1) * PIECE:c * PIECE, :]), in_=planar(raw[c][:]))
-        w_sorted = sbuf("w_sorted", [P, N * PACK + N], U8, tag="slot0")
-        w_codes = w_sorted[:, 0:N * PACK].bitcast(I32).rearrange("p (t m) -> p t m", t=PACK)
-        w_plane = w_sorted[:, N * PACK:].rearrange("p (t m) -> p t m", t=PACK)
-        nc.vector.tensor_copy(out=w_codes.rearrange("p t m -> p m t"), in_=w_in[:].rearrange("p (m t) -> p m t", t=PACK))
-        nc.vector.tensor_copy(out=w_plane, in_=ws_in[:].rearrange("p (m t) -> p t m", t=PACK))
+        w_codes = sbuf("w_codes", [P, PACK, P], U32, tag="ws_in")
+        nc.scalar.copy(out=w_codes[:].rearrange("p t m -> p m t"), in_=w_in[:].bitcast(U32).rearrange("p (m t) -> p m t", t=PACK))
+        stage = sbuf("stage", [P, BLOCK + PIECE, PACK], BF16, tag="w_in")
+        nc.scalar.copy(out=woven(stage[:, 0:BLOCK, :]), in_=planar(raw_block(3)))
+        nc.scalar.copy(out=woven(stage[:, BLOCK:, :]), in_=planar(raw[2][:]))
         product_pass(banks[4][:, 0:PIECE], 0, q0[0], q0[1], E5M2, True)
         left0 = sbuf("left0", [P, PIECE, PACK], BF16)
         for s in range(2):
             subtract(left0[:, s * BLOCK:(s + 1) * BLOCK, :], s, banks[s])
-        q1 = operand("q1", PIECE, tag="raw0")
-        quantise(*q1, stage[:, 0:PIECE, :], E5M2)
+        q1 = operand("q1", PIECE, tag="first0")
+        quantise(*cols(q1, 0, BLOCK), rounded[2], E5M2)
         r0 = operand("r0", PIECE)
         quantise(*r0, left0[:], E4M3)
+        quantise(*cols(q1, BLOCK, PIECE), stage[:, 0:BLOCK, :], E5M2)
         bring_back(banks[2], *cols(q1, 0, BLOCK))
         product_pass(banks[4][:, 0:PIECE], 0, r0[0], r0[1], E4M3, False)
         dx00 = sbuf("dx00", [P, PIECE], F32)
@@ -168,25 +180,25 @@ def tile_list_embg_tgq8_noneP_kernel(tc, dy, w_words, w_scales, wgo, offs, out_0
 
         left1 = sbuf("left1", [P, PIECE, PACK], BF16)
         subtract(left1[:, 0:BLOCK, :], 2, banks[2])
-        clear(1, "left0")
+        q23 = operand("q23", HALF, tag="first2")
+        quantise(*cols(q23, 0, PIECE), stage[:, BLOCK:, :], E5M2)
+        clear(1, "w_in")
         scatter(0, 0, PIECE, dx00[:])
         rounded3 = sbuf("rounded3", [P, PIECE, PACK], BF16, tag="q0_codes")
         nc.scalar.copy(out=woven(rounded3[:]), in_=planar(raw[3][:]))
-        dx10 = sbuf("dx10", [P, PIECE], F32, tag="r0_codes")
-        nc.scalar.copy(out=dx10[:], in_=banks[5][:, 0:PIECE])
         spill = sbuf("spill", [P, J], F32)
         nc.scalar.copy(out=spill[:].rearrange("p (t c j) -> p t c j", t=2, c=2)[:, :, 0, :], in_=banks[6][:].rearrange("p (t j) -> p t j", t=2))
         subtract(left1[:, BLOCK:, :], 3, banks[3])
-        q23 = operand("q23", HALF, tag="raw1")
-        quantise(*cols(q23, 0, PIECE), stage[:, PIECE:, :], E5M2)
+        dx10 = sbuf("dx10", [P, PIECE], F32, tag="first3")
+        nc.scalar.copy(out=dx10[:], in_=banks[5][:, 0:PIECE])
         r1 = operand("r1", PIECE)
         quantise(*r1, left1[:], E4M3)
         quantise(*cols(q23, PIECE, HALF), rounded3[:], E5M2)
         scatter(1, 0, PIECE, dx10[:])
-        clear(2, "r0_codes")
+        clear(2, "q0_codes")
 
-        back_banks = {4: banks[0], 5: banks[1], 6: banks[7], 7: banks[1]}
-        sum_banks = {4: banks[2], 5: banks[3], 6: banks[6], 7: banks[0]}
+        back_banks = {4: banks[0], 5: banks[1], 6: banks[7], 7: banks[5]}
+        sum_banks = {4: banks[4], 5: banks[6], 6: banks[2], 7: banks[3]}
         late = sbuf("late", [P, HALF, PACK], BF16)
         late_words = flat(late[:]).bitcast(F32)
         minus = {}
@@ -220,23 +232,23 @@ def tile_list_embg_tgq8_noneP_kernel(tc, dy, w_words, w_scales, wgo, offs, out_0
 
         back(4)
         back(5)
-        for t in (0, 1):
-            product(banks[4][:, t * PIECE:(t + 1) * PIECE], t, q1, r1)
-        dx1 = sbuf("dx1", [P, 2, PIECE], F32)
-        nc.scalar.copy(out=flat(dx1[:]), in_=banks[4][:])
-        scatter(0, PIECE, HALF, dx1[:, 0, :])
-        scatter(1, PIECE, HALF, dx1[:, 1, :])
-        clear(3, "dx1")
         for b in (4, 5):
             turn(b, raw_block(b), True)
         for b in (4, 5):
             negate(b)
+        for t in (0, 1):
+            product(banks[t][:, 0:PIECE], t, q1, r1)
+            dx1 = sbuf("dx1_%d" % t, [P, PIECE], F32)
+            nc.scalar.copy(out=dx1[:], in_=banks[t][:, 0:PIECE])
+            scatter(t, PIECE, HALF, dx1[:])
+        clear(3, "dx1_0")
+        for b in (4, 5):
             turn(b, minus[b], False)
         back(6)
         back(7)
         for t in (2, 3):
-            product(banks[5][:, (t - 2) * PIECE:(t - 1) * PIECE], t, q1, r1)
-        nc.scalar.copy(out=spill[:, PIECE:HALF], in_=banks[5][:, 0:PIECE])
+            product(banks[0][:, (t - 2) * PIECE:(t - 1) * PIECE], t, q1, r1)
+        nc.scalar.copy(out=spill[:, PIECE:HALF], in_=banks[0][:, 0:PIECE])
         scatter(2, 0, HALF, spill[:, 0:HALF])
         scatter(3, 0, PIECE, spill[:, HALF:HALF + PIECE])
         for b in (6, 7):
@@ -256,10 +268,10 @@ def tile_list_embg_tgq8_noneP_kernel(tc, dy, w_words, w_scales, wgo, offs, out_0
             lay_words(b)
         r23 = operand("r23", HALF)
         quantise(*r23, late[:], E4M3)
-        nc.scalar.copy(out=spill[:, J - PIECE:], in_=banks[5][:, PIECE:])
+        nc.scalar.copy(out=spill[:, J - PIECE:], in_=banks[0][:, PIECE:])
         scatter(3, PIECE, HALF, spill[:, J - PIECE:])
 
-        last_banks = [banks[4], banks[7], banks[2], banks[3]]
+        last_banks = [banks[1], banks[7], banks[6], banks[4]]
         dx23 = []
         for t in range(PACK):
             product(last_banks[t][:], t, q23, r23)

@@ -28,7 +28,7 @@ PAD = 64
 BLOCK = 128
 LAST_ON_VECTOR = 1024
 SEAM = 16
-CLEARED_BY_VECTOR = 512
+CLEARED_BY_VECTOR = 768
 
 
 def woven(tile3, run=PACK):
@@ -45,7 +45,6 @@ def flat(tile3):
 
 def tile_list_embg_tgq8_noneP_kernel(tc, dy, w_words, w_scales, wgo, offs, out_0, out_1, out_2):
     nc = tc.nc
-    pieces = J // PIECE
 
     with ExitStack() as ctx:
         sb = ctx.enter_context(tc.tile_pool(name="sb", bufs=1))
@@ -55,44 +54,38 @@ def tile_list_embg_tgq8_noneP_kernel(tc, dy, w_words, w_scales, wgo, offs, out_0
             return sb.tile(shape, dtype, name=name, tag=tag or name, align_bytes=64)
 
         dy_planes = dy.rearrange("(p t) j -> p t j", t=PACK)
-        ws_in = sbuf("ws_in", [P, N], U8)
-        for q in range(QUADS):
-            nc.sync.dma_start(out=ws_in[32 * q:32 * (q + 1), :].bitcast(I32),
-                              in_=w_scales[0, 4 * q:4 * q + 4, :].bitcast(I32).unsqueeze(0).to_broadcast([8, 4, N // 4]))
         first = [sbuf("first%d" % s, [P, PACK, BLOCK], F32) for s in range(4)]
 
         def load_block(b):
             nc.sync.dma_start(out=first[b][:], in_=dy_planes[:, :, b * BLOCK:(b + 1) * BLOCK])
 
-        for b in range(3):
-            load_block(b)
-        raw = {c: sbuf("raw%d" % c, [P, PACK, PIECE], F32) for c in range(2, pieces)}
-
-        def load_piece(c):
-            nc.sync.dma_start(out=raw[c][:], in_=dy_planes[:, :, c * PIECE:(c + 1) * PIECE])
-
+        load_block(0)
+        load_block(1)
+        ws_in = sbuf("ws_in", [P, N], U8)
+        for q in range(QUADS):
+            nc.sync.dma_start(out=ws_in[32 * q:32 * (q + 1), :].bitcast(I32),
+                              in_=w_scales[0, 4 * q:4 * q + 4, :].bitcast(I32).unsqueeze(0).to_broadcast([8, 4, N // 4]))
+        load_block(2)
         w_in = sbuf("w_in", [P, N], I32)
         nc.sync.dma_start(out=w_in[:], in_=w_words[0].rearrange("p n i -> p (n i)").bitcast(I32))
         load_block(3)
-        load_piece(2)
         offsets = sb.tile([P, J // GROUP], U16, name="offsets")
         nc.sync.dma_start(offsets[:], offs)
         gain = [sbuf("gain%d" % h, [P, HALF], F32) for h in range(2)]
         nc.sync.dma_start(out=gain[0][:], in_=wgo[:, 0:HALF])
-        load_piece(3)
+        second = sbuf("second", [P, PACK, HALF], F32)
+        nc.sync.dma_start(out=second[:], in_=dy_planes[:, :, HALF:])
         nc.sync.dma_start(out=gain[1][:], in_=wgo[:, HALF:])
 
-        ones = sbuf("ones", [P, P], BF16, tag="page0")
+        ones = sbuf("ones", [P, P], F32, tag="page0")
         nc.gpsimd.memset(ones[:], 1.0)
-        small_eye = sbuf("small_eye", [P, P], BF16)
-        nc.gpsimd.affine_select(out=small_eye[:], in_=ones[:], pattern=[[-1, P]], compare_op=mybir.AluOpType.is_equal, fill=0.0, base=0, channel_multiplier=1)
         eye = sbuf("eye", [P, P], F32)
-        nc.scalar.copy(out=eye[:], in_=small_eye[:])
+        nc.gpsimd.affine_select(out=eye[:], in_=ones[:], pattern=[[-1, P]], compare_op=mybir.AluOpType.is_equal, fill=0.0, base=0, channel_multiplier=1)
+        eye_in = sbuf("eye_in", [P, P, PACK], BF16)
+        nc.scalar.copy(out=eye_in[:], in_=eye[:].unsqueeze(2).to_broadcast([P, P, PACK]))
         row = P * PACK
         eye_codes = sbuf("eye_codes", [P, PACK * row + PAD], U8)
         nc.vector.memset(eye_codes[:].bitcast(I32), 0)
-        eye_in = sbuf("eye_in", [P, P, PACK], BF16)
-        nc.vector.tensor_copy(out=eye_in[:], in_=small_eye[:].unsqueeze(2).to_broadcast([P, P, PACK]))
         pages = {0: sbuf("page0", [P, T], F32)}
         nc.vector.memset(pages[0][:, 0:CLEARED_BY_VECTOR].bitcast(I32), 0)
         nc.gpsimd.memset(pages[0][:, CLEARED_BY_VECTOR:], 0.0)
@@ -100,17 +93,14 @@ def tile_list_embg_tgq8_noneP_kernel(tc, dy, w_words, w_scales, wgo, offs, out_0
         eye_scales = sbuf("eye_scales", [P, P], U8)
         nc.vector.quantize_mx(out=flat(eye_base[:]).bitcast(E4M3), scales=eye_scales[:], in_=flat(eye_in[:]))
         diagonal = eye_codes[:, 0:PACK * (row + 1)].rearrange("p (t x) -> p t x", t=PACK)[:, :, 0:row:PACK]
-        w_plane = sbuf("w_plane", [P, PACK, P], U8, tag="eye_in")
         nc.vector.tensor_copy(out=diagonal, in_=eye_base[:].rearrange("p m t -> p t m"))
-        nc.vector.tensor_copy(out=w_plane[:], in_=ws_in[:].rearrange("p (m t) -> p t m", t=PACK))
 
         banks = [psum.tile([P, HALF], F32, name="bank%d" % b) for b in range(8)]
 
         def raw_block(b):
-            c, s = divmod(b, 2)
             if b < 4:
                 return first[b][:]
-            return raw[c][:, :, s * BLOCK:(s + 1) * BLOCK]
+            return second[:, :, (b - 4) * BLOCK:(b - 3) * BLOCK]
 
         def quantise(codes, scales, values, fmt):
             nc.vector.quantize_mx(out=codes.bitcast(fmt), scales=scales, in_=flat(values))
@@ -145,21 +135,22 @@ def tile_list_embg_tgq8_noneP_kernel(tc, dy, w_words, w_scales, wgo, offs, out_0
         def cols(pair, lo, hi):
             return pair[0][:, lo:hi], pair[1][:, lo:hi]
 
-        early = sbuf("early", [P, 2 * BLOCK, PACK], BF16, tag="eye_base")
-        rounded = {0: sbuf("rounded0", [P, BLOCK, PACK], BF16, tag="ws_in")[:], 1: early[:, 0:BLOCK, :], 2: early[:, BLOCK:, :]}
+        early = sbuf("early", [P, 2 * BLOCK, PACK], BF16, tag="eye_in")
+        rounded = {0: sbuf("rounded0", [P, BLOCK, PACK], BF16, tag="eye_base")[:], 1: early[:, 0:BLOCK, :], 2: early[:, BLOCK:, :]}
         q0 = operand("q0", PIECE)
         nc.vector.tensor_copy(out=woven(rounded[0]), in_=planar(raw_block(0)))
         for b in (1, 2):
             nc.scalar.copy(out=woven(rounded[b]), in_=planar(raw_block(b)))
-        for s in range(2):
-            quantise(*cols(q0, s * BLOCK, (s + 1) * BLOCK), rounded[s], E5M2)
+        quantise(*cols(q0, 0, BLOCK), rounded[0], E5M2)
+        w_plane = sbuf("w_plane", [P, PACK, P], U8, tag="eye_base")
+        nc.vector.tensor_copy(out=w_plane[:], in_=ws_in[:].rearrange("p (m t) -> p t m", t=PACK))
+        quantise(*cols(q0, BLOCK, PIECE), rounded[1], E5M2)
         for s in range(2):
             bring_back(banks[s], *cols(q0, s * BLOCK, (s + 1) * BLOCK))
         w_codes = sbuf("w_codes", [P, PACK, P], U32, tag="ws_in")
         nc.scalar.copy(out=w_codes[:].rearrange("p t m -> p m t"), in_=w_in[:].bitcast(U32).rearrange("p (m t) -> p m t", t=PACK))
-        stage = sbuf("stage", [P, BLOCK + PIECE, PACK], BF16, tag="w_in")
-        nc.scalar.copy(out=woven(stage[:, 0:BLOCK, :]), in_=planar(raw_block(3)))
-        nc.scalar.copy(out=woven(stage[:, BLOCK:, :]), in_=planar(raw[2][:]))
+        stage = sbuf("stage", [P, BLOCK, PACK], BF16, tag="w_in")
+        nc.scalar.copy(out=woven(stage[:]), in_=planar(raw_block(3)))
         product_pass(banks[4][:, 0:PIECE], 0, q0[0], q0[1], E5M2, True)
         left0 = sbuf("left0", [P, PIECE, PACK], BF16)
         for s in range(2):
@@ -168,7 +159,7 @@ def tile_list_embg_tgq8_noneP_kernel(tc, dy, w_words, w_scales, wgo, offs, out_0
         quantise(*cols(q1, 0, BLOCK), rounded[2], E5M2)
         r0 = operand("r0", PIECE)
         quantise(*r0, left0[:], E4M3)
-        quantise(*cols(q1, BLOCK, PIECE), stage[:, 0:BLOCK, :], E5M2)
+        quantise(*cols(q1, BLOCK, PIECE), stage[:], E5M2)
         bring_back(banks[2], *cols(q1, 0, BLOCK))
         product_pass(banks[4][:, 0:PIECE], 0, r0[0], r0[1], E4M3, False)
         dx00 = sbuf("dx00", [P, PIECE], F32)
@@ -179,26 +170,29 @@ def tile_list_embg_tgq8_noneP_kernel(tc, dy, w_words, w_scales, wgo, offs, out_0
             product(banks[6][:, (t - 2) * PIECE:(t - 1) * PIECE], t, q0, r0)
 
         left1 = sbuf("left1", [P, PIECE, PACK], BF16)
-        subtract(left1[:, 0:BLOCK, :], 2, banks[2])
-        q23 = operand("q23", HALF, tag="first2")
-        quantise(*cols(q23, 0, PIECE), stage[:, BLOCK:, :], E5M2)
+        for s in range(2):
+            subtract(left1[:, s * BLOCK:(s + 1) * BLOCK, :], 2 + s, banks[2 + s])
         clear(1, "w_in")
         scatter(0, 0, PIECE, dx00[:])
-        rounded3 = sbuf("rounded3", [P, PIECE, PACK], BF16, tag="q0_codes")
-        nc.scalar.copy(out=woven(rounded3[:]), in_=planar(raw[3][:]))
+        rounded23 = sbuf("rounded23", [P, HALF, PACK], BF16, tag="q0_codes")
+        nc.scalar.copy(out=woven(rounded23[:, 0:PIECE, :]), in_=planar(second[:, :, 0:PIECE]))
+        dx10 = sbuf("dx10", [P, PIECE], F32, tag="r0_codes")
+        nc.scalar.copy(out=dx10[:], in_=banks[5][:, 0:PIECE])
+        nc.scalar.copy(out=woven(rounded23[:, PIECE:, :]), in_=planar(second[:, :, PIECE:]))
         spill = sbuf("spill", [P, J], F32)
         nc.scalar.copy(out=spill[:].rearrange("p (t c j) -> p t c j", t=2, c=2)[:, :, 0, :], in_=banks[6][:].rearrange("p (t j) -> p t j", t=2))
-        subtract(left1[:, BLOCK:, :], 3, banks[3])
-        dx10 = sbuf("dx10", [P, PIECE], F32, tag="first3")
-        nc.scalar.copy(out=dx10[:], in_=banks[5][:, 0:PIECE])
+        for t in (0, 1):
+            product_pass(banks[2 + t][:, 0:PIECE], t, q1[0], q1[1], E5M2, True)
         r1 = operand("r1", PIECE)
         quantise(*r1, left1[:], E4M3)
-        quantise(*cols(q23, PIECE, HALF), rounded3[:], E5M2)
+        q23 = operand("q23", HALF)
+        quantise(*cols(q23, 0, PIECE), rounded23[:, 0:PIECE, :], E5M2)
         scatter(1, 0, PIECE, dx10[:])
+        quantise(*cols(q23, PIECE, HALF), rounded23[:, PIECE:, :], E5M2)
         clear(2, "q0_codes")
 
-        back_banks = {4: banks[0], 5: banks[1], 6: banks[7], 7: banks[5]}
-        sum_banks = {4: banks[4], 5: banks[6], 6: banks[2], 7: banks[3]}
+        back_banks = {4: banks[0], 5: banks[1], 6: banks[7], 7: banks[1]}
+        sum_banks = {4: banks[4], 5: banks[6], 6: banks[0], 7: banks[2]}
         late = sbuf("late", [P, HALF, PACK], BF16)
         late_words = flat(late[:]).bitcast(F32)
         minus = {}
@@ -230,25 +224,24 @@ def tile_list_embg_tgq8_noneP_kernel(tc, dy, w_words, w_scales, wgo, offs, out_0
             nc.scalar.copy(out=late_words[:, at:at + 2 * P].rearrange("p (j u) -> p j u", u=2),
                            in_=sum_banks[b][:, 0:2 * P].rearrange("p (u j) -> p j u", u=2))
 
+        for t in (0, 1):
+            product_pass(banks[2 + t][:, 0:PIECE], t, r1[0], r1[1], E4M3, False)
+            dx1 = sbuf("dx1_%d" % t, [P, PIECE], F32)
+            nc.scalar.copy(out=dx1[:], in_=banks[2 + t][:, 0:PIECE])
+            scatter(t, PIECE, HALF, dx1[:])
+        clear(3, "dx1_0")
         back(4)
         back(5)
         for b in (4, 5):
             turn(b, raw_block(b), True)
         for b in (4, 5):
             negate(b)
-        for t in (0, 1):
-            product(banks[t][:, 0:PIECE], t, q1, r1)
-            dx1 = sbuf("dx1_%d" % t, [P, PIECE], F32)
-            nc.scalar.copy(out=dx1[:], in_=banks[t][:, 0:PIECE])
-            scatter(t, PIECE, HALF, dx1[:])
-        clear(3, "dx1_0")
-        for b in (4, 5):
             turn(b, minus[b], False)
         back(6)
         back(7)
         for t in (2, 3):
-            product(banks[0][:, (t - 2) * PIECE:(t - 1) * PIECE], t, q1, r1)
-        nc.scalar.copy(out=spill[:, PIECE:HALF], in_=banks[0][:, 0:PIECE])
+            product(banks[5][:, (t - 2) * PIECE:(t - 1) * PIECE], t, q1, r1)
+        nc.scalar.copy(out=spill[:, PIECE:HALF], in_=banks[5][:, 0:PIECE])
         scatter(2, 0, HALF, spill[:, 0:HALF])
         scatter(3, 0, PIECE, spill[:, HALF:HALF + PIECE])
         for b in (6, 7):
@@ -268,10 +261,10 @@ def tile_list_embg_tgq8_noneP_kernel(tc, dy, w_words, w_scales, wgo, offs, out_0
             lay_words(b)
         r23 = operand("r23", HALF)
         quantise(*r23, late[:], E4M3)
-        nc.scalar.copy(out=spill[:, J - PIECE:], in_=banks[0][:, PIECE:])
+        nc.scalar.copy(out=spill[:, J - PIECE:], in_=banks[5][:, PIECE:])
         scatter(3, PIECE, HALF, spill[:, J - PIECE:])
 
-        last_banks = [banks[1], banks[7], banks[6], banks[4]]
+        last_banks = [banks[3], banks[7], banks[6], banks[4]]
         dx23 = []
         for t in range(PACK):
             product(last_banks[t][:], t, q23, r23)

@@ -54,27 +54,25 @@ def tile_list_embg_tgq8_noneP_kernel(tc, dy, w_words, w_scales, wgo, offs, out_0
             return sb.tile(shape, dtype, name=name, tag=tag or name, align_bytes=64)
 
         dy_planes = dy.rearrange("(p t) j -> p t j", t=PACK)
-        first = [sbuf("first%d" % s, [P, PACK, BLOCK], F32) for s in range(4)]
+        raw = [sbuf("raw%d" % c, [P, PACK, PIECE], F32) for c in range(J // PIECE)]
 
-        def load_block(b):
-            nc.sync.dma_start(out=first[b][:], in_=dy_planes[:, :, b * BLOCK:(b + 1) * BLOCK])
+        def load_piece(c):
+            nc.sync.dma_start(out=raw[c][:], in_=dy_planes[:, :, c * PIECE:(c + 1) * PIECE])
 
-        load_block(0)
-        load_block(1)
         ws_in = sbuf("ws_in", [P, N], U8)
-        for q in range(QUADS):
-            nc.sync.dma_start(out=ws_in[32 * q:32 * (q + 1), :].bitcast(I32),
-                              in_=w_scales[0, 4 * q:4 * q + 4, :].bitcast(I32).unsqueeze(0).to_broadcast([8, 4, N // 4]))
-        load_block(2)
+        nc.gpsimd.memset(ws_in[:].bitcast(I32), 0)
+        load_piece(0)
         w_in = sbuf("w_in", [P, N], I32)
         nc.sync.dma_start(out=w_in[:], in_=w_words[0].rearrange("p n i -> p (n i)").bitcast(I32))
-        load_block(3)
+        for q in range(QUADS):
+            nc.sync.dma_start(out=ws_in[32 * q:32 * q + 4, :].bitcast(I32), in_=w_scales[0, 4 * q:4 * q + 4, :].bitcast(I32))
+        load_piece(1)
         offsets = sb.tile([P, J // GROUP], U16, name="offsets")
         nc.sync.dma_start(offsets[:], offs)
         gain = [sbuf("gain%d" % h, [P, HALF], F32) for h in range(2)]
         nc.sync.dma_start(out=gain[0][:], in_=wgo[:, 0:HALF])
-        second = sbuf("second", [P, PACK, HALF], F32)
-        nc.sync.dma_start(out=second[:], in_=dy_planes[:, :, HALF:])
+        load_piece(2)
+        load_piece(3)
         nc.sync.dma_start(out=gain[1][:], in_=wgo[:, HALF:])
 
         ones = sbuf("ones", [P, P], F32, tag="page0")
@@ -98,9 +96,8 @@ def tile_list_embg_tgq8_noneP_kernel(tc, dy, w_words, w_scales, wgo, offs, out_0
         banks = [psum.tile([P, HALF], F32, name="bank%d" % b) for b in range(8)]
 
         def raw_block(b):
-            if b < 4:
-                return first[b][:]
-            return second[:, :, (b - 4) * BLOCK:(b - 3) * BLOCK]
+            c, s = divmod(b, 2)
+            return raw[c][:, :, s * BLOCK:(s + 1) * BLOCK]
 
         def quantise(codes, scales, values, fmt):
             nc.vector.quantize_mx(out=codes.bitcast(fmt), scales=scales, in_=flat(values))
@@ -135,31 +132,30 @@ def tile_list_embg_tgq8_noneP_kernel(tc, dy, w_words, w_scales, wgo, offs, out_0
         def cols(pair, lo, hi):
             return pair[0][:, lo:hi], pair[1][:, lo:hi]
 
-        early = sbuf("early", [P, 2 * BLOCK, PACK], BF16, tag="eye_in")
-        rounded = {0: sbuf("rounded0", [P, BLOCK, PACK], BF16, tag="eye_base")[:], 1: early[:, 0:BLOCK, :], 2: early[:, BLOCK:, :]}
+        stage = {0: sbuf("rounded0", [P, BLOCK, PACK], BF16, tag="eye_base"), 1: sbuf("rounded1", [P, BLOCK, PACK], BF16, tag="eye_in")}
         q0 = operand("q0", PIECE)
-        nc.vector.tensor_copy(out=woven(rounded[0]), in_=planar(raw_block(0)))
-        for b in (1, 2):
-            nc.scalar.copy(out=woven(rounded[b]), in_=planar(raw_block(b)))
-        quantise(*cols(q0, 0, BLOCK), rounded[0], E5M2)
-        w_plane = sbuf("w_plane", [P, PACK, P], U8, tag="eye_base")
-        nc.vector.tensor_copy(out=w_plane[:], in_=ws_in[:].rearrange("p (m t) -> p t m", t=PACK))
-        quantise(*cols(q0, BLOCK, PIECE), rounded[1], E5M2)
+        nc.vector.tensor_copy(out=woven(stage[0][:]), in_=planar(raw_block(0)))
+        nc.scalar.copy(out=woven(stage[1][:]), in_=planar(raw_block(1)))
+        for s in range(2):
+            quantise(*cols(q0, s * BLOCK, (s + 1) * BLOCK), stage[s][:], E5M2)
         for s in range(2):
             bring_back(banks[s], *cols(q0, s * BLOCK, (s + 1) * BLOCK))
-        w_codes = sbuf("w_codes", [P, PACK, P], U32, tag="ws_in")
+        w_codes = sbuf("w_codes", [P, PACK, P], U32, tag="eye_base")
         nc.scalar.copy(out=w_codes[:].rearrange("p t m -> p m t"), in_=w_in[:].bitcast(U32).rearrange("p (m t) -> p m t", t=PACK))
-        stage = sbuf("stage", [P, BLOCK, PACK], BF16, tag="w_in")
-        nc.scalar.copy(out=woven(stage[:]), in_=planar(raw_block(3)))
+        w_plane = sbuf("w_plane", [P, PACK, P], U8, tag="eye_in")
+        nc.vector.tensor_copy(out=w_plane[:], in_=ws_in[:].rearrange("p (m t) -> p t m", t=PACK))
+        rounded1 = sbuf("rounded23x", [P, PIECE, PACK], BF16, tag="w_in")
+        for s in range(2):
+            nc.scalar.copy(out=woven(rounded1[:, s * BLOCK:(s + 1) * BLOCK, :]), in_=planar(raw_block(2 + s)))
         product_pass(banks[4][:, 0:PIECE], 0, q0[0], q0[1], E5M2, True)
         left0 = sbuf("left0", [P, PIECE, PACK], BF16)
         for s in range(2):
             subtract(left0[:, s * BLOCK:(s + 1) * BLOCK, :], s, banks[s])
-        q1 = operand("q1", PIECE, tag="first0")
-        quantise(*cols(q1, 0, BLOCK), rounded[2], E5M2)
+        q1 = operand("q1", PIECE, tag="raw0")
+        quantise(*cols(q1, 0, BLOCK), rounded1[:, 0:BLOCK, :], E5M2)
         r0 = operand("r0", PIECE)
         quantise(*r0, left0[:], E4M3)
-        quantise(*cols(q1, BLOCK, PIECE), stage[:], E5M2)
+        quantise(*cols(q1, BLOCK, PIECE), rounded1[:, BLOCK:, :], E5M2)
         bring_back(banks[2], *cols(q1, 0, BLOCK))
         product_pass(banks[4][:, 0:PIECE], 0, r0[0], r0[1], E4M3, False)
         dx00 = sbuf("dx00", [P, PIECE], F32)
@@ -175,10 +171,10 @@ def tile_list_embg_tgq8_noneP_kernel(tc, dy, w_words, w_scales, wgo, offs, out_0
         clear(1, "w_in")
         scatter(0, 0, PIECE, dx00[:])
         rounded23 = sbuf("rounded23", [P, HALF, PACK], BF16, tag="q0_codes")
-        nc.scalar.copy(out=woven(rounded23[:, 0:PIECE, :]), in_=planar(second[:, :, 0:PIECE]))
+        nc.scalar.copy(out=woven(rounded23[:, 0:PIECE, :]), in_=planar(raw[2][:]))
         dx10 = sbuf("dx10", [P, PIECE], F32, tag="r0_codes")
         nc.scalar.copy(out=dx10[:], in_=banks[5][:, 0:PIECE])
-        nc.scalar.copy(out=woven(rounded23[:, PIECE:, :]), in_=planar(second[:, :, PIECE:]))
+        nc.scalar.copy(out=woven(rounded23[:, PIECE:, :]), in_=planar(raw[3][:]))
         spill = sbuf("spill", [P, J], F32)
         nc.scalar.copy(out=spill[:].rearrange("p (t c j) -> p t c j", t=2, c=2)[:, :, 0, :], in_=banks[6][:].rearrange("p (t j) -> p t j", t=2))
         for t in (0, 1):

@@ -28,6 +28,7 @@ PAD = 64
 BLOCK = 128
 LAST_ON_VECTOR = 1024
 SEAM = 16
+LAST_WORDS_ON_VECTOR = 160
 CLEARED_BY_VECTOR = 768
 
 
@@ -141,13 +142,14 @@ def tile_list_embg_tgq8_noneP_kernel(tc, dy, w_words, w_scales, wgo, offs, out_0
         for s in range(2):
             bring_back(banks[s], *cols(q0, s * BLOCK, (s + 1) * BLOCK))
         w_codes = sbuf("w_codes", [P, PACK, P], U32, tag="eye_base")
-        nc.scalar.copy(out=w_codes[:].rearrange("p t m -> p m t"), in_=w_in[:].bitcast(U32).rearrange("p (m t) -> p m t", t=PACK))
+        nc.scalar.copy(out=planar(w_codes[:]), in_=woven(w_in[:].bitcast(U32).rearrange("p (m t) -> p m t", t=PACK)))
         w_plane = sbuf("w_plane", [P, PACK, P], U8, tag="eye_in")
         nc.vector.tensor_copy(out=w_plane[:], in_=ws_in[:].rearrange("p (m t) -> p t m", t=PACK))
         rounded1 = sbuf("rounded23x", [P, PIECE, PACK], BF16, tag="w_in")
         for s in range(2):
             nc.scalar.copy(out=woven(rounded1[:, s * BLOCK:(s + 1) * BLOCK, :]), in_=planar(raw_block(2 + s)))
-        product_pass(banks[4][:, 0:PIECE], 0, q0[0], q0[1], E5M2, True)
+        for t in range(PACK):
+            product_pass(banks[4 + t][:, 0:PIECE], t, q0[0], q0[1], E5M2, True)
         left0 = sbuf("left0", [P, PIECE, PACK], BF16)
         for s in range(2):
             subtract(left0[:, s * BLOCK:(s + 1) * BLOCK, :], s, banks[s])
@@ -161,34 +163,34 @@ def tile_list_embg_tgq8_noneP_kernel(tc, dy, w_words, w_scales, wgo, offs, out_0
         dx00 = sbuf("dx00", [P, PIECE], F32)
         nc.scalar.copy(out=dx00[:], in_=banks[4][:, 0:PIECE])
         bring_back(banks[3], *cols(q1, BLOCK, PIECE))
-        product(banks[5][:, 0:PIECE], 1, q0, r0)
-        for t in (2, 3):
-            product(banks[6][:, (t - 2) * PIECE:(t - 1) * PIECE], t, q0, r0)
+        for t in range(1, PACK):
+            product_pass(banks[4 + t][:, 0:PIECE], t, r0[0], r0[1], E4M3, False)
 
         left1 = sbuf("left1", [P, PIECE, PACK], BF16)
         for s in range(2):
             subtract(left1[:, s * BLOCK:(s + 1) * BLOCK, :], 2 + s, banks[2 + s])
         clear(1, "w_in")
         scatter(0, 0, PIECE, dx00[:])
-        rounded23 = sbuf("rounded23", [P, HALF, PACK], BF16, tag="q0_codes")
+        rounded23 = sbuf("rounded23", [P, HALF, PACK], BF16, tag="r0_codes")
         nc.scalar.copy(out=woven(rounded23[:, 0:PIECE, :]), in_=planar(raw[2][:]))
-        dx10 = sbuf("dx10", [P, PIECE], F32, tag="r0_codes")
+        dx10 = sbuf("dx10", [P, PIECE], F32, tag="raw1")
         nc.scalar.copy(out=dx10[:], in_=banks[5][:, 0:PIECE])
         nc.scalar.copy(out=woven(rounded23[:, PIECE:, :]), in_=planar(raw[3][:]))
         spill = sbuf("spill", [P, J], F32)
-        nc.scalar.copy(out=spill[:].rearrange("p (t c j) -> p t c j", t=2, c=2)[:, :, 0, :], in_=banks[6][:].rearrange("p (t j) -> p t j", t=2))
+        for t in (2, 3):
+            nc.scalar.copy(out=spill[:, (t - 2) * HALF:(t - 2) * HALF + PIECE], in_=banks[4 + t][:, 0:PIECE])
         for t in (0, 1):
-            product_pass(banks[2 + t][:, 0:PIECE], t, q1[0], q1[1], E5M2, True)
+            product_pass(banks[t][:, 0:PIECE], t, q1[0], q1[1], E5M2, True)
         r1 = operand("r1", PIECE)
         quantise(*r1, left1[:], E4M3)
         q23 = operand("q23", HALF)
         quantise(*cols(q23, 0, PIECE), rounded23[:, 0:PIECE, :], E5M2)
         scatter(1, 0, PIECE, dx10[:])
         quantise(*cols(q23, PIECE, HALF), rounded23[:, PIECE:, :], E5M2)
-        clear(2, "q0_codes")
+        clear(2, "r0_codes")
 
-        back_banks = {4: banks[0], 5: banks[1], 6: banks[7], 7: banks[1]}
-        sum_banks = {4: banks[4], 5: banks[6], 6: banks[0], 7: banks[2]}
+        back_banks = {4: banks[7], 5: banks[0], 6: banks[1], 7: banks[7]}
+        sum_banks = {4: banks[4], 5: banks[2], 6: banks[3], 7: banks[5]}
         late = sbuf("late", [P, HALF, PACK], BF16)
         late_words = flat(late[:]).bitcast(F32)
         minus = {}
@@ -221,27 +223,25 @@ def tile_list_embg_tgq8_noneP_kernel(tc, dy, w_words, w_scales, wgo, offs, out_0
                            in_=sum_banks[b][:, 0:2 * P].rearrange("p (u j) -> p j u", u=2))
 
         for t in (0, 1):
-            product_pass(banks[2 + t][:, 0:PIECE], t, r1[0], r1[1], E4M3, False)
+            product_pass(banks[t][:, 0:PIECE], t, r1[0], r1[1], E4M3, False)
             dx1 = sbuf("dx1_%d" % t, [P, PIECE], F32)
-            nc.scalar.copy(out=dx1[:], in_=banks[2 + t][:, 0:PIECE])
+            nc.scalar.copy(out=dx1[:], in_=banks[t][:, 0:PIECE])
             scatter(t, PIECE, HALF, dx1[:])
         clear(3, "dx1_0")
+        for t in (2, 3):
+            product(banks[6][:, (t - 2) * PIECE:(t - 1) * PIECE], t, q1, r1)
+        nc.scalar.copy(out=spill[:, PIECE:HALF], in_=banks[6][:, 0:PIECE])
         back(4)
         back(5)
-        for b in (4, 5):
+        for b in (4, 5, 6, 7):
             turn(b, raw_block(b), True)
         for b in (4, 5):
             negate(b)
             turn(b, minus[b], False)
         back(6)
         back(7)
-        for t in (2, 3):
-            product(banks[5][:, (t - 2) * PIECE:(t - 1) * PIECE], t, q1, r1)
-        nc.scalar.copy(out=spill[:, PIECE:HALF], in_=banks[5][:, 0:PIECE])
         scatter(2, 0, HALF, spill[:, 0:HALF])
         scatter(3, 0, PIECE, spill[:, HALF:HALF + PIECE])
-        for b in (6, 7):
-            turn(b, raw_block(b), True)
         for b in (4, 5):
             round_sums(b)
             turn_back(b)
@@ -257,16 +257,16 @@ def tile_list_embg_tgq8_noneP_kernel(tc, dy, w_words, w_scales, wgo, offs, out_0
             lay_words(b)
         r23 = operand("r23", HALF)
         quantise(*r23, late[:], E4M3)
-        nc.scalar.copy(out=spill[:, J - PIECE:], in_=banks[5][:, PIECE:])
+        nc.scalar.copy(out=spill[:, J - PIECE:], in_=banks[6][:, PIECE:])
         scatter(3, PIECE, HALF, spill[:, J - PIECE:])
 
-        last_banks = [banks[3], banks[7], banks[6], banks[4]]
-        dx23 = []
-        for t in range(PACK):
-            product(last_banks[t][:], t, q23, r23)
-        for t in range(PACK):
-            dx23.append(sbuf("dx23_%d" % t, [P, HALF], F32))
-            nc.scalar.copy(out=dx23[t][:], in_=last_banks[t][:])
+        dx23 = [sbuf("dx23_%d" % t, [P, HALF], F32) for t in range(PACK)]
+        for s, bank in enumerate((banks[4], banks[2])):
+            product(bank[:, 0:PIECE], 0, cols(q23, s * PIECE, (s + 1) * PIECE), cols(r23, s * PIECE, (s + 1) * PIECE))
+            nc.scalar.copy(out=dx23[0][:, s * PIECE:(s + 1) * PIECE], in_=bank[:, 0:PIECE])
+        for t, bank in ((1, banks[0]), (2, banks[1]), (3, banks[7])):
+            product(bank[:], t, q23, r23)
+            nc.scalar.copy(out=dx23[t][:], in_=bank[:])
 
         out_planes = out_0.rearrange("(p t) c -> p t c", t=PACK)
         shares = ((0, LAST_ON_VECTOR), (LAST_ON_VECTOR, T))
@@ -290,18 +290,21 @@ def tile_list_embg_tgq8_noneP_kernel(tc, dy, w_words, w_scales, wgo, offs, out_0
 
         words_out = out_1[0].rearrange("p c i -> p (c i)").bitcast(I32)
         y_scales = sbuf("y_scales", [P, T // 2], U8)
-        grouped = []
-        for c in range(T // CHUNK):
-            i = 0 if c * CHUNK < LAST_ON_VECTOR else 1
-            at = c * CHUNK - shares[i][0]
-            grouped.append(sbuf("grouped%d" % c, [P, CHUNK * PACK], BF16))
-            word = (I32, U32)[i]
-            src = pairs[i][:].bitcast(word).rearrange("p (u c) -> p u c", u=2)[:, :, at:at + CHUNK].rearrange("p u (c i) -> p c u i", i=PACK)
-            dst = grouped[c][:].bitcast(word).rearrange("p (c i u) -> p c u i", i=PACK, u=2)
-            if i == 0:
-                nc.vector.tensor_copy(out=dst, in_=src)
-            else:
-                nc.scalar.copy(out=dst, in_=src)
+        grouped = [sbuf("grouped%d" % c, [P, CHUNK * PACK], BF16) for c in range(T // CHUNK)]
+
+        def weave_words(lo, hi, on_vector):
+            c, i = lo // CHUNK, 0 if lo < LAST_ON_VECTOR else 1
+            word = I32 if on_vector else U32
+            src = pairs[i][:].bitcast(word).rearrange("p (u c) -> p u c", u=2)[:, :, lo - shares[i][0]:hi - shares[i][0]]
+            dst = grouped[c][:].bitcast(word)[:, 2 * (lo - c * CHUNK):2 * (hi - c * CHUNK)]
+            copy = nc.vector.tensor_copy if on_vector else nc.scalar.copy
+            copy(out=dst.rearrange("p (c i u) -> p c u i", i=PACK, u=2), in_=src.rearrange("p u (c i) -> p c u i", i=PACK))
+
+        weave_words(0, CHUNK, True)
+        weave_words(CHUNK, 2 * CHUNK, True)
+        weave_words(2 * CHUNK, 3 * CHUNK, False)
+        weave_words(3 * CHUNK, T - LAST_WORDS_ON_VECTOR, False)
+        weave_words(T - LAST_WORDS_ON_VECTOR, T, True)
         for c in range(T // CHUNK):
             columns = slice(c * CHUNK, (c + 1) * CHUNK)
             shift, side = divmod(c, 2)

@@ -22,14 +22,14 @@ QUADS = 4
 GROUP = 16
 HALF = 512
 PIECE = 256
-CHUNK = 512
-PAD = 64
-
 BLOCK = 128
+CHUNK = 512
+PAD = 68
+
 LAST_ON_VECTOR = 1024
 SEAM = 16
-LAST_WORDS_ON_VECTOR = 160
-CLEARED_BY_VECTOR = 768
+LAST_CHUNK = 256
+EARLY = 3 * BLOCK
 
 
 def woven(tile3, run=PACK):
@@ -55,26 +55,28 @@ def tile_list_embg_tgq8_noneP_kernel(tc, dy, w_words, w_scales, wgo, offs, out_0
             return sb.tile(shape, dtype, name=name, tag=tag or name, align_bytes=64)
 
         dy_planes = dy.rearrange("(p t) j -> p t j", t=PACK)
-        raw = [sbuf("raw%d" % c, [P, PACK, PIECE], F32) for c in range(J // PIECE)]
+        spans = ((0, 1), (1, 2), (2, 4), (4, 6), (6, 8))
+        raw = [sbuf("raw%d" % lo, [P, PACK, (hi - lo) * BLOCK], F32) for lo, hi in spans]
 
         def load_piece(c):
-            nc.sync.dma_start(out=raw[c][:], in_=dy_planes[:, :, c * PIECE:(c + 1) * PIECE])
+            nc.sync.dma_start(out=raw[c][:], in_=dy_planes[:, :, spans[c][0] * BLOCK:spans[c][1] * BLOCK])
 
         ws_in = sbuf("ws_in", [P, N], U8)
         nc.gpsimd.memset(ws_in[:].bitcast(I32), 0)
         load_piece(0)
-        w_in = sbuf("w_in", [P, N], I32)
-        nc.sync.dma_start(out=w_in[:], in_=w_words[0].rearrange("p n i -> p (n i)").bitcast(I32))
+        load_piece(1)
         for q in range(QUADS):
             nc.sync.dma_start(out=ws_in[32 * q:32 * q + 4, :].bitcast(I32), in_=w_scales[0, 4 * q:4 * q + 4, :].bitcast(I32))
-        load_piece(1)
+        load_piece(2)
+        w_in = sbuf("w_in", [P, N], I32)
+        nc.sync.dma_start(out=w_in[:], in_=w_words[0].rearrange("p n i -> p (n i)").bitcast(I32))
+        load_piece(3)
         offsets = sb.tile([P, J // GROUP], U16, name="offsets")
         nc.sync.dma_start(offsets[:], offs)
-        gain = [sbuf("gain%d" % h, [P, HALF], F32) for h in range(2)]
-        nc.sync.dma_start(out=gain[0][:], in_=wgo[:, 0:HALF])
-        load_piece(2)
-        load_piece(3)
-        nc.sync.dma_start(out=gain[1][:], in_=wgo[:, HALF:])
+        gain = sbuf("gain", [P, J], F32)
+        nc.sync.dma_start(out=gain[:, 0:EARLY], in_=wgo[:, 0:EARLY])
+        load_piece(4)
+        nc.sync.dma_start(out=gain[:, EARLY:], in_=wgo[:, EARLY:])
 
         ones = sbuf("ones", [P, P], F32, tag="page0")
         nc.gpsimd.memset(ones[:], 1.0)
@@ -85,47 +87,24 @@ def tile_list_embg_tgq8_noneP_kernel(tc, dy, w_words, w_scales, wgo, offs, out_0
         row = P * PACK
         eye_codes = sbuf("eye_codes", [P, PACK * row + PAD], U8)
         nc.vector.memset(eye_codes[:].bitcast(I32), 0)
-        pages = {0: sbuf("page0", [P, T], F32)}
-        nc.vector.memset(pages[0][:, 0:CLEARED_BY_VECTOR].bitcast(I32), 0)
-        nc.gpsimd.memset(pages[0][:, CLEARED_BY_VECTOR:], 0.0)
+        pages = {0: sbuf("page0", [P, T], F32), 1: sbuf("page1", [P, T], F32)}
+        nc.vector.memset(pages[1][:, 0:T // 2 - 1].bitcast(I32), 0)
+        nc.vector.memset(pages[1][:, T // 2 - 1:].bitcast(I32), 0)
+        nc.gpsimd.memset(pages[0][:], 0.0)
         eye_base = sbuf("eye_base", [P, P, PACK], U8)
         eye_scales = sbuf("eye_scales", [P, P], U8)
         nc.vector.quantize_mx(out=flat(eye_base[:]).bitcast(E4M3), scales=eye_scales[:], in_=flat(eye_in[:]))
         diagonal = eye_codes[:, 0:PACK * (row + 1)].rearrange("p (t x) -> p t x", t=PACK)[:, :, 0:row:PACK]
-        nc.vector.tensor_copy(out=diagonal, in_=eye_base[:].rearrange("p m t -> p t m"))
 
         banks = [psum.tile([P, HALF], F32, name="bank%d" % b) for b in range(8)]
 
         def raw_block(b):
-            c, s = divmod(b, 2)
+            c = max(i for i, span in enumerate(spans) if span[0] <= b)
+            s = b - spans[c][0]
             return raw[c][:, :, s * BLOCK:(s + 1) * BLOCK]
 
-        def quantise(codes, scales, values, fmt):
-            nc.vector.quantize_mx(out=codes.bitcast(fmt), scales=scales, in_=flat(values))
-
-        def bring_back(bank, codes, scales):
-            for t in range(PACK):
-                nc.tensor.matmul_mx(out=bank[:, t * BLOCK:(t + 1) * BLOCK], lhsT=eye_codes[:, t * row:(t + 1) * row].bitcast(E4M3),
-                                    lhsT_scale=eye_scales[:], rhs=codes.bitcast(E5M2), rhs_scale=scales, start=True, stop=True)
-
-        def subtract(left, b, bank):
-            nc.vector.tensor_tensor(woven(left, 2), planar(raw_block(b), 2), planar(bank[:].rearrange("p (t j) -> p t j", t=PACK), 2), SUB)
-
-        def product_pass(out, t, codes, scales, fmt, opens):
-            nc.tensor.matmul_mx(out=out, lhsT=w_codes[:, t, :].bitcast(E4M3), lhsT_scale=w_plane[:, t, :],
-                                rhs=codes.bitcast(fmt), rhs_scale=scales, start=opens, stop=not opens)
-
-        def product(out, t, q, r):
-            product_pass(out, t, q[0], q[1], E5M2, True)
-            product_pass(out, t, r[0], r[1], E4M3, False)
-
-        def scatter(t, lo, hi, dx):
-            h = lo // HALF
-            nc.vector.tensor_tensor(pages[t][:].indirect(offsets[:, lo // GROUP:hi // GROUP]), dx, gain[h][:, lo - h * HALF:hi - h * HALF], MULT)
-
-        def clear(t, freed):
-            pages[t] = sbuf("page%d" % t, [P, T], F32, tag=freed)
-            nc.gpsimd.memset(pages[t][:], 0.0)
+        def block_of(tile3, s):
+            return tile3[:, s * BLOCK:(s + 1) * BLOCK, :]
 
         def operand(name, width, tag=None):
             return sbuf(name + "_codes", [P, width], U32, tag=tag)[:], sbuf(name + "_scales", [P, width], U8)[:]
@@ -133,150 +112,187 @@ def tile_list_embg_tgq8_noneP_kernel(tc, dy, w_words, w_scales, wgo, offs, out_0
         def cols(pair, lo, hi):
             return pair[0][:, lo:hi], pair[1][:, lo:hi]
 
-        stage = {0: sbuf("rounded0", [P, BLOCK, PACK], BF16, tag="eye_base"), 1: sbuf("rounded1", [P, BLOCK, PACK], BF16, tag="eye_in")}
-        q0 = operand("q0", PIECE)
-        nc.vector.tensor_copy(out=woven(stage[0][:]), in_=planar(raw_block(0)))
-        nc.scalar.copy(out=woven(stage[1][:]), in_=planar(raw_block(1)))
-        for s in range(2):
-            quantise(*cols(q0, s * BLOCK, (s + 1) * BLOCK), stage[s][:], E5M2)
-        for s in range(2):
-            bring_back(banks[s], *cols(q0, s * BLOCK, (s + 1) * BLOCK))
-        w_codes = sbuf("w_codes", [P, PACK, P], U32, tag="eye_base")
-        nc.scalar.copy(out=planar(w_codes[:]), in_=woven(w_in[:].bitcast(U32).rearrange("p (m t) -> p m t", t=PACK)))
-        w_plane = sbuf("w_plane", [P, PACK, P], U8, tag="eye_in")
-        nc.vector.tensor_copy(out=w_plane[:], in_=ws_in[:].rearrange("p (m t) -> p t m", t=PACK))
-        rounded1 = sbuf("rounded23x", [P, PIECE, PACK], BF16, tag="w_in")
-        for s in range(2):
-            nc.scalar.copy(out=woven(rounded1[:, s * BLOCK:(s + 1) * BLOCK, :]), in_=planar(raw_block(2 + s)))
-        for t in range(PACK):
-            product_pass(banks[4 + t][:, 0:PIECE], t, q0[0], q0[1], E5M2, True)
-        left0 = sbuf("left0", [P, PIECE, PACK], BF16)
-        for s in range(2):
-            subtract(left0[:, s * BLOCK:(s + 1) * BLOCK, :], s, banks[s])
-        q1 = operand("q1", PIECE, tag="raw0")
-        quantise(*cols(q1, 0, BLOCK), rounded1[:, 0:BLOCK, :], E5M2)
-        r0 = operand("r0", PIECE)
-        quantise(*r0, left0[:], E4M3)
-        quantise(*cols(q1, BLOCK, PIECE), rounded1[:, BLOCK:, :], E5M2)
-        bring_back(banks[2], *cols(q1, 0, BLOCK))
-        product_pass(banks[4][:, 0:PIECE], 0, r0[0], r0[1], E4M3, False)
-        dx00 = sbuf("dx00", [P, PIECE], F32)
-        nc.scalar.copy(out=dx00[:], in_=banks[4][:, 0:PIECE])
-        bring_back(banks[3], *cols(q1, BLOCK, PIECE))
-        for t in range(1, PACK):
-            product_pass(banks[4 + t][:, 0:PIECE], t, r0[0], r0[1], E4M3, False)
+        def quantise(pair, values, fmt):
+            nc.vector.quantize_mx(out=pair[0].bitcast(fmt), scales=pair[1], in_=flat(values))
 
-        left1 = sbuf("left1", [P, PIECE, PACK], BF16)
-        for s in range(2):
-            subtract(left1[:, s * BLOCK:(s + 1) * BLOCK, :], 2 + s, banks[2 + s])
-        clear(1, "w_in")
-        scatter(0, 0, PIECE, dx00[:])
-        rounded23 = sbuf("rounded23", [P, HALF, PACK], BF16, tag="r0_codes")
-        nc.scalar.copy(out=woven(rounded23[:, 0:PIECE, :]), in_=planar(raw[2][:]))
-        dx10 = sbuf("dx10", [P, PIECE], F32, tag="raw1")
-        nc.scalar.copy(out=dx10[:], in_=banks[5][:, 0:PIECE])
-        nc.scalar.copy(out=woven(rounded23[:, PIECE:, :]), in_=planar(raw[3][:]))
-        spill = sbuf("spill", [P, J], F32)
-        for t in (2, 3):
-            nc.scalar.copy(out=spill[:, (t - 2) * HALF:(t - 2) * HALF + PIECE], in_=banks[4 + t][:, 0:PIECE])
-        for t in (0, 1):
-            product_pass(banks[t][:, 0:PIECE], t, q1[0], q1[1], E5M2, True)
-        r1 = operand("r1", PIECE)
-        quantise(*r1, left1[:], E4M3)
-        q23 = operand("q23", HALF)
-        quantise(*cols(q23, 0, PIECE), rounded23[:, 0:PIECE, :], E5M2)
-        scatter(1, 0, PIECE, dx10[:])
-        quantise(*cols(q23, PIECE, HALF), rounded23[:, PIECE:, :], E5M2)
-        clear(2, "r0_codes")
+        def round_block(out, b):
+            nc.scalar.copy(out=woven(out), in_=planar(raw_block(b)))
 
-        back_banks = {4: banks[7], 5: banks[0], 6: banks[1], 7: banks[7]}
-        sum_banks = {4: banks[4], 5: banks[2], 6: banks[3], 7: banks[5]}
-        late = sbuf("late", [P, HALF, PACK], BF16)
-        late_words = flat(late[:]).bitcast(F32)
-        minus = {}
-        turned = {}
-
-        def back(b):
-            bring_back(back_banks[b], *cols(q23, (b - 4) * BLOCK, (b - 3) * BLOCK))
-
-        def turn(b, values, first):
+        def bring_back(bank, pair):
             for t in range(PACK):
-                nc.tensor.matmul(sum_banks[b][:, t * P:(t + 1) * P], lhsT=values[:, t, :], rhs=eye[:], is_transpose=True,
+                nc.tensor.matmul_mx(out=bank[:, t * BLOCK:(t + 1) * BLOCK], lhsT=eye_codes[:, t * row:(t + 1) * row].bitcast(E4M3),
+                                    lhsT_scale=eye_scales[:], rhs=pair[0].bitcast(E5M2), rhs_scale=pair[1], start=True, stop=True)
+
+        def empty(name, sums, width, tag=None):
+            dx = sbuf(name, [P, width], F32, tag=tag)
+            nc.scalar.copy(out=dx[:], in_=sums)
+            return dx
+
+        def scatter(t, lo, hi, dx):
+            nc.vector.tensor_tensor(pages[t][:].indirect(offsets[:, lo // GROUP:hi // GROUP]), dx, gain[:, lo:hi], MULT)
+
+        def clear(t, freed):
+            pages[t] = sbuf("page%d" % t, [P, T], F32, tag=freed)
+            nc.gpsimd.memset(pages[t][:], 0.0)
+
+        def turn(bank, values, first):
+            for t in range(PACK):
+                nc.tensor.matmul(bank[:, t * P:(t + 1) * P], lhsT=values[:, t, :], rhs=eye[:], is_transpose=True,
                                  start=(first and t == 0), stop=(not first and t == PACK - 1))
 
-        def negate(b):
-            minus[b] = sbuf("minus%d" % b, [P, PACK, BLOCK], F32)
-            nc.scalar.mul(flat(minus[b][:]), back_banks[b][:], -1.0)
+        def negate(b, bank):
+            minus = sbuf("minus%d" % b, [P, PACK, BLOCK], F32)
+            nc.scalar.mul(flat(minus[:]), bank[:], -1.0)
+            return minus
 
-        def round_sums(b):
-            turned[b] = spill[:, J - PIECE:] if b == 7 else sbuf("turned%d" % b, [P, 2 * P], F32)[:]
-            nc.scalar.copy(out=turned[b].bitcast(BF16).rearrange("p (u m e) -> p u m e", u=2, e=2),
-                           in_=sum_banks[b][:].rearrange("p (u e m) -> p u m e", u=2, e=2))
-
-        def turn_back(b):
+        def round_sums(b, bank):
+            turned = sbuf("turned%d" % b, [P, 2 * P], F32)
+            nc.scalar.copy(out=turned[:].bitcast(BF16).rearrange("p (u m e) -> p u m e", u=2, e=2),
+                           in_=bank[:].rearrange("p (u e m) -> p u m e", u=2, e=2))
             for u in range(2):
-                nc.tensor.transpose(sum_banks[b][:, u * P:(u + 1) * P], turned[b][:, u * P:(u + 1) * P], eye[:])
+                nc.tensor.transpose(bank[:, u * P:(u + 1) * P], turned[:, u * P:(u + 1) * P], eye[:])
 
-        def lay_words(b):
-            at = 2 * (b - 4) * BLOCK
-            nc.scalar.copy(out=late_words[:, at:at + 2 * P].rearrange("p (j u) -> p j u", u=2),
-                           in_=sum_banks[b][:, 0:2 * P].rearrange("p (u j) -> p j u", u=2))
+        def lay_words(left, s, bank):
+            nc.scalar.copy(out=flat(block_of(left, s)).bitcast(F32).rearrange("p (j u) -> p j u", u=2),
+                           in_=bank[:, 0:2 * P].rearrange("p (u j) -> p j u", u=2))
 
-        for t in (0, 1):
-            product_pass(banks[t][:, 0:PIECE], t, r1[0], r1[1], E4M3, False)
-            dx1 = sbuf("dx1_%d" % t, [P, PIECE], F32)
-            nc.scalar.copy(out=dx1[:], in_=banks[t][:, 0:PIECE])
-            scatter(t, PIECE, HALF, dx1[:])
-        clear(3, "dx1_0")
-        for t in (2, 3):
-            product(banks[6][:, (t - 2) * PIECE:(t - 1) * PIECE], t, q1, r1)
-        nc.scalar.copy(out=spill[:, PIECE:HALF], in_=banks[6][:, 0:PIECE])
+        def subtract(out, b):
+            nc.vector.tensor_tensor(woven(out, 2), planar(raw_block(b), 2),
+                                    planar(banks[b][:].rearrange("p (t j) -> p t j", t=PACK), 2), SUB)
+
+        def run_of(tile3, lo, hi):
+            return tile3[:, lo * BLOCK:hi * BLOCK, :]
+
+        def blocks(pair, lo, hi):
+            return cols(pair, lo * BLOCK, hi * BLOCK)
+
+        def product(bank, t, first, second, backwards=False):
+            passes = []
+            for parts, fmt in ((first, E5M2), (second, E4M3)):
+                at = 0
+                for pair in parts:
+                    width = pair[0].shape[1]
+                    passes.append((at, width, pair, fmt))
+                    at = at + width
+            passes = passes[::-1] if backwards else passes
+            return [lambda i=i, x=x: nc.tensor.matmul_mx(out=bank[:, x[0]:x[0] + x[1]], lhsT=w_codes[:, t, :].bitcast(E4M3), lhsT_scale=w_plane[:, t, :],
+                                                         rhs=x[2][0].bitcast(x[3]), rhs_scale=x[2][1], start=(i == 0), stop=(i == len(passes) - 1))
+                    for i, x in enumerate(passes)]
+
+        def issue(calls):
+            for call in calls:
+                call()
+
+        rounded01 = sbuf("rounded01", [P, 2 * BLOCK, PACK], BF16, tag="eye_in")
+        q01 = operand("q01", 2 * BLOCK)
+        nc.vector.tensor_copy(out=woven(run_of(rounded01[:], 0, 1)), in_=planar(raw_block(0)))
+        nc.vector.tensor_copy(out=diagonal, in_=eye_base[:].rearrange("p m t -> p t m"))
+        round_block(run_of(rounded01[:], 1, 2), 1)
+        for s in range(2):
+            quantise(blocks(q01, s, s + 1), run_of(rounded01[:], s, s + 1), E5M2)
+        for s in range(2):
+            bring_back(banks[s], blocks(q01, s, s + 1))
+        w_plane = sbuf("w_plane", [P, PACK, P], U8, tag="eye_in")
+        nc.vector.tensor_copy(out=w_plane[:], in_=ws_in[:].rearrange("p (m t) -> p t m", t=PACK))
+        rounded2 = sbuf("rounded2", [P, BLOCK, PACK], BF16, tag="eye_base")
+        round_block(rounded2[:], 2)
+        w_codes = sbuf("w_codes", [P, PACK, P], U32, tag="ws_in")
+        nc.scalar.copy(out=planar(w_codes[:]), in_=woven(w_in[:].bitcast(U32).rearrange("p (m t) -> p m t", t=PACK)))
+        rounded34 = sbuf("rounded34", [P, 2 * BLOCK, PACK], BF16, tag="eye_base")
+        for s in range(2):
+            round_block(run_of(rounded34[:], s, s + 1), 3 + s)
+
+        left01 = sbuf("left01", [P, 2 * BLOCK, PACK], BF16)
+        r012 = operand("r012", 3 * BLOCK)
+        r_late = operand("r_late", 5 * BLOCK)
+        subtract(run_of(left01[:], 0, 1), 0)
+        q2 = operand("q2", BLOCK, tag="raw0")
+        quantise(q2, rounded2[:], E5M2)
+        subtract(run_of(left01[:], 1, 2), 1)
+        bring_back(banks[2], q2)
+        for s in range(2):
+            quantise(blocks(r012, s, s + 1), run_of(left01[:], s, s + 1), E4M3)
+        opening = product(banks[4], 0, [q01], [blocks(r012, 0, 1), blocks(r012, 1, 2)])
+        early = {t: product(bank, t, [q01, q2], [blocks(r012, 0, 2), blocks(r012, 2, 3)], t > 1) for t, bank in ((1, banks[1]), (2, banks[6]), (3, banks[7]))}
+        issue(opening)
+        dx00 = empty("dx00", banks[4][:, 0:2 * BLOCK], 2 * BLOCK)
+        left2 = sbuf("left2", [P, BLOCK, PACK], BF16, tag="left01")
+        subtract(left2[:], 2)
+        q_late = operand("q_late", 5 * BLOCK)
+        quantise(blocks(q_late, 0, 2), rounded34[:], E5M2)
+        quantise(blocks(r012, 2, 3), left2[:], E4M3)
+        clear(2, "eye_base")
+        scatter(0, 0, 2 * BLOCK, dx00[:])
+        issue(early[1])
+        scatter(1, 0, 3 * BLOCK, empty("dx1a", banks[1][:, 0:3 * BLOCK], 3 * BLOCK)[:])
+
+        back_banks = {3: banks[3], 4: banks[0], 5: banks[5], 6: banks[3], 7: banks[0]}
+        sum_banks = {3: banks[2], 4: banks[4], 5: banks[1], 6: banks[6], 7: banks[5]}
+        left_late = sbuf("left_late", [P, 5 * BLOCK, PACK], BF16)
+
+        def back(b):
+            bring_back(back_banks[b], blocks(q_late, b - 3, b - 2))
+
+        def add_up(b):
+            turn(sum_banks[b], raw_block(b), True)
+            turn(sum_banks[b], negate(b, back_banks[b]), False)
+
+        back(3)
         back(4)
-        back(5)
-        for b in (4, 5, 6, 7):
-            turn(b, raw_block(b), True)
-        for b in (4, 5):
-            negate(b)
-            turn(b, minus[b], False)
-        back(6)
-        back(7)
-        scatter(2, 0, HALF, spill[:, 0:HALF])
-        scatter(3, 0, PIECE, spill[:, HALF:HALF + PIECE])
-        for b in (4, 5):
-            round_sums(b)
-            turn_back(b)
-        for b in (6, 7):
-            negate(b)
-            turn(b, minus[b], False)
-        for b in (4, 5):
-            lay_words(b)
-        for b in (6, 7):
-            round_sums(b)
-            turn_back(b)
-        for b in (6, 7):
-            lay_words(b)
-        r23 = operand("r23", HALF)
-        quantise(*r23, late[:], E4M3)
-        nc.scalar.copy(out=spill[:, J - PIECE:], in_=banks[6][:, PIECE:])
-        scatter(3, PIECE, HALF, spill[:, J - PIECE:])
-
-        dx23 = [sbuf("dx23_%d" % t, [P, HALF], F32) for t in range(PACK)]
-        for s, bank in enumerate((banks[4], banks[2])):
-            product(bank[:, 0:PIECE], 0, cols(q23, s * PIECE, (s + 1) * PIECE), cols(r23, s * PIECE, (s + 1) * PIECE))
-            nc.scalar.copy(out=dx23[0][:, s * PIECE:(s + 1) * PIECE], in_=bank[:, 0:PIECE])
-        for t, bank in ((1, banks[0]), (2, banks[1]), (3, banks[7])):
-            product(bank[:], t, q23, r23)
-            nc.scalar.copy(out=dx23[t][:], in_=bank[:])
+        add_up(3)
+        add_up(4)
+        rounded57 = sbuf("rounded57", [P, 3 * BLOCK, PACK], BF16, tag="dx00")
+        for s in range(3):
+            round_block(run_of(rounded57[:], s, s + 1), 5 + s)
+        issue(early[2])
+        issue(early[3])
+        quantise(blocks(q_late, 2, 3), run_of(rounded57[:], 0, 1), E5M2)
+        quantise(blocks(q_late, 3, 5), run_of(rounded57[:], 1, 3), E5M2)
+        clear(3, "dx00")
+        scatter(2, 0, 3 * BLOCK, empty("dx2a", banks[6][:, 0:3 * BLOCK], 3 * BLOCK, tag="minus3")[:])
+        for b in (3, 4):
+            round_sums(b, sum_banks[b])
+        for b in (3, 4):
+            lay_words(left_late[:], b - 3, sum_banks[b])
+        quantise(blocks(r_late, 0, 2), run_of(left_late[:], 0, 2), E4M3)
+        scatter(3, 0, 3 * BLOCK, empty("dx3a", banks[7][:, 0:3 * BLOCK], 3 * BLOCK, tag="turned4")[:])
+        for b in (5, 6, 7):
+            back(b)
+        issue(product(banks[2], 0, [q2, blocks(q_late, 0, 2)], [blocks(r012, 2, 3), blocks(r_late, 0, 2)]))
+        add_up(5)
+        add_up(6)
+        scatter(0, 2 * BLOCK, 5 * BLOCK, empty("dx0b", banks[2][:, 0:3 * BLOCK], 3 * BLOCK, tag="minus5")[:])
+        add_up(7)
+        for b in (5, 6, 7):
+            round_sums(b, sum_banks[b])
+        for b in (5, 6, 7):
+            lay_words(left_late[:], b - 3, sum_banks[b])
+        issue(product(banks[1], 1, [blocks(q_late, 0, 2)], [blocks(r_late, 0, 2)]))
+        for t in (2, 3):
+            issue(product(banks[6][:, (t - 2) * 2 * BLOCK:], t, [blocks(q_late, 0, 2)], [blocks(r_late, 0, 2)]))
+        quantise(blocks(r_late, 2, 5), run_of(left_late[:], 2, 5), E4M3)
+        scatter(1, 3 * BLOCK, 5 * BLOCK, empty("dx1b", banks[1][:, 0:2 * BLOCK], 2 * BLOCK, tag="turned7")[:])
+        dx_late = sbuf("dx_late", [P, 2, 5 * BLOCK], F32, tag="turned6")
+        nc.scalar.copy(out=dx_late[:, :, 0:2 * BLOCK], in_=banks[6][:].rearrange("p (t j) -> p t j", t=2))
+        last = [blocks(q_late, 2, 4), blocks(q_late, 4, 5)], [blocks(r_late, 2, 4), blocks(r_late, 4, 5)]
+        late = {}
+        for t, bank in enumerate((banks[3], banks[4], banks[7], banks[0])):
+            issue(product(bank, t, last[0], last[1], t > 0))
+            if t < 2:
+                late[t] = (5 * BLOCK, empty("dx%dc" % t, bank[:, 0:3 * BLOCK], 3 * BLOCK)[:])
+            else:
+                nc.scalar.copy(out=dx_late[:, t - 2, 2 * BLOCK:], in_=bank[:, 0:3 * BLOCK])
+                late[t] = (3 * BLOCK, dx_late[:, t - 2, :])
 
         out_planes = out_0.rearrange("(p t) c -> p t c", t=PACK)
         shares = ((0, LAST_ON_VECTOR), (LAST_ON_VECTOR, T))
-        pairs = [sbuf("pairs%d" % i, [P, PACK * (hi - lo)], BF16, tag=tag) for (i, (lo, hi)), tag in zip(enumerate(shares), ("r23_codes", "late"))]
+        pairs = [sbuf("pairs%d" % i, [P, PACK * (hi - lo)], BF16, tag=tag) for (i, (lo, hi)), tag in zip(enumerate(shares), ("r_late_codes", "left_late"))]
 
         def pair_view(i):
             return pairs[i][:].rearrange("p (u c e) -> p u c e", u=2, e=2)
 
         for t in range(PACK):
-            scatter(t, HALF, J, dx23[t][:])
+            scatter(t, late[t][0], J, late[t][1])
             nc.sync.dma_start(out=out_planes[:, t, :], in_=pages[t][:])
             u, e = divmod(t, 2)
             for i, (lo, hi) in enumerate(shares):
@@ -300,18 +316,17 @@ def tile_list_embg_tgq8_noneP_kernel(tc, dy, w_words, w_scales, wgo, offs, out_0
             copy = nc.vector.tensor_copy if on_vector else nc.scalar.copy
             copy(out=dst.rearrange("p (c i u) -> p c u i", i=PACK, u=2), in_=src.rearrange("p u (c i) -> p c u i", i=PACK))
 
-        weave_words(0, CHUNK, True)
-        weave_words(CHUNK, 2 * CHUNK, True)
-        weave_words(2 * CHUNK, 3 * CHUNK, False)
-        weave_words(3 * CHUNK, T - LAST_WORDS_ON_VECTOR, False)
-        weave_words(T - LAST_WORDS_ON_VECTOR, T, True)
-        for c in range(T // CHUNK):
-            columns = slice(c * CHUNK, (c + 1) * CHUNK)
-            shift, side = divmod(c, 2)
-            y_codes = sbuf("y_codes%d" % c, [P, CHUNK], U32)
-            nc.vector.quantize_mx(out=y_codes[:].bitcast(E4M3), scales=y_scales[4 * shift:, side * CHUNK:(side + 1) * CHUNK],
-                                  in_=grouped[c][:])
-            nc.sync.dma_start(out=words_out[:, columns], in_=y_codes[:].bitcast(I32))
+        cuts = (0, CHUNK, 2 * CHUNK, 3 * CHUNK, T - LAST_CHUNK, T)
+        for lo, hi in zip(cuts, cuts[1:]):
+            weave_words(lo, hi, hi <= LAST_ON_VECTOR)
+        for lo, hi in zip(cuts, cuts[1:]):
+            c, at = divmod(lo, CHUNK)
+            shift, column = divmod(lo, T // 2)
+            y_codes = sbuf("y_codes%d" % lo, [P, hi - lo], U32)
+            nc.vector.quantize_mx(out=y_codes[:].bitcast(E4M3), scales=y_scales[4 * shift:, column:column + hi - lo],
+                                  in_=grouped[c][:, PACK * at:PACK * (at + hi - lo)])
+            nc.sync.dma_start(out=words_out[:, lo:hi], in_=y_codes[:].bitcast(I32))
         for q in range(QUADS):
-            nc.scalar.dma_start(out=out_2[0, 4 * q:4 * q + 4, :].bitcast(I32).rearrange("r (u x) -> u r x", u=2),
-                                in_=y_scales[32 * q:32 * q + 8, :].bitcast(I32))
+            queue = nc.scalar if q < 2 else nc.sync
+            queue.dma_start(out=out_2[0, 4 * q:4 * q + 4, :].bitcast(I32).rearrange("r (u x) -> u r x", u=2),
+                            in_=y_scales[32 * q:32 * q + 8, :].bitcast(I32))

@@ -221,8 +221,11 @@ def tile_list_embg_tgq8_noneP_kernel(tc, dy, w_words, w_scales, wgo, offs, out_0
         q_late = operand("q_late", 5 * BLOCK)
         quantise(blocks(q_late, 0, 2), rounded34[:], E5M2)
         quantise(blocks(r012, 2, 3), left2[:], E4M3)
-        clear(2, "eye_base")
         scatter(0, 0, 2 * BLOCK, dx00[:])
+        rounded5 = sbuf("rounded5", [P, BLOCK, PACK], BF16, tag="left01")
+        round_block(rounded5[:], 5)
+        quantise(blocks(q_late, 2, 3), rounded5[:], E5M2)
+        clear(2, "left01")
         issue(early[1])
         scatter(1, 0, 3 * BLOCK, empty("dx1a", banks[1][:, 0:3 * BLOCK], 3 * BLOCK)[:])
 
@@ -241,31 +244,33 @@ def tile_list_embg_tgq8_noneP_kernel(tc, dy, w_words, w_scales, wgo, offs, out_0
         back(4)
         add_up(3)
         add_up(4)
-        rounded57 = sbuf("rounded57", [P, 3 * BLOCK, PACK], BF16, tag="dx00")
-        for s in range(3):
-            round_block(run_of(rounded57[:], s, s + 1), 5 + s)
+        rounded67 = sbuf("rounded67", [P, 2 * BLOCK, PACK], BF16, tag="dx00")
+        for s in range(2):
+            round_block(run_of(rounded67[:], s, s + 1), 6 + s)
         issue(early[2])
-        issue(early[3])
-        quantise(blocks(q_late, 2, 3), run_of(rounded57[:], 0, 1), E5M2)
-        quantise(blocks(q_late, 3, 5), run_of(rounded57[:], 1, 3), E5M2)
+        back(5)
+        quantise(blocks(q_late, 3, 5), rounded67[:], E5M2)
         clear(3, "dx00")
         scatter(2, 0, 3 * BLOCK, empty("dx2a", banks[6][:, 0:3 * BLOCK], 3 * BLOCK, tag="minus3")[:])
-        for b in (3, 4):
-            round_sums(b, sum_banks[b])
-        for b in (3, 4):
-            lay_words(left_late[:], b - 3, sum_banks[b])
+        round_sums(3, sum_banks[3])
+        add_up(5)
+        issue(early[3])
+        round_sums(4, sum_banks[4])
+        lay_words(left_late[:], 0, sum_banks[3])
+        lay_words(left_late[:], 1, sum_banks[4])
         quantise(blocks(r_late, 0, 2), run_of(left_late[:], 0, 2), E4M3)
         scatter(3, 0, 3 * BLOCK, empty("dx3a", banks[7][:, 0:3 * BLOCK], 3 * BLOCK, tag="turned4")[:])
-        for b in (5, 6, 7):
+        round_sums(5, sum_banks[5])
+        for b in (6, 7):
             back(b)
-        issue(product(banks[2], 0, [q2, blocks(q_late, 0, 2)], [blocks(r012, 2, 3), blocks(r_late, 0, 2)]))
-        add_up(5)
         add_up(6)
-        scatter(0, 2 * BLOCK, 5 * BLOCK, empty("dx0b", banks[2][:, 0:3 * BLOCK], 3 * BLOCK, tag="minus5")[:])
+        issue(product(banks[2], 0, [q2, blocks(q_late, 0, 2)], [blocks(r012, 2, 3), blocks(r_late, 0, 2)]))
+        scatter(0, 2 * BLOCK, 5 * BLOCK, empty("dx0b", banks[2][:, 0:3 * BLOCK], 3 * BLOCK, tag="turned5")[:])
         add_up(7)
-        for b in (5, 6, 7):
+        lay_words(left_late[:], 2, sum_banks[5])
+        for b in (6, 7):
             round_sums(b, sum_banks[b])
-        for b in (5, 6, 7):
+        for b in (6, 7):
             lay_words(left_late[:], b - 3, sum_banks[b])
         issue(product(banks[1], 1, [blocks(q_late, 0, 2)], [blocks(r_late, 0, 2)]))
         for t in (2, 3):
@@ -297,10 +302,14 @@ def tile_list_embg_tgq8_noneP_kernel(tc, dy, w_words, w_scales, wgo, offs, out_0
             u, e = divmod(t, 2)
             for i, (lo, hi) in enumerate(shares):
                 if t == PACK - 1 and i == 0:
-                    nc.vector.tensor_copy(out=pair_view(i)[:, u, :, e], in_=pages[t][:, lo:hi])
+                    for at in range(lo, hi, CHUNK):
+                        nc.vector.tensor_copy(out=pair_view(i)[:, u, at:at + CHUNK, e], in_=pages[t][:, at:at + CHUNK])
                 elif t == PACK - 2 and i == 0:
-                    nc.scalar.copy(out=pair_view(i)[:, u, 0:hi - SEAM, e], in_=pages[t][:, 0:hi - SEAM])
-                    nc.scalar.copy(out=pair_view(i)[:, u, hi - SEAM:hi, :], in_=pages[t][:, hi - SEAM:hi].unsqueeze(2).to_broadcast([P, SEAM, 2]))
+                    by_chunk = pair_view(i)[:, u].rearrange("p (k c) e -> p k c e", c=CHUNK)
+                    source = pages[t][:, lo:hi].rearrange("p (k c) -> p k c", c=CHUNK)
+                    nc.scalar.copy(out=by_chunk[:, :, 0:CHUNK - SEAM, e], in_=source[:, :, 0:CHUNK - SEAM])
+                    nc.scalar.copy(out=by_chunk[:, :, CHUNK - SEAM:, :],
+                                   in_=source[:, :, CHUNK - SEAM:].unsqueeze(3).to_broadcast([P, (hi - lo) // CHUNK, SEAM, 2]))
                 else:
                     nc.scalar.copy(out=pair_view(i)[:, u, :, e], in_=pages[t][:, lo:hi])
 

@@ -62,11 +62,11 @@ def tile_list_embg_tgq8_noneP_kernel(tc, dy, w_words, w_scales, wgo, offs, out_0
             nc.sync.dma_start(out=raw[c][:], in_=dy_planes[:, :, spans[c][0] * BLOCK:spans[c][1] * BLOCK])
 
         ws_in = sbuf("ws_in", [P, N], U8)
-        nc.gpsimd.memset(ws_in[:].bitcast(I32), 0)
         load_piece(0)
         load_piece(1)
         for q in range(QUADS):
-            nc.sync.dma_start(out=ws_in[32 * q:32 * q + 4, :].bitcast(I32), in_=w_scales[0, 4 * q:4 * q + 4, :].bitcast(I32))
+            nc.sync.dma_start(out=ws_in[32 * q:32 * q + 32, :].bitcast(I32),
+                              in_=w_scales[0, 4 * q:4 * q + 4, :].bitcast(I32).unsqueeze(0).to_broadcast([8, 4, N // 4]))
         load_piece(2)
         w_in = sbuf("w_in", [P, N], I32)
         nc.sync.dma_start(out=w_in[:], in_=w_words[0].rearrange("p n i -> p (n i)").bitcast(I32))

@@ -30,6 +30,8 @@ LAST_ON_VECTOR = 1024
 SEAM = 16
 LAST_CHUNK = 256
 EARLY = 3 * BLOCK
+AHEAD_OF_IDENTITY = 1408
+CLEARED_BY_VECTOR = 1792
 
 
 def woven(tile3, run=PACK):
@@ -78,19 +80,20 @@ def tile_list_embg_tgq8_noneP_kernel(tc, dy, w_words, w_scales, wgo, offs, out_0
         load_piece(4)
         nc.sync.dma_start(out=gain[:, EARLY:], in_=wgo[:, EARLY:])
 
-        ones = sbuf("ones", [P, P], F32, tag="page0")
-        nc.gpsimd.memset(ones[:], 1.0)
-        eye = sbuf("eye", [P, P], F32)
-        nc.gpsimd.affine_select(out=eye[:], in_=ones[:], pattern=[[-1, P]], compare_op=mybir.AluOpType.is_equal, fill=0.0, base=0, channel_multiplier=1)
-        eye_in = sbuf("eye_in", [P, P, PACK], BF16)
-        nc.scalar.copy(out=eye_in[:], in_=eye[:].unsqueeze(2).to_broadcast([P, P, PACK]))
         row = P * PACK
         eye_codes = sbuf("eye_codes", [P, PACK * row + PAD], U8)
         nc.vector.memset(eye_codes[:].bitcast(I32), 0)
         pages = {0: sbuf("page0", [P, T], F32), 1: sbuf("page1", [P, T], F32)}
-        nc.vector.memset(pages[1][:, 0:T // 2 - 1].bitcast(I32), 0)
-        nc.vector.memset(pages[1][:, T // 2 - 1:].bitcast(I32), 0)
-        nc.gpsimd.memset(pages[0][:], 0.0)
+        nc.gpsimd.memset(pages[0][:, 0:AHEAD_OF_IDENTITY], 0.0)
+        eye = sbuf("eye", [P, P], F32)
+        nc.gpsimd.affine_select(out=eye[:], in_=eye_codes[:, 0:row].bitcast(F32), pattern=[[-1, P]], compare_op=mybir.AluOpType.not_equal,
+                                fill=1.0, base=0, channel_multiplier=1)
+        eye_in = sbuf("eye_in", [P, P, PACK], BF16)
+        nc.scalar.copy(out=eye_in[:], in_=eye[:].unsqueeze(2).to_broadcast([P, P, PACK]))
+        nc.vector.memset(pages[1][:, 0:CLEARED_BY_VECTOR // 2 - 1].bitcast(I32), 0)
+        nc.vector.memset(pages[1][:, CLEARED_BY_VECTOR // 2 - 1:CLEARED_BY_VECTOR].bitcast(I32), 0)
+        nc.gpsimd.memset(pages[0][:, AHEAD_OF_IDENTITY:], 0.0)
+        nc.gpsimd.memset(pages[1][:, CLEARED_BY_VECTOR:], 0.0)
         eye_base = sbuf("eye_base", [P, P, PACK], U8)
         eye_scales = sbuf("eye_scales", [P, P], U8)
         nc.vector.quantize_mx(out=flat(eye_base[:]).bitcast(E4M3), scales=eye_scales[:], in_=flat(eye_in[:]))

@@ -201,9 +201,8 @@ def tile_list_embg_tgq8_noneP_kernel(tc, dy, w_words, w_scales, wgo, offs, out_0
         round_block(rounded2[:], 2)
         w_codes = sbuf("w_codes", [P, PACK, P], U32, tag="ws_in")
         nc.scalar.copy(out=planar(w_codes[:]), in_=woven(w_in[:].bitcast(U32).rearrange("p (m t) -> p m t", t=PACK)))
-        rounded34 = sbuf("rounded34", [P, 2 * BLOCK, PACK], BF16, tag="eye_base")
-        for s in range(2):
-            round_block(run_of(rounded34[:], s, s + 1), 3 + s)
+        rounded3 = sbuf("rounded3", [P, BLOCK, PACK], BF16, tag="eye_base")
+        round_block(rounded3[:], 3)
 
         left01 = sbuf("left01", [P, 2 * BLOCK, PACK], BF16)
         r012 = operand("r012", 3 * BLOCK)
@@ -219,11 +218,15 @@ def tile_list_embg_tgq8_noneP_kernel(tc, dy, w_words, w_scales, wgo, offs, out_0
         early = {t: product(bank, t, [q01, q2], [blocks(r012, 0, 2), blocks(r012, 2, 3)], t > 1) for t, bank in ((1, banks[1]), (2, banks[6]), (3, banks[7]))}
         issue(opening)
         dx00 = empty("dx00", banks[4][:, 0:2 * BLOCK], 2 * BLOCK)
-        left2 = sbuf("left2", [P, BLOCK, PACK], BF16, tag="left01")
-        subtract(left2[:], 2)
-        q_late = operand("q_late", 5 * BLOCK)
-        quantise(blocks(q_late, 0, 2), rounded34[:], E5M2)
-        quantise(blocks(r012, 2, 3), left2[:], E4M3)
+        staged = sbuf("staged", [P, 2 * BLOCK, PACK], BF16, tag="left01")
+        left2, rounded4 = run_of(staged[:], 0, 1), run_of(staged[:], 1, 2)
+        subtract(left2, 2)
+        nc.vector.tensor_copy(out=woven(rounded4[:, 0:BLOCK // 2, :]), in_=planar(raw_block(4)[:, :, 0:BLOCK // 2]))
+        nc.scalar.copy(out=woven(rounded4[:, BLOCK // 2:, :]), in_=planar(raw_block(4)[:, :, BLOCK // 2:]))
+        quantise(blocks(r012, 2, 3), left2, E4M3)
+        q_late = operand("q_late", 5 * BLOCK, tag="raw1")
+        quantise(blocks(q_late, 0, 1), rounded3[:], E5M2)
+        quantise(blocks(q_late, 1, 2), rounded4, E5M2)
         scatter(0, 0, 2 * BLOCK, dx00[:])
         rounded5 = sbuf("rounded5", [P, BLOCK, PACK], BF16, tag="left01")
         round_block(rounded5[:], 5)

@@ -57,7 +57,7 @@ def tile_list_embg_tgq8_noneP_kernel(tc, dy, w_words, w_scales, wgo, offs, out_0
             return sb.tile(shape, dtype, name=name, tag=tag or name, align_bytes=64)
 
         dy_planes = dy.rearrange("(p t) j -> p t j", t=PACK)
-        spans = ((0, 1), (1, 2), (2, 4), (4, 6), (6, 8))
+        spans = ((0, 1), (1, 2), (2, 3), (3, 5), (5, 8))
         raw = [sbuf("raw%d" % lo, [P, PACK, (hi - lo) * BLOCK], F32) for lo, hi in spans]
 
         def load_piece(c):
@@ -66,10 +66,10 @@ def tile_list_embg_tgq8_noneP_kernel(tc, dy, w_words, w_scales, wgo, offs, out_0
         ws_in = sbuf("ws_in", [P, N], U8)
         load_piece(0)
         load_piece(1)
+        load_piece(2)
         for q in range(QUADS):
             nc.sync.dma_start(out=ws_in[32 * q:32 * q + 32, :].bitcast(I32),
                               in_=w_scales[0, 4 * q:4 * q + 4, :].bitcast(I32).unsqueeze(0).to_broadcast([8, 4, N // 4]))
-        load_piece(2)
         w_in = sbuf("w_in", [P, N], I32)
         nc.sync.dma_start(out=w_in[:], in_=w_words[0].rearrange("p n i -> p (n i)").bitcast(I32))
         load_piece(3)

@@ -64,8 +64,9 @@ def tile_list_embg_tgq8_noneP_kernel(tc, dy, w_words, w_scales, wgo, offs, out_0
             nc.sync.dma_start(out=raw[c][:], in_=dy_planes[:, :, spans[c][0] * BLOCK:spans[c][1] * BLOCK])
 
         ws_in = sbuf("ws_in", [P, N], U8)
-        load_piece(0)
-        load_piece(1)
+        for b in range(2):
+            for queue, rows in ((nc.sync, slice(0, 2)), (nc.scalar, slice(2, 4))):
+                queue.dma_start(out=raw[b][:, rows, :], in_=dy_planes[:, rows, b * BLOCK:(b + 1) * BLOCK])
         load_piece(2)
         for q in range(QUADS):
             nc.sync.dma_start(out=ws_in[32 * q:32 * q + 32, :].bitcast(I32),

@@ -25,6 +25,7 @@ PIECE = 256
 BLOCK = 128
 CHUNK = 512
 PAD = 68
+TWO_ONES = 1.0 + 16256.0 / 8388608.0
 
 LAST_ON_VECTOR = 1024
 SEAM = 16
@@ -86,11 +87,13 @@ def tile_list_embg_tgq8_noneP_kernel(tc, dy, w_words, w_scales, wgo, offs, out_0
         nc.vector.memset(eye_codes[:].bitcast(I32), 0)
         pages = {0: sbuf("page0", [P, T], F32), 1: sbuf("page1", [P, T], F32)}
         nc.gpsimd.memset(pages[0][:, 0:AHEAD_OF_IDENTITY], 0.0)
-        eye = sbuf("eye", [P, P], F32)
-        nc.gpsimd.affine_select(out=eye[:], in_=eye_codes[:, 0:row].bitcast(F32), pattern=[[-1, P]], compare_op=mybir.AluOpType.not_equal,
-                                fill=1.0, base=0, channel_multiplier=1)
+        eye_pairs = sbuf("eye_pairs", [P, P], F32)
+        nc.gpsimd.affine_select(out=eye_pairs[:], in_=eye_codes[:, 0:row].bitcast(F32), pattern=[[-1, P]], compare_op=mybir.AluOpType.not_equal,
+                                fill=TWO_ONES, base=0, channel_multiplier=1)
         eye_in = sbuf("eye_in", [P, P, PACK], BF16)
-        nc.scalar.copy(out=eye_in[:], in_=eye[:].unsqueeze(2).to_broadcast([P, P, PACK]))
+        nc.scalar.copy(out=eye_in[:].bitcast(F32), in_=eye_pairs[:].unsqueeze(2).to_broadcast([P, P, 2]))
+        eye = sbuf("eye", [P, P], F32)
+        nc.scalar.copy(out=eye[:], in_=eye_pairs[:].bitcast(BF16).rearrange("p (m e) -> p m e", e=2)[:, :, 0])
         nc.vector.memset(pages[1][:, 0:CLEARED_BY_VECTOR // 2 - 1].bitcast(I32), 0)
         nc.vector.memset(pages[1][:, CLEARED_BY_VECTOR // 2 - 1:CLEARED_BY_VECTOR].bitcast(I32), 0)
         nc.gpsimd.memset(pages[0][:, AHEAD_OF_IDENTITY:], 0.0)

@@ -148,20 +148,20 @@ def tile_list_embg_tgq8_noneP_kernel(tc, dy, w_words, w_scales, wgo, offs, out_0
                                  start=(first and t == 0), stop=(not first and t == PACK - 1))
 
         def negate(b, bank):
-            minus = sbuf("minus%d" % b, [P, PACK, BLOCK], F32)
+            minus = sbuf("minus%d" % b, [P, PACK, BLOCK], F32, tag="turned5" if b == 7 else None)
             nc.scalar.mul(flat(minus[:]), bank[:], -1.0)
             return minus
 
-        def round_sums(b, bank):
+        def round_sums(b, bank, into):
             turned = sbuf("turned%d" % b, [P, 2 * P], F32)
             nc.scalar.copy(out=turned[:].bitcast(BF16).rearrange("p (u m e) -> p u m e", u=2, e=2),
                            in_=bank[:].rearrange("p (u e m) -> p u m e", u=2, e=2))
             for u in range(2):
-                nc.tensor.transpose(bank[:, u * P:(u + 1) * P], turned[:, u * P:(u + 1) * P], eye[:])
+                nc.tensor.transpose(into[:, u * P:(u + 1) * P], turned[:, u * P:(u + 1) * P], eye[:])
 
-        def lay_words(left, s, bank):
-            nc.scalar.copy(out=flat(block_of(left, s)).bitcast(F32).rearrange("p (j u) -> p j u", u=2),
-                           in_=bank[:, 0:2 * P].rearrange("p (u j) -> p j u", u=2))
+        def lay_words(left, lo, hi, bank):
+            nc.scalar.copy(out=flat(left[:, lo * BLOCK:hi * BLOCK, :]).bitcast(F32).rearrange("p (s j u) -> p s j u", j=BLOCK, u=2),
+                           in_=bank[:, 0:(hi - lo) * 2 * P].rearrange("p (s u j) -> p s j u", j=BLOCK, u=2))
 
         def subtract(out, b):
             nc.vector.tensor_tensor(woven(out, 2), planar(raw_block(b), 2),
@@ -239,8 +239,8 @@ def tile_list_embg_tgq8_noneP_kernel(tc, dy, w_words, w_scales, wgo, offs, out_0
         issue(early[1])
         scatter(1, 0, 3 * BLOCK, empty("dx1a", banks[1][:, 0:3 * BLOCK], 3 * BLOCK)[:])
 
-        back_banks = {3: banks[3], 4: banks[0], 5: banks[5], 6: banks[3], 7: banks[0]}
-        sum_banks = {3: banks[2], 4: banks[4], 5: banks[1], 6: banks[6], 7: banks[5]}
+        back_banks = {3: banks[3], 4: banks[0], 5: banks[5], 6: banks[4], 7: banks[5]}
+        sum_banks = {3: banks[2], 4: banks[4], 5: banks[1], 6: banks[6], 7: banks[3]}
         left_late = sbuf("left_late", [P, 5 * BLOCK, PACK], BF16)
 
         def back(b):
@@ -255,33 +255,30 @@ def tile_list_embg_tgq8_noneP_kernel(tc, dy, w_words, w_scales, wgo, offs, out_0
         add_up(3)
         add_up(4)
         rounded67 = sbuf("rounded67", [P, 2 * BLOCK, PACK], BF16, tag="dx00")
-        for s in range(2):
-            round_block(run_of(rounded67[:], s, s + 1), 6 + s)
+        nc.scalar.copy(out=woven(rounded67[:]), in_=planar(raw[4][:, :, BLOCK:]))
         issue(early[2])
         back(5)
+        issue(early[3])
         quantise(blocks(q_late, 3, 5), rounded67[:], E5M2)
         clear(3, "dx00")
         scatter(2, 0, 3 * BLOCK, empty("dx2a", banks[6][:, 0:3 * BLOCK], 3 * BLOCK, tag="minus3")[:])
-        round_sums(3, sum_banks[3])
+        round_sums(3, sum_banks[3], sum_banks[3])
+        round_sums(4, sum_banks[4], sum_banks[3][:, 2 * P:])
+        back(6)
         add_up(5)
-        issue(early[3])
-        round_sums(4, sum_banks[4])
-        lay_words(left_late[:], 0, sum_banks[3])
-        lay_words(left_late[:], 1, sum_banks[4])
+        back(7)
+        lay_words(left_late[:], 0, 2, sum_banks[3])
         quantise(blocks(r_late, 0, 2), run_of(left_late[:], 0, 2), E4M3)
         scatter(3, 0, 3 * BLOCK, empty("dx3a", banks[7][:, 0:3 * BLOCK], 3 * BLOCK, tag="turned4")[:])
-        round_sums(5, sum_banks[5])
-        for b in (6, 7):
-            back(b)
+        round_sums(5, sum_banks[5], sum_banks[5])
         add_up(6)
         issue(product(banks[2], 0, [q2, blocks(q_late, 0, 2)], [blocks(r012, 2, 3), blocks(r_late, 0, 2)]))
-        scatter(0, 2 * BLOCK, 5 * BLOCK, empty("dx0b", banks[2][:, 0:3 * BLOCK], 3 * BLOCK, tag="turned5")[:])
+        scatter(0, 2 * BLOCK, 5 * BLOCK, empty("dx0b", banks[2][:, 0:3 * BLOCK], 3 * BLOCK)[:])
         add_up(7)
-        lay_words(left_late[:], 2, sum_banks[5])
+        lay_words(left_late[:], 2, 3, sum_banks[5])
         for b in (6, 7):
-            round_sums(b, sum_banks[b])
-        for b in (6, 7):
-            lay_words(left_late[:], b - 3, sum_banks[b])
+            round_sums(b, sum_banks[b], sum_banks[6][:, (b - 6) * 2 * P:])
+        lay_words(left_late[:], 3, 5, sum_banks[6])
         issue(product(banks[1], 1, [blocks(q_late, 0, 2)], [blocks(r_late, 0, 2)]))
         for t in (2, 3):
             issue(product(banks[6][:, (t - 2) * 2 * BLOCK:], t, [blocks(q_late, 0, 2)], [blocks(r_late, 0, 2)]))
@@ -324,7 +321,7 @@ def tile_list_embg_tgq8_noneP_kernel(tc, dy, w_words, w_scales, wgo, offs, out_0
                     nc.scalar.copy(out=pair_view(i)[:, u, :, e], in_=pages[t][:, lo:hi])
 
         words_out = out_1[0].rearrange("p c i -> p (c i)").bitcast(I32)
-        y_scales = sbuf("y_scales", [P, T // 2], U8)
+        y_scales = sbuf("y_scales", [P, CHUNK], U8)
         grouped = [sbuf("grouped%d" % c, [P, CHUNK * PACK], BF16) for c in range(T // CHUNK)]
 
         def weave_words(lo, hi, on_vector):
@@ -339,13 +336,13 @@ def tile_list_embg_tgq8_noneP_kernel(tc, dy, w_words, w_scales, wgo, offs, out_0
         for lo, hi in zip(cuts, cuts[1:]):
             weave_words(lo, hi, hi <= LAST_ON_VECTOR)
         for lo, hi in zip(cuts, cuts[1:]):
-            c, at = divmod(lo, CHUNK)
-            shift, column = divmod(lo, T // 2)
             y_codes = sbuf("y_codes%d" % lo, [P, hi - lo], U32)
-            nc.vector.quantize_mx(out=y_codes[:].bitcast(E4M3), scales=y_scales[4 * shift:, column:column + hi - lo],
-                                  in_=grouped[c][:, PACK * at:PACK * (at + hi - lo)])
+            for part in range(lo, hi, LAST_CHUNK):
+                c, at = divmod(part, CHUNK)
+                nc.vector.quantize_mx(out=y_codes[:, part - lo:part - lo + LAST_CHUNK].bitcast(E4M3), scales=y_scales[4 * c:, at:at + LAST_CHUNK],
+                                      in_=grouped[c][:, PACK * at:PACK * (at + LAST_CHUNK)])
             nc.sync.dma_start(out=words_out[:, lo:hi], in_=y_codes[:].bitcast(I32))
         for q in range(QUADS):
             queue = nc.scalar if q < 2 else nc.sync
-            queue.dma_start(out=out_2[0, 4 * q:4 * q + 4, :].bitcast(I32).rearrange("r (u x) -> u r x", u=2),
-                            in_=y_scales[32 * q:32 * q + 8, :].bitcast(I32))
+            queue.dma_start(out=out_2[0, 4 * q:4 * q + 4, :].bitcast(I32).rearrange("r (u x) -> u r x", u=4),
+                            in_=y_scales[32 * q:32 * q + 16, :].bitcast(I32))

@@ -58,7 +58,7 @@ def tile_list_embg_tgq8_noneP_kernel(tc, dy, w_words, w_scales, wgo, offs, out_0
             return sb.tile(shape, dtype, name=name, tag=tag or name, align_bytes=64)
 
         dy_planes = dy.rearrange("(p t) j -> p t j", t=PACK)
-        spans = ((0, 1), (1, 2), (2, 3), (3, 5), (5, 8))
+        spans = ((0, 1), (1, 2), (2, 3), (3, 5), (5, 6), (6, 8))
         raw = [sbuf("raw%d" % lo, [P, PACK, (hi - lo) * BLOCK], F32) for lo, hi in spans]
 
         def load_piece(c):
@@ -80,6 +80,7 @@ def tile_list_embg_tgq8_noneP_kernel(tc, dy, w_words, w_scales, wgo, offs, out_0
         gain = sbuf("gain", [P, J], F32)
         nc.sync.dma_start(out=gain[:, 0:EARLY], in_=wgo[:, 0:EARLY])
         load_piece(4)
+        load_piece(5)
         nc.sync.dma_start(out=gain[:, EARLY:], in_=wgo[:, EARLY:])
 
         row = P * PACK
@@ -255,7 +256,7 @@ def tile_list_embg_tgq8_noneP_kernel(tc, dy, w_words, w_scales, wgo, offs, out_0
         add_up(3)
         add_up(4)
         rounded67 = sbuf("rounded67", [P, 2 * BLOCK, PACK], BF16, tag="dx00")
-        nc.scalar.copy(out=woven(rounded67[:]), in_=planar(raw[4][:, :, BLOCK:]))
+        nc.scalar.copy(out=woven(rounded67[:]), in_=planar(raw[5][:]))
         issue(early[2])
         back(5)
         issue(early[3])

@@ -58,7 +58,7 @@ def tile_list_embg_tgq8_noneP_kernel(tc, dy, w_words, w_scales, wgo, offs, out_0
             return sb.tile(shape, dtype, name=name, tag=tag or name, align_bytes=64)
 
         dy_planes = dy.rearrange("(p t) j -> p t j", t=PACK)
-        spans = ((0, 1), (1, 2), (2, 3), (3, 5), (5, 6), (6, 8))
+        spans = ((0, 1), (1, 2), (2, 3), (3, 5), (5, 8))
         raw = [sbuf("raw%d" % lo, [P, PACK, (hi - lo) * BLOCK], F32) for lo, hi in spans]
 
         def load_piece(c):
@@ -80,7 +80,6 @@ def tile_list_embg_tgq8_noneP_kernel(tc, dy, w_words, w_scales, wgo, offs, out_0
         gain = sbuf("gain", [P, J], F32)
         nc.sync.dma_start(out=gain[:, 0:EARLY], in_=wgo[:, 0:EARLY])
         load_piece(4)
-        load_piece(5)
         nc.sync.dma_start(out=gain[:, EARLY:], in_=wgo[:, EARLY:])
 
         row = P * PACK
@@ -206,8 +205,6 @@ def tile_list_embg_tgq8_noneP_kernel(tc, dy, w_words, w_scales, wgo, offs, out_0
         round_block(rounded2[:], 2)
         w_codes = sbuf("w_codes", [P, PACK, P], U32, tag="ws_in")
         nc.scalar.copy(out=planar(w_codes[:]), in_=woven(w_in[:].bitcast(U32).rearrange("p (m t) -> p m t", t=PACK)))
-        rounded3 = sbuf("rounded3", [P, BLOCK, PACK], BF16, tag="eye_base")
-        round_block(rounded3[:], 3)
 
         left01 = sbuf("left01", [P, 2 * BLOCK, PACK], BF16)
         r012 = operand("r012", 3 * BLOCK)
@@ -223,15 +220,14 @@ def tile_list_embg_tgq8_noneP_kernel(tc, dy, w_words, w_scales, wgo, offs, out_0
         early = {t: product(bank, t, [q01, q2], [blocks(r012, 0, 2), blocks(r012, 2, 3)], t > 1) for t, bank in ((1, banks[1]), (2, banks[6]), (3, banks[7]))}
         issue(opening)
         dx00 = empty("dx00", banks[4][:, 0:2 * BLOCK], 2 * BLOCK)
-        staged = sbuf("staged", [P, 2 * BLOCK, PACK], BF16, tag="left01")
-        left2, rounded4 = run_of(staged[:], 0, 1), run_of(staged[:], 1, 2)
+        staged = sbuf("staged", [P, 3 * BLOCK, PACK], BF16, tag="left01")
+        left2, rounded34 = run_of(staged[:], 0, 1), run_of(staged[:], 1, 3)
         subtract(left2, 2)
-        nc.vector.tensor_copy(out=woven(rounded4[:, 0:BLOCK // 2, :]), in_=planar(raw_block(4)[:, :, 0:BLOCK // 2]))
-        nc.scalar.copy(out=woven(rounded4[:, BLOCK // 2:, :]), in_=planar(raw_block(4)[:, :, BLOCK // 2:]))
+        nc.vector.tensor_copy(out=woven(rounded34[:, 0:3 * BLOCK // 2, :]), in_=planar(raw[3][:, :, 0:3 * BLOCK // 2]))
+        nc.scalar.copy(out=woven(rounded34[:, 3 * BLOCK // 2:, :]), in_=planar(raw[3][:, :, 3 * BLOCK // 2:]))
         quantise(blocks(r012, 2, 3), left2, E4M3)
         q_late = operand("q_late", 5 * BLOCK, tag="raw1")
-        quantise(blocks(q_late, 0, 1), rounded3[:], E5M2)
-        quantise(blocks(q_late, 1, 2), rounded4, E5M2)
+        quantise(blocks(q_late, 0, 2), rounded34, E5M2)
         scatter(0, 0, 2 * BLOCK, dx00[:])
         rounded5 = sbuf("rounded5", [P, BLOCK, PACK], BF16, tag="left01")
         round_block(rounded5[:], 5)
@@ -256,7 +252,7 @@ def tile_list_embg_tgq8_noneP_kernel(tc, dy, w_words, w_scales, wgo, offs, out_0
         add_up(3)
         add_up(4)
         rounded67 = sbuf("rounded67", [P, 2 * BLOCK, PACK], BF16, tag="dx00")
-        nc.scalar.copy(out=woven(rounded67[:]), in_=planar(raw[5][:]))
+        nc.scalar.copy(out=woven(rounded67[:]), in_=planar(raw[4][:, :, BLOCK:]))
         issue(early[2])
         back(5)
         issue(early[3])

@@ -306,14 +306,15 @@ def tile_list_embg_tgq8_noneP_kernel(tc, dy, w_words, w_scales, wgo, offs, out_0
             u, e = divmod(t, 2)
             for i, (lo, hi) in enumerate(shares):
                 if t == PACK - 1 and i == 0:
+                    nc.vector.tensor_copy(out=seam[:, :, :, 1 - e], in_=seam[:, :, :, e])
                     for at in range(lo, hi, CHUNK):
                         nc.vector.tensor_copy(out=pair_view(i)[:, u, at:at + CHUNK, e], in_=pages[t][:, at:at + CHUNK])
                 elif t == PACK - 2 and i == 0:
                     by_chunk = pair_view(i)[:, u].rearrange("p (k c) e -> p k c e", c=CHUNK)
                     source = pages[t][:, lo:hi].rearrange("p (k c) -> p k c", c=CHUNK)
                     nc.scalar.copy(out=by_chunk[:, :, 0:CHUNK - SEAM, e], in_=source[:, :, 0:CHUNK - SEAM])
-                    nc.scalar.copy(out=by_chunk[:, :, CHUNK - SEAM:, :],
-                                   in_=source[:, :, CHUNK - SEAM:].unsqueeze(3).to_broadcast([P, (hi - lo) // CHUNK, SEAM, 2]))
+                    nc.scalar.copy(out=by_chunk[:, :, CHUNK - SEAM:, 1 - e], in_=source[:, :, CHUNK - SEAM:])
+                    seam = by_chunk[:, :, CHUNK - SEAM:, :]
                 else:
                     nc.scalar.copy(out=pair_view(i)[:, u, :, e], in_=pages[t][:, lo:hi])
 

from contextlib import ExitStack

import concourse.mybir as mybir

K, N, T, J = 512, 512, 2048, 1024
FLOPS = 2 * K * N * J * 3

F32 = mybir.dt.float32
BF16 = mybir.dt.bfloat16
I32 = mybir.dt.int32
U32 = mybir.dt.uint32
U16 = mybir.dt.uint16
U8 = mybir.dt.uint8
E4M3 = mybir.dt.float8_e4m3fn_x4
E5M2 = mybir.dt.float8_e5m2_x4
MULT = mybir.AluOpType.mult
SUB = mybir.AluOpType.subtract

P = 128
PACK = 4
QUADS = 4
GROUP = 16
HALF = 512
PIECE = 256
BLOCK = 128
CHUNK = 512
PAD = 68
TWO_ONES = 1.0 + 16256.0 / 8388608.0

LAST_ON_VECTOR = 1024
SEAM = 16
LAST_CHUNK = 256
EARLY = 3 * BLOCK
AHEAD_OF_IDENTITY = 1408
CLEARED_BY_VECTOR = 1792


def woven(tile3, run=PACK):
    return tile3.rearrange("p (c i) t -> p c t i", i=run)


def planar(tile3, run=PACK):
    return tile3.rearrange("p t (c i) -> p c t i", i=run)


def flat(tile3):
    return tile3.rearrange("p a b -> p (a b)")


def tile_list_embg_tgq8_noneP_kernel(tc, dy, w_words, w_scales, wgo, offs, out_0, out_1, out_2):
    nc = tc.nc

    with ExitStack() as ctx:
        sb = ctx.enter_context(tc.tile_pool(name="sb", bufs=1))
        psum = ctx.enter_context(tc.psum_pool(name="psum", bufs=1))

        def sbuf(name, shape, dtype, tag=None):
            return sb.tile(shape, dtype, name=name, tag=tag or name, align_bytes=64)

        dy_planes = dy.rearrange("(p t) j -> p t j", t=PACK)
        spans = ((0, 1), (1, 2), (2, 3), (3, 5), (5, 8))
        raw = [sbuf("raw%d" % lo, [P, PACK, (hi - lo) * BLOCK], F32) for lo, hi in spans]

        def load_piece(c):
            nc.sync.dma_start(out=raw[c][:], in_=dy_planes[:, :, spans[c][0] * BLOCK:spans[c][1] * BLOCK])

        ws_in = sbuf("ws_in", [P, N], U8)
        for b in range(2):
            for queue, rows in ((nc.sync, slice(0, 2)), (nc.scalar, slice(2, 4))):
                queue.dma_start(out=raw[b][:, rows, :], in_=dy_planes[:, rows, b * BLOCK:(b + 1) * BLOCK])
        load_piece(2)
        for q in range(QUADS):
            nc.sync.dma_start(out=ws_in[32 * q:32 * q + 32, :].bitcast(I32),
                              in_=w_scales[0, 4 * q:4 * q + 4, :].bitcast(I32).unsqueeze(0).to_broadcast([8, 4, N // 4]))
        w_in = sbuf("w_in", [P, N], I32)
        nc.sync.dma_start(out=w_in[:], in_=w_words[0].rearrange("p n i -> p (n i)").bitcast(I32))
        load_piece(3)
        offsets = sb.tile([P, J // GROUP], U16, name="offsets")
        nc.sync.dma_start(offsets[:], offs)
        gain = sbuf("gain", [P, J], F32)
        nc.sync.dma_start(out=gain[:, 0:EARLY], in_=wgo[:, 0:EARLY])
        load_piece(4)
        nc.sync.dma_start(out=gain[:, EARLY:], in_=wgo[:, EARLY:])

        row = P * PACK
        eye_codes = sbuf("eye_codes", [P, PACK * row + PAD], U8)
        nc.vector.memset(eye_codes[:].bitcast(I32), 0)
        pages = {0: sbuf("page0", [P, T], F32), 1: sbuf("page1", [P, T], F32)}
        nc.gpsimd.memset(pages[0][:, 0:AHEAD_OF_IDENTITY], 0.0)
        eye_pairs = sbuf("eye_pairs", [P, P], F32)
        nc.gpsimd.affine_select(out=eye_pairs[:], in_=eye_codes[:, 0:row].bitcast(F32), pattern=[[-1, P]], compare_op=mybir.AluOpType.not_equal,
                                fill=TWO_ONES, base=0, channel_multiplier=1)
        eye_in = sbuf("eye_in", [P, P, PACK], BF16)
        nc.scalar.copy(out=eye_in[:].bitcast(F32), in_=eye_pairs[:].unsqueeze(2).to_broadcast([P, P, 2]))
        eye = sbuf("eye", [P, P], F32)
        nc.scalar.copy(out=eye[:], in_=eye_pairs[:].bitcast(BF16).rearrange("p (m e) -> p m e", e=2)[:, :, 0])
        nc.vector.memset(pages[1][:, 0:CLEARED_BY_VECTOR // 2 - 1].bitcast(I32), 0)
        nc.vector.memset(pages[1][:, CLEARED_BY_VECTOR // 2 - 1:CLEARED_BY_VECTOR].bitcast(I32), 0)
        nc.gpsimd.memset(pages[0][:, AHEAD_OF_IDENTITY:], 0.0)
        nc.gpsimd.memset(pages[1][:, CLEARED_BY_VECTOR:], 0.0)
        eye_base = sbuf("eye_base", [P, P, PACK], U8)
        eye_scales = sbuf("eye_scales", [P, P], U8)
        nc.vector.quantize_mx(out=flat(eye_base[:]).bitcast(E4M3), scales=eye_scales[:], in_=flat(eye_in[:]))
        diagonal = eye_codes[:, 0:PACK * (row + 1)].rearrange("p (t x) -> p t x", t=PACK)[:, :, 0:row:PACK]

        banks = [psum.tile([P, HALF], F32, name="bank%d" % b) for b in range(8)]

        def raw_block(b):
            c = max(i for i, span in enumerate(spans) if span[0] <= b)
            s = b - spans[c][0]
            return raw[c][:, :, s * BLOCK:(s + 1) * BLOCK]

        def block_of(tile3, s):
            return tile3[:, s * BLOCK:(s + 1) * BLOCK, :]

        def operand(name, width, tag=None):
            return sbuf(name + "_codes", [P, width], U32, tag=tag)[:], sbuf(name + "_scales", [P, width], U8)[:]

        def cols(pair, lo, hi):
            return pair[0][:, lo:hi], pair[1][:, lo:hi]

        def quantise(pair, values, fmt):
            nc.vector.quantize_mx(out=pair[0].bitcast(fmt), scales=pair[1], in_=flat(values))

        def round_block(out, b):
            nc.scalar.copy(out=woven(out), in_=planar(raw_block(b)))

        def bring_back(bank, pair):
            for t in range(PACK):
                nc.tensor.matmul_mx(out=bank[:, t * BLOCK:(t + 1) * BLOCK], lhsT=eye_codes[:, t * row:(t + 1) * row].bitcast(E4M3),
                                    lhsT_scale=eye_scales[:], rhs=pair[0].bitcast(E5M2), rhs_scale=pair[1], start=True, stop=True)

        def empty(name, sums, width, tag=None):
            dx = sbuf(name, [P, width], F32, tag=tag)
            nc.scalar.copy(out=dx[:], in_=sums)
            return dx

        def scatter(t, lo, hi, dx):
            nc.vector.tensor_tensor(pages[t][:].indirect(offsets[:, lo // GROUP:hi // GROUP]), dx, gain[:, lo:hi], MULT)

        def clear(t, freed):
            pages[t] = sbuf("page%d" % t, [P, T], F32, tag=freed)
            nc.gpsimd.memset(pages[t][:], 0.0)

        def turn(bank, values, first):
            for t in range(PACK):
                nc.tensor.matmul(bank[:, t * P:(t + 1) * P], lhsT=values[:, t, :], rhs=eye[:], is_transpose=True,
                                 start=(first and t == 0), stop=(not first and t == PACK - 1))

        def negate(b, bank):
            minus = sbuf("minus%d" % b, [P, PACK, BLOCK], F32, tag="turned5" if b == 7 else None)
            nc.scalar.mul(flat(minus[:]), bank[:], -1.0)
            return minus

        def round_sums(b, bank, into):
            turned = sbuf("turned%d" % b, [P, 2 * P], F32)
            nc.scalar.copy(out=turned[:].bitcast(BF16).rearrange("p (u m e) -> p u m e", u=2, e=2),
                           in_=bank[:].rearrange("p (u e m) -> p u m e", u=2, e=2))
            for u in range(2):
                nc.tensor.transpose(into[:, u * P:(u + 1) * P], turned[:, u * P:(u + 1) * P], eye[:])

        def lay_words(left, lo, hi, bank):
            nc.scalar.copy(out=flat(left[:, lo * BLOCK:hi * BLOCK, :]).bitcast(F32).rearrange("p (s j u) -> p s j u", j=BLOCK, u=2),
                           in_=bank[:, 0:(hi - lo) * 2 * P].rearrange("p (s u j) -> p s j u", j=BLOCK, u=2))

        def subtract(out, b):
            nc.vector.tensor_tensor(woven(out, 2), planar(raw_block(b), 2),
                                    planar(banks[b][:].rearrange("p (t j) -> p t j", t=PACK), 2), SUB)

        def run_of(tile3, lo, hi):
            return tile3[:, lo * BLOCK:hi * BLOCK, :]

        def blocks(pair, lo, hi):
            return cols(pair, lo * BLOCK, hi * BLOCK)

        def product(bank, t, first, second, backwards=False):
            passes = []
            for parts, fmt in ((first, E5M2), (second, E4M3)):
                at = 0
                for pair in parts:
                    width = pair[0].shape[1]
                    passes.append((at, width, pair, fmt))
                    at = at + width
            passes = passes[::-1] if backwards else passes
            return [lambda i=i, x=x: nc.tensor.matmul_mx(out=bank[:, x[0]:x[0] + x[1]], lhsT=w_codes[:, t, :].bitcast(E4M3), lhsT_scale=w_plane[:, t, :],
                                                         rhs=x[2][0].bitcast(x[3]), rhs_scale=x[2][1], start=(i == 0), stop=(i == len(passes) - 1))
                    for i, x in enumerate(passes)]

        def issue(calls):
            for call in calls:
                call()

        rounded01 = sbuf("rounded01", [P, 2 * BLOCK, PACK], BF16, tag="eye_in")
        q01 = operand("q01", 2 * BLOCK)
        nc.vector.tensor_copy(out=woven(run_of(rounded01[:], 0, 1)), in_=planar(raw_block(0)))
        nc.vector.tensor_copy(out=diagonal, in_=eye_base[:].rearrange("p m t -> p t m"))
        round_block(run_of(rounded01[:], 1, 2), 1)
        for s in range(2):
            quantise(blocks(q01, s, s + 1), run_of(rounded01[:], s, s + 1), E5M2)
        for s in range(2):
            bring_back(banks[s], blocks(q01, s, s + 1))
        w_plane = sbuf("w_plane", [P, PACK, P], U8, tag="eye_in")
        nc.vector.tensor_copy(out=w_plane[:], in_=ws_in[:].rearrange("p (m t) -> p t m", t=PACK))
        rounded2 = sbuf("rounded2", [P, BLOCK, PACK], BF16, tag="eye_base")
        round_block(rounded2[:], 2)
        w_codes = sbuf("w_codes", [P, PACK, P], U32, tag="ws_in")
        nc.scalar.copy(out=planar(w_codes[:]), in_=woven(w_in[:].bitcast(U32).rearrange("p (m t) -> p m t", t=PACK)))

        left01 = sbuf("left01", [P, 2 * BLOCK, PACK], BF16)
        r012 = operand("r012", 3 * BLOCK)
        r_late = operand("r_late", 5 * BLOCK)
        subtract(run_of(left01[:], 0, 1), 0)
        q2 = operand("q2", BLOCK, tag="raw0")
        quantise(q2, rounded2[:], E5M2)
        subtract(run_of(left01[:], 1, 2), 1)
        bring_back(banks[2], q2)
        for s in range(2):
            quantise(blocks(r012, s, s + 1), run_of(left01[:], s, s + 1), E4M3)
        opening = product(banks[4], 0, [q01], [blocks(r012, 0, 1), blocks(r012, 1, 2)])
        early = {t: product(bank, t, [q01, q2], [blocks(r012, 0, 2), blocks(r012, 2, 3)], t > 1) for t, bank in ((1, banks[1]), (2, banks[6]), (3, banks[7]))}
        issue(opening)
        dx00 = empty("dx00", banks[4][:, 0:2 * BLOCK], 2 * BLOCK)
        staged = sbuf("staged", [P, 3 * BLOCK, PACK], BF16, tag="left01")
        left2, rounded34 = run_of(staged[:], 0, 1), run_of(staged[:], 1, 3)
        subtract(left2, 2)
        nc.vector.tensor_copy(out=woven(rounded34[:, 0:3 * BLOCK // 2, :]), in_=planar(raw[3][:, :, 0:3 * BLOCK // 2]))
        nc.scalar.copy(out=woven(rounded34[:, 3 * BLOCK // 2:, :]), in_=planar(raw[3][:, :, 3 * BLOCK // 2:]))
        quantise(blocks(r012, 2, 3), left2, E4M3)
        q_late = operand("q_late", 5 * BLOCK, tag="raw1")
        quantise(blocks(q_late, 0, 2), rounded34, E5M2)
        scatter(0, 0, 2 * BLOCK, dx00[:])
        rounded5 = sbuf("rounded5", [P, BLOCK, PACK], BF16, tag="left01")
        round_block(rounded5[:], 5)
        quantise(blocks(q_late, 2, 3), rounded5[:], E5M2)
        clear(2, "left01")
        issue(early[1])
        scatter(1, 0, 3 * BLOCK, empty("dx1a", banks[1][:, 0:3 * BLOCK], 3 * BLOCK)[:])

        back_banks = {3: banks[3], 4: banks[0], 5: banks[5], 6: banks[4], 7: banks[5]}
        sum_banks = {3: banks[2], 4: banks[4], 5: banks[1], 6: banks[6], 7: banks[3]}
        left_late = sbuf("left_late", [P, 5 * BLOCK, PACK], BF16)

        def back(b):
            bring_back(back_banks[b], blocks(q_late, b - 3, b - 2))

        def add_up(b):
            turn(sum_banks[b], raw_block(b), True)
            turn(sum_banks[b], negate(b, back_banks[b]), False)

        back(3)
        back(4)
        add_up(3)
        add_up(4)
        rounded67 = sbuf("rounded67", [P, 2 * BLOCK, PACK], BF16, tag="dx00")
        nc.scalar.copy(out=woven(rounded67[:]), in_=planar(raw[4][:, :, BLOCK:]))
        issue(early[2])
        back(5)
        issue(early[3])
        quantise(blocks(q_late, 3, 5), rounded67[:], E5M2)
        clear(3, "dx00")
        scatter(2, 0, 3 * BLOCK, empty("dx2a", banks[6][:, 0:3 * BLOCK], 3 * BLOCK, tag="minus3")[:])
        round_sums(3, sum_banks[3], sum_banks[3])
        round_sums(4, sum_banks[4], sum_banks[3][:, 2 * P:])
        back(6)
        add_up(5)
        back(7)
        lay_words(left_late[:], 0, 2, sum_banks[3])
        quantise(blocks(r_late, 0, 2), run_of(left_late[:], 0, 2), E4M3)
        scatter(3, 0, 3 * BLOCK, empty("dx3a", banks[7][:, 0:3 * BLOCK], 3 * BLOCK, tag="turned4")[:])
        round_sums(5, sum_banks[5], sum_banks[5])
        add_up(6)
        issue(product(banks[2], 0, [q2, blocks(q_late, 0, 2)], [blocks(r012, 2, 3), blocks(r_late, 0, 2)]))
        scatter(0, 2 * BLOCK, 5 * BLOCK, empty("dx0b", banks[2][:, 0:3 * BLOCK], 3 * BLOCK)[:])
        add_up(7)
        lay_words(left_late[:], 2, 3, sum_banks[5])
        for b in (6, 7):
            round_sums(b, sum_banks[b], sum_banks[6][:, (b - 6) * 2 * P:])
        lay_words(left_late[:], 3, 5, sum_banks[6])
        issue(product(banks[1], 1, [blocks(q_late, 0, 2)], [blocks(r_late, 0, 2)]))
        for t in (2, 3):
            issue(product(banks[6][:, (t - 2) * 2 * BLOCK:], t, [blocks(q_late, 0, 2)], [blocks(r_late, 0, 2)]))
        quantise(blocks(r_late, 2, 5), run_of(left_late[:], 2, 5), E4M3)
        scatter(1, 3 * BLOCK, 5 * BLOCK, empty("dx1b", banks[1][:, 0:2 * BLOCK], 2 * BLOCK, tag="turned7")[:])
        dx_late = sbuf("dx_late", [P, 2, 5 * BLOCK], F32, tag="turned6")
        nc.scalar.copy(out=dx_late[:, :, 0:2 * BLOCK], in_=banks[6][:].rearrange("p (t j) -> p t j", t=2))
        last = [blocks(q_late, 2, 4), blocks(q_late, 4, 5)], [blocks(r_late, 2, 4), blocks(r_late, 4, 5)]
        late = {}
        for t, bank in enumerate((banks[3], banks[4], banks[7], banks[0])):
            issue(product(bank, t, last[0], last[1], t > 0))
            if t < 2:
                late[t] = (5 * BLOCK, empty("dx%dc" % t, bank[:, 0:3 * BLOCK], 3 * BLOCK)[:])
            else:
                nc.scalar.copy(out=dx_late[:, t - 2, 2 * BLOCK:], in_=bank[:, 0:3 * BLOCK])
                late[t] = (3 * BLOCK, dx_late[:, t - 2, :])

        out_planes = out_0.rearrange("(p t) c -> p t c", t=PACK)
        shares = ((0, LAST_ON_VECTOR), (LAST_ON_VECTOR, T))
        pairs = [sbuf("pairs%d" % i, [P, PACK * (hi - lo)], BF16, tag=tag) for (i, (lo, hi)), tag in zip(enumerate(shares), ("r_late_codes", "left_late"))]

        def pair_view(i):
            return pairs[i][:].rearrange("p (u c e) -> p u c e", u=2, e=2)

        for t in range(PACK):
            scatter(t, late[t][0], J, late[t][1])
            nc.sync.dma_start(out=out_planes[:, t, :], in_=pages[t][:])
            u, e = divmod(t, 2)
            for i, (lo, hi) in enumerate(shares):
                if t == PACK - 1 and i == 0:
                    nc.vector.tensor_copy(out=seam[:, :, :, 1 - e], in_=seam[:, :, :, e])
                    for at in range(lo, hi, CHUNK):
                        nc.vector.tensor_copy(out=pair_view(i)[:, u, at:at + CHUNK, e], in_=pages[t][:, at:at + CHUNK])
                elif t == PACK - 2 and i == 0:
                    by_chunk = pair_view(i)[:, u].rearrange("p (k c) e -> p k c e", c=CHUNK)
                    source = pages[t][:, lo:hi].rearrange("p (k c) -> p k c", c=CHUNK)
                    nc.scalar.copy(out=by_chunk[:, :, 0:CHUNK - SEAM, e], in_=source[:, :, 0:CHUNK - SEAM])
                    nc.scalar.copy(out=by_chunk[:, :, CHUNK - SEAM:, 1 - e], in_=source[:, :, CHUNK - SEAM:])
                    seam = by_chunk[:, :, CHUNK - SEAM:, :]
                else:
                    nc.scalar.copy(out=pair_view(i)[:, u, :, e], in_=pages[t][:, lo:hi])

        words_out = out_1[0].rearrange("p c i -> p (c i)").bitcast(I32)
        y_scales = sbuf("y_scales", [P, CHUNK], U8)
        grouped = [sbuf("grouped%d" % c, [P, CHUNK * PACK], BF16) for c in range(T // CHUNK)]

        def weave_words(lo, hi, on_vector):
            c, i = lo // CHUNK, 0 if lo < LAST_ON_VECTOR else 1
            word = I32 if on_vector else U32
            src = pairs[i][:].bitcast(word).rearrange("p (u c) -> p u c", u=2)[:, :, lo - shares[i][0]:hi - shares[i][0]]
            dst = grouped[c][:].bitcast(word)[:, 2 * (lo - c * CHUNK):2 * (hi - c * CHUNK)]
            copy = nc.vector.tensor_copy if on_vector else nc.scalar.copy
            copy(out=dst.rearrange("p (c i u) -> p c u i", i=PACK, u=2), in_=src.rearrange("p u (c i) -> p c u i", i=PACK))

        cuts = (0, CHUNK, 2 * CHUNK, 3 * CHUNK, T - LAST_CHUNK, T)
        for lo, hi in zip(cuts, cuts[1:]):
            weave_words(lo, hi, hi <= LAST_ON_VECTOR)
        for lo, hi in zip(cuts, cuts[1:]):
            y_codes = sbuf("y_codes%d" % lo, [P, hi - lo], U32)
            for part in range(lo, hi, LAST_CHUNK):
                c, at = divmod(part, CHUNK)
                nc.vector.quantize_mx(out=y_codes[:, part - lo:part - lo + LAST_CHUNK].bitcast(E4M3), scales=y_scales[4 * c:, at:at + LAST_CHUNK],
                                      in_=grouped[c][:, PACK * at:PACK * (at + LAST_CHUNK)])
            nc.sync.dma_start(out=words_out[:, lo:hi], in_=y_codes[:].bitcast(I32))
        for q in range(QUADS):
            queue = nc.scalar if q < 2 else nc.sync
            queue.dma_start(out=out_2[0, 4 * q:4 * q + 4, :].bitcast(I32).rearrange("r (u x) -> u r x", u=4),
                            in_=y_scales[32 * q:32 * q + 16, :].bitcast(I32))
